import numpy as np
import ml_dtypes


def mxq(x, axis, fmt="e4m3"):
    dtype, down = {"e4m3": (ml_dtypes.float8_e4m3fn, 7), "e5m2": (ml_dtypes.float8_e5m2, 14)}[fmt]
    v = np.moveaxis(np.asarray(x, np.float32).astype(ml_dtypes.bfloat16).astype(np.float64), axis, -1)
    blocks = v.reshape(v.shape[:-1] + (-1, 32))
    amax = np.abs(blocks).max(-1, keepdims=True)
    byte = np.maximum(np.where(amax > 0, np.frexp(amax)[1] - 1 + 127, 0) - down, 1)
    scale = np.exp2(byte - 127.0)
    codes = (blocks / scale).astype(np.float32).astype(dtype).astype(np.float64)
    return np.moveaxis((codes * scale).reshape(v.shape), -1, axis)


WIDE = False


def mx_kscale(k):
    if not WIDE:
        return np.ones(k)
    levels = np.array([10, -10, 5, -5, 0])
    if k % 512:
        return np.exp2(np.random.permutation(np.resize(levels, k // 32))).repeat(32)
    a = np.empty((k // 512, 16))
    for p in range(k // 512):
        a[p, :8] = np.random.permutation(np.resize(levels, 8))
        for g in range(8):
            far = levels[np.abs(levels - a[p, g]) >= 10]
            a[p, g + 8] = far[np.random.randint(len(far))]
    return np.exp2(a.ravel()).repeat(32)


BF16 = ml_dtypes.bfloat16


def bf(x):
    return np.asarray(x, np.float32).astype(BF16)


def f64(x):
    return np.asarray(x).astype(np.float64)

E4M3FN = np.array([(-1.0 if i & 128 else 1.0) * ((1.0 + (i & 7) / 8.0) * 2.0 ** (((i >> 3) & 15) - 7) if i & 120 else (i & 7) * 2.0 ** -9) for i in range(256)])


def e4m3fn_bytes(y):
    return np.clip(np.asarray(y, np.float64), -448.0, 448.0).astype(np.float32).astype(ml_dtypes.float8_e4m3fn).view(np.uint8)


def e4m3fn_values(b):
    return E4M3FN[b]


T, E, D, N, B = 1024, 1024, 2048, 1536, 128


def setup_inputs():
    s, u = mx_kscale(E), mx_kscale(D)
    e = np.random.standard_normal((T, E)) * s
    f = np.random.standard_normal((T, D)) * u
    w = np.random.standard_normal((E + D, N)) / np.sqrt(E + D) / np.concatenate([s, u])[:, None]
    f_scale = (np.abs(f).reshape(T, D // B, B).max(axis=2) / 448.0).astype(np.float32)
    f_bytes = e4m3fn_bytes(f / np.repeat(f64(f_scale), B, axis=1))
    w_scale = (np.abs(w).reshape((E + D) // B, B, N // B, B).max(axis=(1, 3)) / 448.0).astype(np.float32)
    w_bytes = e4m3fn_bytes(w / np.repeat(np.repeat(f64(w_scale), B, axis=0), B, axis=1))
    return {"e": bf(e),
            "f_bytes": f_bytes,
            "f_scale": f_scale,
            "w_bytes": w_bytes,
            "w_scale": w_scale,
            "trust": bf(np.random.uniform(0.5, 1.5, (T, 1))),
            "b": bf(0.3 * np.random.standard_normal(N))}


def reference(e, f_bytes, f_scale, w_bytes, w_scale, trust, b):
    f = e4m3fn_values(f_bytes) * np.repeat(f64(f_scale), B, axis=1)
    w = e4m3fn_values(w_bytes) * np.repeat(np.repeat(f64(w_scale), B, axis=0), B, axis=1)
    wq = mxq(w, 0, "e4m3")
    a = mxq(f64(e), 1, "e4m3") @ wq[:E]
    c = mxq(f, 1, "e4m3") @ wq[E:]
    z = a + f64(trust) * c + f64(b)
    return z / (1.0 + np.exp(-z))

@@ -1,0 +1,216 @@
+from contextlib import ExitStack
+
+import concourse.mybir as mybir
+from concourse.masks import make_identity
+
+T, E, D, N = 1024, 1024, 2048, 1536
+P = 128
+K_PASS = 512
+FLOPS = 2 * T * (E + D) * N
+
+F32 = mybir.dt.float32
+BF16 = mybir.dt.bfloat16
+U32 = mybir.dt.uint32
+U8 = mybir.dt.uint8
+FP8 = mybir.dt.float8_e4m3fn
+FP8X4 = mybir.dt.float8_e4m3fn_x4
+ADD = mybir.AluOpType.add
+MULT = mybir.AluOpType.mult
+ACT = mybir.ActivationFunctionType
+
+M_TILES = T // P
+E_PASSES = E // K_PASS
+F_PASSES = D // K_PASS
+PASSES = E_PASSES + F_PASSES
+F_BLOCKS = D // P
+
+CHUNKS = [(0, 512), (512, 512), (1024, 256), (1280, 256)]
+UNIT = 2048
+F_ON_SCALAR = 16
+
+
+def tile_drafter_feature_fusion_d2_kernel(tc, e, f_bytes, f_scale, w_bytes, w_scale, trust, b, out):
+    nc = tc.nc
+    with ExitStack() as ctx:
+        once = ctx.enter_context(tc.tile_pool(name="once", bufs=1))
+        codes8 = ctx.enter_context(tc.tile_pool(name="keep", bufs=1))
+        work = ctx.enter_context(tc.tile_pool(name="work", bufs=3))
+        psum = ctx.enter_context(tc.psum_pool(name="psum", bufs=2))
+
+        e_v = e.rearrange("(p m) k -> p m k", m=M_TILES)
+        f_v = f_bytes.rearrange("(p m) k -> p m k", m=M_TILES)
+        o_v = out.rearrange("(p m) n -> p m n", m=M_TILES)
+        w_v = w_bytes.rearrange("(g p t) n -> p g t n", p=P, t=4)
+
+        wall = once.tile([P, 24 * 12], F32)
+        nc.scalar.dma_start(out=wall[:], in_=w_scale.rearrange("r j -> (r j)").partition_broadcast(P))
+        fs = once.tile([P, M_TILES * F_BLOCKS], F32)
+        nc.scalar.dma_start(out=fs[:], in_=f_scale.rearrange("(p m) j -> p (m j)", m=M_TILES))
+
+        zero = once.tile([P, 1], F32)
+        nc.vector.memset(zero[:], 0.0)
+        warm = once.tile([P, 1], F32)
+        nc.scalar.activation(out=warm[:], in_=zero[:], func=ACT.Silu)
+
+        units = []
+        for c in range(len(CHUNKS)):
+            width = CHUNKS[c][1]
+            per = UNIT // (4 * width)
+            for g in range(0, PASSES, per):
+                units.append((c, g, per))
+
+        wb = {}
+        eb = {}
+        fb = {}
+
+        def load_w(c, g, per):
+            n0, width = CHUNKS[c]
+            t = once.tile([P, UNIT], U8, name="wb%d_%d" % (c, g))
+            if per == 1:
+                nc.sync.dma_start(out=t[:].rearrange("p (t n) -> p t n", t=4), in_=w_v[:, g, :, n0:n0 + width])
+            else:
+                for i in range(per):
+                    part = UNIT // per
+                    nc.sync.dma_start(
+                        out=t[:, i * part:(i + 1) * part].rearrange("p (t n) -> p t n", t=4),
+                        in_=w_v[:, g + i, :, n0:n0 + width])
+            wb[(c, g)] = t
+
+        def load_x(m):
+            t = once.tile([P, E], BF16, name="eb%d" % m)
+            nc.sync.dma_start(out=t[:], in_=e_v[:, m, :])
+            eb[m] = t
+            t2 = once.tile([P, D], U8, name="fb%d" % m)
+            nc.sync.dma_start(out=t2[:], in_=f_v[:, m, :])
+            fb[m] = t2
+
+        c0 = [u for u in units if u[0] == 0]
+        rest = [u for u in units if u[0] != 0]
+        load_w(*c0[0])
+        load_x(0)
+        for u in c0[1:]:
+            load_w(*u)
+        load_x(1)
+        load_x(2)
+        tr = once.tile([P, M_TILES], BF16)
+        nc.sync.dma_start(out=tr[:], in_=trust.rearrange("(p m) o -> p (m o)", m=M_TILES))
+        bt = once.tile([P, N], BF16)
+        nc.sync.dma_start(out=bt[:], in_=b.partition_broadcast(P))
+        load_x(3)
+        for i, u in enumerate(rest):
+            load_w(*u)
+            if i < 4:
+                load_x(4 + i)
+
+        ident = once.tile([P, P], F32)
+        make_identity(nc, ident[:])
+
+        ws = once.tile([P, PASSES, 12], F32)
+        wall_v = wall[:].rearrange("p (g q j) -> p g q j", g=PASSES, q=4)
+        for q in range(4):
+            rows = slice(32 * q, 32 * q + 32)
+            nc.gpsimd.tensor_copy(out=ws[rows, :, :], in_=wall_v[rows, :, q, :])
+
+        wq = {}
+
+        def prep_w(c, g, per):
+            n0, width = CHUNKS[c]
+            planes = work.tile([P, UNIT], BF16, name="planes")
+            nc.scalar.copy(out=planes[:], in_=wb[(c, g)][:].bitcast(FP8))
+            laced = work.tile([P, UNIT], BF16, align_bytes=64, name="laced")
+            part = UNIT // per
+            for i in range(per):
+                src = planes[:, i * part:(i + 1) * part].rearrange("p (t c i) -> p c t i", t=4, i=4)
+                dst = laced[:, i * part:(i + 1) * part].rearrange("p (c i t) -> p c t i", t=4, i=4)
+                for j in range(width // P):
+                    blk = slice(j * 32, (j + 1) * 32)
+                    jj = n0 // P + j
+                    nc.vector.tensor_scalar(out=dst[:, blk], in0=src[:, blk], scalar1=ws[:, g + i, jj:jj + 1],
+                                            scalar2=None, op0=MULT)
+            wc = once.tile([P, UNIT // 4], U32, align_bytes=64, name="wc%d_%d" % (c, g))
+            wsc = once.tile([P, UNIT // 4], U8, align_bytes=64, name="wsc%d_%d" % (c, g))
+            nc.vector.quantize_mx(out=wc[:].bitcast(FP8X4), scales=wsc[:], in_=laced[:])
+            for i in range(per):
+                cols = slice(i * width, (i + 1) * width)
+                wq[(c, g + i)] = (wc, wsc, cols)
+
+        xq = {}
+
+        def turn(words, g0, name, gr, goff):
+            bank = psum.tile([P, 2, 2, P], F32, name="turn")
+            for h in range(2):
+                for u in range(2):
+                    s = 256 * (g0 + h) + u
+                    nc.tensor.transpose(bank[:, h, u, :], words[:, s:256 * (g0 + h + 1):2], ident[:])
+            dst = gr[:, goff:goff + 1024].bitcast(F32).rearrange("p (h r u) -> p h r u", h=2, u=2)
+            nc.scalar.copy(out=dst, in_=bank[:].rearrange("p h u r -> p h r u"))
+
+        def prep_x(m):
+            ge = work.tile([P, E], BF16, align_bytes=64, name="ge")
+            turn(eb[m][:].bitcast(F32), 0, "e", ge, 0)
+            ec = once.tile([P, E // 4], U32, align_bytes=64, name="ec%d" % m)
+            es = once.tile([P, E // 4], U8, align_bytes=64, name="es%d" % m)
+            nc.vector.quantize_mx(out=ec[:].bitcast(FP8X4), scales=es[:], in_=ge[:])
+            fw = work.tile([P, D], BF16, name="fw")
+            for j in range(F_BLOCKS):
+                cols = slice(j * P, (j + 1) * P)
+                sc = fs[:, m * F_BLOCKS + j:m * F_BLOCKS + j + 1]
+                if j < F_ON_SCALAR:
+                    nc.scalar.activation(out=fw[:, cols], in_=fb[m][:, cols].bitcast(FP8), func=ACT.Copy, scale=sc)
+                else:
+                    nc.vector.tensor_scalar(out=fw[:, cols], in0=fb[m][:, cols].bitcast(FP8), scalar1=sc,
+                                            scalar2=None, op0=MULT)
+            gf = work.tile([P, D], BF16, align_bytes=64, name="gf")
+            turn(fw[:].bitcast(F32), 0, "f", gf, 0)
+            turn(fw[:].bitcast(F32), 2, "f", gf, 1024)
+            fc = once.tile([P, D // 4], U32, align_bytes=64, name="fc%d" % m)
+            fsc = once.tile([P, D // 4], U8, align_bytes=64, name="fsc%d" % m)
+            nc.vector.quantize_mx(out=fc[:].bitcast(FP8X4), scales=fsc[:], in_=gf[:])
+            for g in range(E_PASSES):
+                xq[(m, g)] = (ec, es, slice(g * P, (g + 1) * P))
+            for g in range(F_PASSES):
+                xq[(m, E_PASSES + g)] = (fc, fsc, slice(g * P, (g + 1) * P))
+
+        def mm(acc, m, c, passes):
+            for g in passes:
+                xc, xs, xcols = xq[(m, g)]
+                wc, wsc, wcols = wq[(c, g)]
+                nc.tensor.matmul_mx(out=acc, lhsT=xc[:, xcols].bitcast(FP8X4), lhsT_scale=xs[:, xcols],
+                                    rhs=wc[:, wcols].bitcast(FP8X4), rhs_scale=wsc[:, wcols],
+                                    start=(g == passes[0]), stop=(g == passes[-1]))
+
+        def product(m, c):
+            n0, width = CHUNKS[c]
+            acc_a = psum.tile([P, 512], F32, name="acc", bufs=6)
+            a = acc_a[:, 0:width]
+            if width == 512:
+                acc_c = psum.tile([P, 512], F32, name="acc", bufs=6)
+                cc = acc_c[:, 0:width]
+            else:
+                cc = acc_a[:, width:2 * width]
+            mm(a, m, c, list(range(E_PASSES)))
+            mm(cc, m, c, list(range(E_PASSES, PASSES)))
+            t = work.tile([P, 512], F32, name="t")
+            nc.vector.tensor_tensor(out=t[:, 0:width], in0=a, in1=bt[:, n0:n0 + width], op=ADD)
+            z = work.tile([P, 512], F32, name="z")
+            nc.vector.scalar_tensor_tensor(out=z[:, 0:width], in0=cc, scalar=tr[:, m:m + 1], in1=t[:, 0:width],
+                                           op0=MULT, op1=ADD)
+            o = work.tile([P, 512], F32, name="o", bufs=4)
+            nc.scalar.activation(out=o[:, 0:width], in_=z[:, 0:width], func=ACT.Silu)
+            nc.sync.dma_start(out=o_v[:, m, n0:n0 + width], in_=o[:, 0:width])
+
+        prep_w(*c0[0])
+        prep_x(0)
+        for u in c0[1:]:
+            prep_w(*u)
+        prep_x(1)
+        for m in range(M_TILES):
+            product(m, 0)
+            if m + 2 < M_TILES:
+                prep_x(m + 2)
+        for c in range(1, len(CHUNKS)):
+            for u in units:
+                if u[0] == c:
+                    prep_w(*u)
+            for m in range(M_TILES):
+                product(m, c)

@@ -4,8 +4,6 @@ import concourse.mybir as mybir
 from concourse.masks import make_identity
 
 T, E, D, N = 1024, 1024, 2048, 1536
-P = 128
-K_PASS = 512
 FLOPS = 2 * T * (E + D) * N
 
 F32 = mybir.dt.float32
@@ -18,199 +16,274 @@ ADD = mybir.AluOpType.add
 MULT = mybir.AluOpType.mult
 ACT = mybir.ActivationFunctionType
 
-M_TILES = T // P
-E_PASSES = E // K_PASS
+P = 128
+B = 128
+K_PASS = 512
+TILES = T // P
+PAIRS = TILES // 2
+PASSES = (E + D) // K_PASS
 F_PASSES = D // K_PASS
-PASSES = E_PASSES + F_PASSES
-F_BLOCKS = D // P
-
-CHUNKS = [(0, 512), (512, 512), (1024, 256), (1280, 256)]
-UNIT = 2048
-F_ON_SCALAR = 16
+F_BLOCKS = D // B
+W_BLOCKS = N // B
+CHUNK = 256
+CHUNKS = N // CHUNK
+PARTS = PASSES // 2
+UNITS = CHUNKS * PARTS
+UNIT = 2 * 4 * CHUNK
+EARLY = 512
+F_ON_SCALAR = (0,)
 
 
 def tile_drafter_feature_fusion_d2_kernel(tc, e, f_bytes, f_scale, w_bytes, w_scale, trust, b, out):
     nc = tc.nc
     with ExitStack() as ctx:
         once = ctx.enter_context(tc.tile_pool(name="once", bufs=1))
-        codes8 = ctx.enter_context(tc.tile_pool(name="keep", bufs=1))
         work = ctx.enter_context(tc.tile_pool(name="work", bufs=3))
-        psum = ctx.enter_context(tc.psum_pool(name="psum", bufs=2))
+        psum = ctx.enter_context(tc.psum_pool(name="psum", bufs=1))
+        ctx.enter_context(tc.manual_schedule())
 
-        e_v = e.rearrange("(p m) k -> p m k", m=M_TILES)
-        f_v = f_bytes.rearrange("(p m) k -> p m k", m=M_TILES)
-        o_v = out.rearrange("(p m) n -> p m n", m=M_TILES)
+        e_v = e.rearrange("(p m) k -> p m k", m=TILES)
+        f_v = f_bytes.rearrange("(p m) k -> p m k", m=TILES)
+        o_v = out.rearrange("(p m) n -> p m n", m=TILES)
         w_v = w_bytes.rearrange("(g p t) n -> p g t n", p=P, t=4)
 
-        wall = once.tile([P, 24 * 12], F32)
-        nc.scalar.dma_start(out=wall[:], in_=w_scale.rearrange("r j -> (r j)").partition_broadcast(P))
-        fs = once.tile([P, M_TILES * F_BLOCKS], F32)
-        nc.scalar.dma_start(out=fs[:], in_=f_scale.rearrange("(p m) j -> p (m j)", m=M_TILES))
+        f_scales = once.tile([P, TILES * F_BLOCKS], F32)
+        nc.scalar.dma_start(out=f_scales[:], in_=f_scale.rearrange("(p m) j -> p (m j)", m=TILES))
+        w_scale_all = once.tile([P, 4 * PASSES * W_BLOCKS], F32)
+        nc.scalar.dma_start(out=w_scale_all[:], in_=w_scale.rearrange("r j -> (r j)").partition_broadcast(P))
 
-        zero = once.tile([P, 1], F32)
-        nc.vector.memset(zero[:], 0.0)
-        warm = once.tile([P, 1], F32)
-        nc.scalar.activation(out=warm[:], in_=zero[:], func=ACT.Silu)
+        w_raw = {}
+        e_raw = {}
+        f_raw = {}
 
-        units = []
-        for c in range(len(CHUNKS)):
-            width = CHUNKS[c][1]
-            per = UNIT // (4 * width)
-            for g in range(0, PASSES, per):
-                units.append((c, g, per))
+        def load_w(part, late):
+            cols = slice(EARLY, N) if late else slice(0, EARLY)
+            raw = once.tile([P, 2, 4, cols.stop - cols.start], U8, name="w_raw%d_%d" % (part, late))
+            for h in range(2):
+                nc.sync.dma_start(out=raw[:, h], in_=w_v[:, 2 * part + h, :, cols])
+            w_raw[(part, late)] = raw
 
-        wb = {}
-        eb = {}
-        fb = {}
+        def load_e(pair):
+            raw = once.tile([P, 2 * E], BF16, name="e_raw%d" % pair)
+            nc.sync.dma_start(out=raw[:], in_=e_v[:, 2 * pair:2 * pair + 2, :].rearrange("p m k -> p (m k)"))
+            e_raw[pair] = raw
 
-        def load_w(c, g, per):
-            n0, width = CHUNKS[c]
-            t = once.tile([P, UNIT], U8, name="wb%d_%d" % (c, g))
-            if per == 1:
-                nc.sync.dma_start(out=t[:].rearrange("p (t n) -> p t n", t=4), in_=w_v[:, g, :, n0:n0 + width])
-            else:
-                for i in range(per):
-                    part = UNIT // per
-                    nc.sync.dma_start(
-                        out=t[:, i * part:(i + 1) * part].rearrange("p (t n) -> p t n", t=4),
-                        in_=w_v[:, g + i, :, n0:n0 + width])
-            wb[(c, g)] = t
+        def load_f(m):
+            raw = once.tile([P, D], U8, name="f_raw%d" % m)
+            nc.sync.dma_start(out=raw[:], in_=f_v[:, m, :])
+            f_raw[m] = raw
 
-        def load_x(m):
-            t = once.tile([P, E], BF16, name="eb%d" % m)
-            nc.sync.dma_start(out=t[:], in_=e_v[:, m, :])
-            eb[m] = t
-            t2 = once.tile([P, D], U8, name="fb%d" % m)
-            nc.sync.dma_start(out=t2[:], in_=f_v[:, m, :])
-            fb[m] = t2
-
-        c0 = [u for u in units if u[0] == 0]
-        rest = [u for u in units if u[0] != 0]
-        load_w(*c0[0])
-        load_x(0)
-        for u in c0[1:]:
-            load_w(*u)
-        load_x(1)
-        load_x(2)
-        tr = once.tile([P, M_TILES], BF16)
-        nc.sync.dma_start(out=tr[:], in_=trust.rearrange("(p m) o -> p (m o)", m=M_TILES))
-        bt = once.tile([P, N], BF16)
-        nc.sync.dma_start(out=bt[:], in_=b.partition_broadcast(P))
-        load_x(3)
-        for i, u in enumerate(rest):
-            load_w(*u)
-            if i < 4:
-                load_x(4 + i)
+        load_w(0, 0)
+        load_f(0)
+        load_e(0)
+        load_f(1)
+        load_w(1, 0)
+        load_w(2, 0)
+        bias = once.tile([P, N], BF16)
+        nc.sync.dma_start(out=bias[:], in_=b.partition_broadcast(P))
+        trusts = once.tile([P, TILES], BF16)
+        nc.sync.dma_start(out=trusts[:], in_=trust.rearrange("(p m) o -> p (m o)", m=TILES))
+        for pair in range(1, PAIRS):
+            load_f(2 * pair)
+            load_e(pair)
+            load_f(2 * pair + 1)
+        for part in range(PARTS):
+            load_w(part, 1)
 
         ident = once.tile([P, P], F32)
         make_identity(nc, ident[:])
 
-        ws = once.tile([P, PASSES, 12], F32)
-        wall_v = wall[:].rearrange("p (g q j) -> p g q j", g=PASSES, q=4)
+        w_scales = once.tile([P, PASSES, W_BLOCKS], F32)
+        all_v = w_scale_all[:].rearrange("p (g q j) -> p g q j", g=PASSES, q=4)
         for q in range(4):
             rows = slice(32 * q, 32 * q + 32)
-            nc.gpsimd.tensor_copy(out=ws[rows, :, :], in_=wall_v[rows, :, q, :])
+            nc.gpsimd.tensor_copy(out=w_scales[rows, :, :], in_=all_v[rows, :, q, :])
 
-        wq = {}
+        laced = {}
+        wide = {}
+        w_mx = {}
 
-        def prep_w(c, g, per):
-            n0, width = CHUNKS[c]
-            planes = work.tile([P, UNIT], BF16, name="planes")
-            nc.scalar.copy(out=planes[:], in_=wb[(c, g)][:].bitcast(FP8))
-            laced = work.tile([P, UNIT], BF16, align_bytes=64, name="laced")
-            part = UNIT // per
-            for i in range(per):
-                src = planes[:, i * part:(i + 1) * part].rearrange("p (t c i) -> p c t i", t=4, i=4)
-                dst = laced[:, i * part:(i + 1) * part].rearrange("p (c i t) -> p c t i", t=4, i=4)
-                for j in range(width // P):
-                    blk = slice(j * 32, (j + 1) * 32)
-                    jj = n0 // P + j
-                    nc.vector.tensor_scalar(out=dst[:, blk], in0=src[:, blk], scalar1=ws[:, g + i, jj:jj + 1],
-                                            scalar2=None, op0=MULT)
-            wc = once.tile([P, UNIT // 4], U32, align_bytes=64, name="wc%d_%d" % (c, g))
-            wsc = once.tile([P, UNIT // 4], U8, align_bytes=64, name="wsc%d_%d" % (c, g))
-            nc.vector.quantize_mx(out=wc[:].bitcast(FP8X4), scales=wsc[:], in_=laced[:])
-            for i in range(per):
-                cols = slice(i * width, (i + 1) * width)
-                wq[(c, g + i)] = (wc, wsc, cols)
+        def lace_w(k):
+            c, part = divmod(k, PARTS)
+            late = int(c * CHUNK >= EARLY)
+            n0 = c * CHUNK - late * EARLY
+            src = w_raw[(part, late)][:, :, :, n0:n0 + CHUNK].rearrange("p h t (c i) -> p h c t i", i=4)
+            laced[k] = work.tile([P, UNIT], U8, name="w_laced", bufs=4)
+            dst = laced[k][:].rearrange("p (h c i t) -> p h c t i", h=2, i=4, t=4)
+            nc.vector.tensor_copy(out=dst, in_=src)
 
-        xq = {}
-
-        def turn(words, g0, name, gr, goff):
-            bank = psum.tile([P, 2, 2, P], F32, name="turn")
+        def widen_w(k, on_vector=False):
+            c, part = divmod(k, PARTS)
+            wide[k] = work.tile([P, UNIT], BF16, align_bytes=64, name="w_wide")
             for h in range(2):
-                for u in range(2):
-                    s = 256 * (g0 + h) + u
-                    nc.tensor.transpose(bank[:, h, u, :], words[:, s:256 * (g0 + h + 1):2], ident[:])
-            dst = gr[:, goff:goff + 1024].bitcast(F32).rearrange("p (h r u) -> p h r u", h=2, u=2)
-            nc.scalar.copy(out=dst, in_=bank[:].rearrange("p h u r -> p h r u"))
+                for j in range(CHUNK // B):
+                    cols = slice(4 * (h * CHUNK + j * B), 4 * (h * CHUNK + (j + 1) * B))
+                    col_block = c * CHUNK // B + j
+                    scale = w_scales[:, 2 * part + h, col_block:col_block + 1]
+                    src = laced[k][:, cols].bitcast(FP8)
+                    if on_vector:
+                        nc.vector.tensor_scalar(out=wide[k][:, cols], in0=src, scalar1=scale, scalar2=None, op0=MULT)
+                    else:
+                        nc.scalar.activation(out=wide[k][:, cols], in_=src, func=ACT.Copy, scale=scale)
 
-        def prep_x(m):
-            ge = work.tile([P, E], BF16, align_bytes=64, name="ge")
-            turn(eb[m][:].bitcast(F32), 0, "e", ge, 0)
-            ec = once.tile([P, E // 4], U32, align_bytes=64, name="ec%d" % m)
-            es = once.tile([P, E // 4], U8, align_bytes=64, name="es%d" % m)
-            nc.vector.quantize_mx(out=ec[:].bitcast(FP8X4), scales=es[:], in_=ge[:])
-            fw = work.tile([P, D], BF16, name="fw")
+        def quantise(src, name, bufs):
+            codes = work.tile([P, 512], U32, align_bytes=64, name=name + "_codes", bufs=bufs)
+            scales = work.tile([P, 512], U8, align_bytes=64, name=name + "_scales", bufs=bufs)
+            nc.vector.quantize_mx(out=codes[:].bitcast(FP8X4), scales=scales[:], in_=src[:])
+            return codes, scales
+
+        def quant_w(k):
+            w_mx[k] = quantise(wide[k], "w", 8)
+
+        f_wide = {}
+        turned = {}
+        x_mx = {}
+
+        def scale_f(m):
+            f_wide[m] = work.tile([P, D], BF16, name="f_wide")
             for j in range(F_BLOCKS):
-                cols = slice(j * P, (j + 1) * P)
-                sc = fs[:, m * F_BLOCKS + j:m * F_BLOCKS + j + 1]
-                if j < F_ON_SCALAR:
-                    nc.scalar.activation(out=fw[:, cols], in_=fb[m][:, cols].bitcast(FP8), func=ACT.Copy, scale=sc)
+                src = f_raw[m][:, j * B:(j + 1) * B].bitcast(FP8)
+                scale = f_scales[:, m * F_BLOCKS + j:m * F_BLOCKS + j + 1]
+                if m in F_ON_SCALAR:
+                    nc.scalar.activation(out=f_wide[m][:, j * B:(j + 1) * B], in_=src, func=ACT.Copy, scale=scale)
                 else:
-                    nc.vector.tensor_scalar(out=fw[:, cols], in0=fb[m][:, cols].bitcast(FP8), scalar1=sc,
-                                            scalar2=None, op0=MULT)
-            gf = work.tile([P, D], BF16, align_bytes=64, name="gf")
-            turn(fw[:].bitcast(F32), 0, "f", gf, 0)
-            turn(fw[:].bitcast(F32), 2, "f", gf, 1024)
-            fc = once.tile([P, D // 4], U32, align_bytes=64, name="fc%d" % m)
-            fsc = once.tile([P, D // 4], U8, align_bytes=64, name="fsc%d" % m)
-            nc.vector.quantize_mx(out=fc[:].bitcast(FP8X4), scales=fsc[:], in_=gf[:])
-            for g in range(E_PASSES):
-                xq[(m, g)] = (ec, es, slice(g * P, (g + 1) * P))
-            for g in range(F_PASSES):
-                xq[(m, E_PASSES + g)] = (fc, fsc, slice(g * P, (g + 1) * P))
+                    g, q = divmod(j, 4)
+                    halves = f_wide[m][:, g * K_PASS:(g + 1) * K_PASS].rearrange("p (u r e) -> p r u e", u=2, e=2)
+                    nc.vector.tensor_scalar(out=halves[:, 32 * q:32 * q + 32], in0=src.rearrange("p (r u e) -> p r u e", u=2, e=2),
+                                            scalar1=scale, scalar2=None, op0=MULT)
 
-        def mm(acc, m, c, passes):
-            for g in passes:
-                xc, xs, xcols = xq[(m, g)]
-                wc, wsc, wcols = wq[(c, g)]
-                nc.tensor.matmul_mx(out=acc, lhsT=xc[:, xcols].bitcast(FP8X4), lhsT_scale=xs[:, xcols],
-                                    rhs=wc[:, wcols].bitcast(FP8X4), rhs_scale=wsc[:, wcols],
-                                    start=(g == passes[0]), stop=(g == passes[-1]))
+        def turn(src, key, sorted_words):
+            words = src[:].bitcast(F32)
+            turned[key] = work.tile([P, 2048], BF16, align_bytes=64, name="turned", bufs=4)
+            banks = []
+            for half in range(2):
+                bank = psum.tile([P, 2, 2, P], F32, name="bank%d" % ((2 * len(turned) + half) % 4))
+                for h in range(2):
+                    w0 = 256 * (2 * half + h)
+                    for u in range(2):
+                        cols = slice(w0 + P * u, w0 + P * (u + 1)) if sorted_words else slice(w0 + u, w0 + 256, 2)
+                        nc.tensor.transpose(bank[:, h, u, :], words[:, cols], ident[:])
+                banks.append(bank)
+            for half in range(2):
+                dst = turned[key][:, 1024 * half:1024 * (half + 1)].bitcast(F32).rearrange("p (h r u) -> p h r u", h=2, u=2)
+                nc.scalar.copy(out=dst, in_=banks[half][:].rearrange("p h u r -> p h r u"))
 
-        def product(m, c):
-            n0, width = CHUNKS[c]
-            acc_a = psum.tile([P, 512], F32, name="acc", bufs=6)
-            a = acc_a[:, 0:width]
-            if width == 512:
-                acc_c = psum.tile([P, 512], F32, name="acc", bufs=6)
-                cc = acc_c[:, 0:width]
-            else:
-                cc = acc_a[:, width:2 * width]
-            mm(a, m, c, list(range(E_PASSES)))
-            mm(cc, m, c, list(range(E_PASSES, PASSES)))
-            t = work.tile([P, 512], F32, name="t")
-            nc.vector.tensor_tensor(out=t[:, 0:width], in0=a, in1=bt[:, n0:n0 + width], op=ADD)
-            z = work.tile([P, 512], F32, name="z")
-            nc.vector.scalar_tensor_tensor(out=z[:, 0:width], in0=cc, scalar=tr[:, m:m + 1], in1=t[:, 0:width],
-                                           op0=MULT, op1=ADD)
-            o = work.tile([P, 512], F32, name="o", bufs=4)
-            nc.scalar.activation(out=o[:, 0:width], in_=z[:, 0:width], func=ACT.Silu)
-            nc.sync.dma_start(out=o_v[:, m, n0:n0 + width], in_=o[:, 0:width])
+        def turn_e(pair):
+            turn(e_raw[pair], ("e", pair), False)
 
-        prep_w(*c0[0])
-        prep_x(0)
-        for u in c0[1:]:
-            prep_w(*u)
-        prep_x(1)
-        for m in range(M_TILES):
-            product(m, 0)
-            if m + 2 < M_TILES:
-                prep_x(m + 2)
-        for c in range(1, len(CHUNKS)):
-            for u in units:
-                if u[0] == c:
-                    prep_w(*u)
-            for m in range(M_TILES):
-                product(m, c)
+        def turn_f(m):
+            turn(f_wide[m], ("f", m), m not in F_ON_SCALAR)
+
+        def quant_e(pair):
+            x_mx[("e", pair)] = quantise(turned[("e", pair)], "e", PAIRS)
+
+        def quant_f(m):
+            x_mx[("f", m)] = quantise(turned[("f", m)], "f", TILES)
+
+        def passes(acc, x, x_first, c, parts):
+            steps = [(part, h) for part in parts for h in range(2)]
+            for i, (part, h) in enumerate(steps):
+                x_cols = slice((x_first + i) * P, (x_first + i + 1) * P)
+                w_cols = slice(h * CHUNK, (h + 1) * CHUNK)
+                w = w_mx[c * PARTS + part]
+                nc.tensor.matmul_mx(out=acc, lhsT=x[0][:, x_cols].bitcast(FP8X4), lhsT_scale=x[1][:, x_cols],
+                                    rhs=w[0][:, w_cols].bitcast(FP8X4), rhs_scale=w[1][:, w_cols],
+                                    start=(i == 0), stop=(i == len(steps) - 1))
+
+        a_bank = {}
+        c_bank = {}
+        a_plus_b = {}
+
+        def mm_a(s):
+            c, pair = divmod(s, PAIRS)
+            a_bank[s] = psum.tile([P, 2, CHUNK], F32, name="bank%d" % (4 + len(a_bank) % 2 if s < 2 * PAIRS - 1 else s % 4))
+            for i in range(2):
+                passes(a_bank[s][:, i, :], x_mx[("e", pair)], 2 * i, c, [0])
+
+        def add_b(s):
+            c = s // PAIRS
+            a_plus_b[s] = work.tile([P, 2, CHUNK], F32, name="a_plus_b", bufs=6)
+            row = bias[:, c * CHUNK:(c + 1) * CHUNK].unsqueeze(1).to_broadcast([P, 2, CHUNK])
+            nc.vector.tensor_tensor(out=a_plus_b[s][:], in0=a_bank[s][:], in1=row, op=ADD)
+
+        def mm_c(s):
+            c, pair = divmod(s, PAIRS)
+            c_bank[s] = psum.tile([P, 2, CHUNK], F32, name="bank%d" % (6 + s % 2 if s < PAIRS else 4 + (s + 2) % 4))
+            for i in range(2):
+                passes(c_bank[s][:, i, :], x_mx[("f", 2 * pair + i)], 0, c, [1, 2])
+
+        def finish(s):
+            c, pair = divmod(s, PAIRS)
+            z = work.tile([P, 2, CHUNK], F32, name="z")
+            for i in range(2):
+                m = 2 * pair + i
+                nc.vector.scalar_tensor_tensor(out=z[:, i, :], in0=c_bank[s][:, i, :], scalar=trusts[:, m:m + 1],
+                                               in1=a_plus_b[s][:, i, :], op0=MULT, op1=ADD)
+            res = work.tile([P, 2, CHUNK], F32, name="res", bufs=5)
+            nc.scalar.activation(out=res[:], in_=z[:], func=ACT.Silu)
+            nc.sync.dma_start(out=o_v[:, 2 * pair:2 * pair + 2, c * CHUNK:(c + 1) * CHUNK], in_=res[:])
+
+        lace_w(0)
+        scale_f(0)
+        widen_w(0, on_vector=True)
+        turn_e(0)
+        scale_f(1)
+        turn_f(0)
+        quant_w(0)
+        lace_w(1)
+        widen_w(1)
+        quant_e(0)
+        lace_w(2)
+        turn_f(1)
+        quant_f(0)
+        widen_w(2)
+        mm_a(0)
+        lace_w(3)
+        quant_w(1)
+        scale_f(2)
+        quant_f(1)
+        quant_w(2)
+        for pair in range(PAIRS - 1):
+            nxt = pair + 1
+            k = PARTS + pair
+            turn_e(nxt)
+            mm_c(pair)
+            turn_f(2 * nxt)
+            widen_w(k)
+            add_b(pair)
+            scale_f(2 * nxt + 1)
+            quant_e(nxt)
+            finish(pair)
+            turn_f(2 * nxt + 1)
+            quant_f(2 * nxt)
+            mm_a(nxt)
+            lace_w(k + 1)
+            quant_w(k)
+            if pair > 0:
+                mm_a(PAIRS + pair - 1)
+            if nxt + 1 < PAIRS:
+                scale_f(2 * nxt + 2)
+            if pair > 0:
+                add_b(PAIRS + pair - 1)
+            quant_f(2 * nxt + 1)
+        mm_c(PAIRS - 1)
+        widen_w(2 * PARTS)
+        add_b(PAIRS - 1)
+        mm_a(PAIRS + 2)
+        lace_w(2 * PARTS + 1)
+        for s in range(PAIRS, CHUNKS * PAIRS):
+            c, pair = divmod(s, PAIRS)
+            k = (c + 1) * PARTS + pair
+            mm_c(s)
+            if pair < PARTS and k + 1 < UNITS:
+                widen_w(k + 1)
+            if pair < PARTS and k < UNITS:
+                quant_w(k)
+            if s + 2 < CHUNKS * PAIRS:
+                add_b(s + 2)
+            if s + 3 < CHUNKS * PAIRS:
+                mm_a(s + 3)
+            if pair < PARTS and k + 2 < UNITS:
+                lace_w(k + 2)
+            finish(s - 1)
+        finish(CHUNKS * PAIRS - 1)

@@ -1,7 +1,7 @@
 from contextlib import ExitStack
 
 import concourse.mybir as mybir
-from concourse.masks import make_identity
+from concourse.masks import make_block_diagonal, make_identity
 
 T, E, D, N = 1024, 1024, 2048, 1536
 FLOPS = 2 * T * (E + D) * N
@@ -31,7 +31,10 @@ PARTS = PASSES // 2
 UNITS = CHUNKS * PARTS
 UNIT = 2 * 4 * CHUNK
 EARLY = 512
-F_ON_SCALAR = (0,)
+C_LAG = 3
+A_LEAD = 3
+A_LAG = 2
+F_PASSES_ON_SCALAR = 1
 
 
 def tile_drafter_feature_fusion_d2_kernel(tc, e, f_bytes, f_scale, w_bytes, w_scale, trust, b, out):
@@ -40,6 +43,8 @@ def tile_drafter_feature_fusion_d2_kernel(tc, e, f_bytes, f_scale, w_bytes, w_sc
         once = ctx.enter_context(tc.tile_pool(name="once", bufs=1))
         work = ctx.enter_context(tc.tile_pool(name="work", bufs=3))
         psum = ctx.enter_context(tc.psum_pool(name="psum", bufs=1))
+        quadrants = once.tile([P, P], F32)
+        make_block_diagonal(nc, quadrants[:], 32)
         ctx.enter_context(tc.manual_schedule())
 
         e_v = e.rearrange("(p m) k -> p m k", m=TILES)
@@ -49,8 +54,9 @@ def tile_drafter_feature_fusion_d2_kernel(tc, e, f_bytes, f_scale, w_bytes, w_sc
 
         f_scales = once.tile([P, TILES * F_BLOCKS], F32)
         nc.scalar.dma_start(out=f_scales[:], in_=f_scale.rearrange("(p m) j -> p (m j)", m=TILES))
-        w_scale_all = once.tile([P, 4 * PASSES * W_BLOCKS], F32)
-        nc.scalar.dma_start(out=w_scale_all[:], in_=w_scale.rearrange("r j -> (r j)").partition_broadcast(P))
+        w_scale_rows = once.tile([P, PASSES, W_BLOCKS], F32)
+        nc.vector.memset(w_scale_rows[:], 0.0)
+        nc.scalar.dma_start(out=w_scale_rows[0:P:32], in_=w_scale.rearrange("(g q) j -> q g j", q=4))
 
         w_raw = {}
         e_raw = {}
@@ -80,24 +86,32 @@ def tile_drafter_feature_fusion_d2_kernel(tc, e, f_bytes, f_scale, w_bytes, w_sc
         load_w(1, 0)
         load_w(2, 0)
         bias = once.tile([P, N], BF16)
-        nc.sync.dma_start(out=bias[:], in_=b.partition_broadcast(P))
         trusts = once.tile([P, TILES], BF16)
-        nc.sync.dma_start(out=trusts[:], in_=trust.rearrange("(p m) o -> p (m o)", m=TILES))
         for pair in range(1, PAIRS):
             load_f(2 * pair)
             load_e(pair)
             load_f(2 * pair + 1)
+            if pair == 1:
+                nc.sync.dma_start(out=bias[:, 0:EARLY], in_=b[0:EARLY].partition_broadcast(P))
+                nc.sync.dma_start(out=trusts[:], in_=trust.rearrange("(p m) o -> p (m o)", m=TILES))
         for part in range(PARTS):
             load_w(part, 1)
+        nc.sync.dma_start(out=bias[:, EARLY:N], in_=b[EARLY:N].partition_broadcast(P))
+
+        free_banks = list(range(8))
+
+        def take_bank(shape):
+            number = free_banks.pop(0)
+            return number, psum.tile(shape, F32, name="bank%d" % number)
 
         ident = once.tile([P, P], F32)
         make_identity(nc, ident[:])
 
         w_scales = once.tile([P, PASSES, W_BLOCKS], F32)
-        all_v = w_scale_all[:].rearrange("p (g q j) -> p g q j", g=PASSES, q=4)
-        for q in range(4):
-            rows = slice(32 * q, 32 * q + 32)
-            nc.gpsimd.tensor_copy(out=w_scales[rows, :, :], in_=all_v[rows, :, q, :])
+        number, bank = take_bank([P, PASSES * W_BLOCKS])
+        nc.tensor.matmul(bank[:], lhsT=quadrants[:], rhs=w_scale_rows[:].rearrange("p g j -> p (g j)"), start=True, stop=True)
+        nc.scalar.copy(out=w_scales[:].rearrange("p g j -> p (g j)"), in_=bank[:])
+        free_banks.append(number)
 
         laced = {}
         wide = {}
@@ -136,43 +150,44 @@ def tile_drafter_feature_fusion_d2_kernel(tc, e, f_bytes, f_scale, w_bytes, w_sc
             w_mx[k] = quantise(wide[k], "w", 8)
 
         f_wide = {}
+        natural = {}
         turned = {}
         x_mx = {}
 
-        def scale_f(m):
-            f_wide[m] = work.tile([P, D], BF16, name="f_wide")
-            for j in range(F_BLOCKS):
+        def scale_f(m, on_scalar, part):
+            if m not in f_wide:
+                f_wide[m] = work.tile([P, D], BF16, name="f_wide")
+            natural[m] = on_scalar
+            for j in (range(4 * on_scalar) if part == "scalar" else range(4 * on_scalar, F_BLOCKS)):
+                g, q = divmod(j, 4)
                 src = f_raw[m][:, j * B:(j + 1) * B].bitcast(FP8)
                 scale = f_scales[:, m * F_BLOCKS + j:m * F_BLOCKS + j + 1]
-                if m in F_ON_SCALAR:
+                if g < on_scalar:
                     nc.scalar.activation(out=f_wide[m][:, j * B:(j + 1) * B], in_=src, func=ACT.Copy, scale=scale)
                 else:
-                    g, q = divmod(j, 4)
                     halves = f_wide[m][:, g * K_PASS:(g + 1) * K_PASS].rearrange("p (u r e) -> p r u e", u=2, e=2)
                     nc.vector.tensor_scalar(out=halves[:, 32 * q:32 * q + 32], in0=src.rearrange("p (r u e) -> p r u e", u=2, e=2),
                                             scalar1=scale, scalar2=None, op0=MULT)
 
-        def turn(src, key, sorted_words):
+        def turn(src, key, unsorted):
             words = src[:].bitcast(F32)
             turned[key] = work.tile([P, 2048], BF16, align_bytes=64, name="turned", bufs=4)
-            banks = []
             for half in range(2):
-                bank = psum.tile([P, 2, 2, P], F32, name="bank%d" % ((2 * len(turned) + half) % 4))
+                number, bank = take_bank([P, 2, 2, P])
                 for h in range(2):
-                    w0 = 256 * (2 * half + h)
+                    g = 2 * half + h
                     for u in range(2):
-                        cols = slice(w0 + P * u, w0 + P * (u + 1)) if sorted_words else slice(w0 + u, w0 + 256, 2)
+                        cols = slice(256 * g + u, 256 * (g + 1), 2) if g < unsorted else slice(256 * g + P * u, 256 * g + P * (u + 1))
                         nc.tensor.transpose(bank[:, h, u, :], words[:, cols], ident[:])
-                banks.append(bank)
-            for half in range(2):
                 dst = turned[key][:, 1024 * half:1024 * (half + 1)].bitcast(F32).rearrange("p (h r u) -> p h r u", h=2, u=2)
-                nc.scalar.copy(out=dst, in_=banks[half][:].rearrange("p h u r -> p h r u"))
+                nc.scalar.copy(out=dst, in_=bank[:].rearrange("p h u r -> p h r u"))
+                free_banks.append(number)
 
         def turn_e(pair):
-            turn(e_raw[pair], ("e", pair), False)
+            turn(e_raw[pair], ("e", pair), 4)
 
         def turn_f(m):
-            turn(f_wide[m], ("f", m), m not in F_ON_SCALAR)
+            turn(f_wide[m], ("f", m), natural[m])
 
         def quant_e(pair):
             x_mx[("e", pair)] = quantise(turned[("e", pair)], "e", PAIRS)
@@ -196,94 +211,109 @@ def tile_drafter_feature_fusion_d2_kernel(tc, e, f_bytes, f_scale, w_bytes, w_sc
 
         def mm_a(s):
             c, pair = divmod(s, PAIRS)
-            a_bank[s] = psum.tile([P, 2, CHUNK], F32, name="bank%d" % (4 + len(a_bank) % 2 if s < 2 * PAIRS - 1 else s % 4))
+            a_bank[s] = take_bank([P, 2, CHUNK])
             for i in range(2):
-                passes(a_bank[s][:, i, :], x_mx[("e", pair)], 2 * i, c, [0])
+                passes(a_bank[s][1][:, i, :], x_mx[("e", pair)], 2 * i, c, [0])
 
         def add_b(s):
             c = s // PAIRS
-            a_plus_b[s] = work.tile([P, 2, CHUNK], F32, name="a_plus_b", bufs=6)
+            a_plus_b[s] = work.tile([P, 2, CHUNK], F32, name="a_plus_b", bufs=8)
             row = bias[:, c * CHUNK:(c + 1) * CHUNK].unsqueeze(1).to_broadcast([P, 2, CHUNK])
-            nc.vector.tensor_tensor(out=a_plus_b[s][:], in0=a_bank[s][:], in1=row, op=ADD)
+            nc.vector.tensor_tensor(out=a_plus_b[s][:], in0=a_bank[s][1][:], in1=row, op=ADD)
+            free_banks.append(a_bank[s][0])
 
         def mm_c(s):
             c, pair = divmod(s, PAIRS)
-            c_bank[s] = psum.tile([P, 2, CHUNK], F32, name="bank%d" % (6 + s % 2 if s < PAIRS else 4 + (s + 2) % 4))
+            c_bank[s] = take_bank([P, 2, CHUNK])
             for i in range(2):
-                passes(c_bank[s][:, i, :], x_mx[("f", 2 * pair + i)], 0, c, [1, 2])
+                passes(c_bank[s][1][:, i, :], x_mx[("f", 2 * pair + i)], 0, c, [1, 2])
+
+        sums = {}
+
+        def join(s):
+            pair = s % PAIRS
+            z = sums[s] = work.tile([P, 2, CHUNK], F32, name="z", bufs=4)
+            for i in range(2):
+                m = 2 * pair + i
+                nc.vector.scalar_tensor_tensor(out=z[:, i, :], in0=c_bank[s][1][:, i, :], scalar=trusts[:, m:m + 1],
+                                               in1=a_plus_b[s][:, i, :], op0=MULT, op1=ADD)
+            free_banks.append(c_bank[s][0])
 
         def finish(s):
             c, pair = divmod(s, PAIRS)
-            z = work.tile([P, 2, CHUNK], F32, name="z")
-            for i in range(2):
-                m = 2 * pair + i
-                nc.vector.scalar_tensor_tensor(out=z[:, i, :], in0=c_bank[s][:, i, :], scalar=trusts[:, m:m + 1],
-                                               in1=a_plus_b[s][:, i, :], op0=MULT, op1=ADD)
             res = work.tile([P, 2, CHUNK], F32, name="res", bufs=5)
-            nc.scalar.activation(out=res[:], in_=z[:], func=ACT.Silu)
+            nc.scalar.activation(out=res[:], in_=sums[s][:], func=ACT.Silu)
             nc.sync.dma_start(out=o_v[:, 2 * pair:2 * pair + 2, c * CHUNK:(c + 1) * CHUNK], in_=res[:])
 
         lace_w(0)
-        scale_f(0)
+        scale_f(0, F_PASSES, "scalar")
         widen_w(0, on_vector=True)
         turn_e(0)
-        scale_f(1)
+        scale_f(1, 0, "vector")
         turn_f(0)
         quant_w(0)
         lace_w(1)
         widen_w(1)
         quant_e(0)
         lace_w(2)
-        turn_f(1)
-        quant_f(0)
-        widen_w(2)
         mm_a(0)
         lace_w(3)
-        quant_w(1)
-        scale_f(2)
-        quant_f(1)
-        quant_w(2)
-        for pair in range(PAIRS - 1):
-            nxt = pair + 1
-            k = PARTS + pair
-            turn_e(nxt)
-            mm_c(pair)
-            turn_f(2 * nxt)
-            widen_w(k)
-            add_b(pair)
-            scale_f(2 * nxt + 1)
-            quant_e(nxt)
-            finish(pair)
-            turn_f(2 * nxt + 1)
-            quant_f(2 * nxt)
-            mm_a(nxt)
-            lace_w(k + 1)
-            quant_w(k)
-            if pair > 0:
-                mm_a(PAIRS + pair - 1)
-            if nxt + 1 < PAIRS:
-                scale_f(2 * nxt + 2)
-            if pair > 0:
-                add_b(PAIRS + pair - 1)
-            quant_f(2 * nxt + 1)
+        for m in range(TILES):
+            pair, odd = divmod(m, 2)
+            k = PARTS + pair - 1
+            if m + 2 < TILES:
+                scale_f(m + 2, F_PASSES_ON_SCALAR, "scalar")
+            if m + 1 < TILES:
+                turn_f(m + 1)
+            if not odd and pair > 0:
+                mm_c(pair - 1)
+                mm_a(pair)
+            if m >= PAIRS:
+                mm_a(m)
+            if not odd:
+                widen_w(k)
+            quant_f(m)
+            if m + 2 < TILES:
+                scale_f(m + 2, F_PASSES_ON_SCALAR, "vector")
+            if m == 0:
+                quant_w(1)
+            if odd:
+                quant_w(k)
+                add_b(pair)
+                if pair > 0:
+                    join(pair - 1)
+                if pair + 1 < PAIRS:
+                    quant_e(pair + 1)
+            else:
+                if pair + 1 < PAIRS:
+                    turn_e(pair + 1)
+                lace_w(k + 2)
+                if pair > 1:
+                    finish(pair - 2)
+            if m > PAIRS:
+                add_b(m - 1)
         mm_c(PAIRS - 1)
         widen_w(2 * PARTS)
-        add_b(PAIRS - 1)
-        mm_a(PAIRS + 2)
-        lace_w(2 * PARTS + 1)
-        for s in range(PAIRS, CHUNKS * PAIRS):
+        add_b(TILES - 1)
+        finish(PAIRS - 2)
+        lace_w(2 * PARTS + 2)
+        last = CHUNKS * PAIRS
+        for s in range(PAIRS, last + C_LAG + 1):
             c, pair = divmod(s, PAIRS)
             k = (c + 1) * PARTS + pair
-            mm_c(s)
+            if s - C_LAG - 1 >= PAIRS - 1:
+                finish(s - C_LAG - 1)
+            if PAIRS - 1 <= s - C_LAG < last:
+                join(s - C_LAG)
+            if s < last:
+                mm_c(s)
             if pair < PARTS and k + 1 < UNITS:
                 widen_w(k + 1)
+            if TILES <= s + A_LEAD - A_LAG < last:
+                add_b(s + A_LEAD - A_LAG)
+            if TILES <= s + A_LEAD < last:
+                mm_a(s + A_LEAD)
             if pair < PARTS and k < UNITS:
                 quant_w(k)
-            if s + 2 < CHUNKS * PAIRS:
-                add_b(s + 2)
-            if s + 3 < CHUNKS * PAIRS:
-                mm_a(s + 3)
-            if pair < PARTS and k + 2 < UNITS:
-                lace_w(k + 2)
-            finish(s - 1)
-        finish(CHUNKS * PAIRS - 1)
+            if pair < PARTS and k + 3 < UNITS:
+                lace_w(k + 3)

@@ -58,6 +58,9 @@ def tile_drafter_feature_fusion_d2_kernel(tc, e, f_bytes, f_scale, w_bytes, w_sc
         nc.vector.memset(w_scale_rows[:], 0.0)
         nc.scalar.dma_start(out=w_scale_rows[0:P:32], in_=w_scale.rearrange("(g q) j -> q g j", q=4))
 
+        warm = once.tile([P, 1], F32)
+        nc.scalar.activation(out=warm[:], in_=quadrants[:, 0:1], func=ACT.Silu)
+
         w_raw = {}
         e_raw = {}
         f_raw = {}

@@ -31,9 +31,11 @@ PARTS = PASSES // 2
 UNITS = CHUNKS * PARTS
 UNIT = 2 * 4 * CHUNK
 EARLY = 512
-C_LAG = 3
-A_LEAD = 3
+C_LAG = 2
+A_LEAD = 2
 A_LAG = 2
+G_BLOCKS = 2
+W_ON_VECTOR = 0
 F_PASSES_ON_SCALAR = 1
 
 
@@ -43,6 +45,8 @@ def tile_drafter_feature_fusion_d2_kernel(tc, e, f_bytes, f_scale, w_bytes, w_sc
         once = ctx.enter_context(tc.tile_pool(name="once", bufs=1))
         work = ctx.enter_context(tc.tile_pool(name="work", bufs=3))
         psum = ctx.enter_context(tc.psum_pool(name="psum", bufs=1))
+        w_scale_rows = once.tile([P, PASSES, W_BLOCKS], F32)
+        nc.gpsimd.memset(w_scale_rows[:], 0.0)
         quadrants = once.tile([P, P], F32)
         make_block_diagonal(nc, quadrants[:], 32)
         ctx.enter_context(tc.manual_schedule())
@@ -54,8 +58,6 @@ def tile_drafter_feature_fusion_d2_kernel(tc, e, f_bytes, f_scale, w_bytes, w_sc
 
         f_scales = once.tile([P, TILES * F_BLOCKS], F32)
         nc.scalar.dma_start(out=f_scales[:], in_=f_scale.rearrange("(p m) j -> p (m j)", m=TILES))
-        w_scale_rows = once.tile([P, PASSES, W_BLOCKS], F32)
-        nc.vector.memset(w_scale_rows[:], 0.0)
         nc.scalar.dma_start(out=w_scale_rows[0:P:32], in_=w_scale.rearrange("(g q) j -> q g j", q=4))
 
         warm = once.tile([P, 1], F32)
@@ -65,12 +67,12 @@ def tile_drafter_feature_fusion_d2_kernel(tc, e, f_bytes, f_scale, w_bytes, w_sc
         e_raw = {}
         f_raw = {}
 
-        def load_w(part, late):
+        def load_w(part, late, halves=(0, 1)):
             cols = slice(EARLY, N) if late else slice(0, EARLY)
-            raw = once.tile([P, 2, 4, cols.stop - cols.start], U8, name="w_raw%d_%d" % (part, late))
-            for h in range(2):
-                nc.sync.dma_start(out=raw[:, h], in_=w_v[:, 2 * part + h, :, cols])
-            w_raw[(part, late)] = raw
+            if (part, late) not in w_raw:
+                w_raw[(part, late)] = once.tile([P, 2, 4, cols.stop - cols.start], U8, name="w_raw%d_%d" % (part, late))
+            for h in halves:
+                nc.sync.dma_start(out=w_raw[(part, late)][:, h], in_=w_v[:, 2 * part + h, :, cols])
 
         def load_e(pair):
             raw = once.tile([P, 2 * E], BF16, name="e_raw%d" % pair)
@@ -82,8 +84,9 @@ def tile_drafter_feature_fusion_d2_kernel(tc, e, f_bytes, f_scale, w_bytes, w_sc
             nc.sync.dma_start(out=raw[:], in_=f_v[:, m, :])
             f_raw[m] = raw
 
-        load_w(0, 0)
+        load_w(0, 0, [0])
         load_f(0)
+        load_w(0, 0, [1])
         load_e(0)
         load_f(1)
         load_w(1, 0)
@@ -119,29 +122,53 @@ def tile_drafter_feature_fusion_d2_kernel(tc, e, f_bytes, f_scale, w_bytes, w_sc
         laced = {}
         wide = {}
         w_mx = {}
+        lent = {}
+        free_slots = list(range(5))
 
-        def lace_w(k):
+        def raw_columns(k):
             c, part = divmod(k, PARTS)
             late = int(c * CHUNK >= EARLY)
             n0 = c * CHUNK - late * EARLY
-            src = w_raw[(part, late)][:, :, :, n0:n0 + CHUNK].rearrange("p h t (c i) -> p h c t i", i=4)
-            laced[k] = work.tile([P, UNIT], U8, name="w_laced", bufs=4)
-            dst = laced[k][:].rearrange("p (h c i t) -> p h c t i", h=2, i=4, t=4)
-            nc.vector.tensor_copy(out=dst, in_=src)
+            return w_raw[(part, late)][:, :, :, n0:n0 + CHUNK]
 
-        def widen_w(k, on_vector=False):
-            c, part = divmod(k, PARTS)
-            wide[k] = work.tile([P, UNIT], BF16, align_bytes=64, name="w_wide")
-            for h in range(2):
-                for j in range(CHUNK // B):
-                    cols = slice(4 * (h * CHUNK + j * B), 4 * (h * CHUNK + (j + 1) * B))
-                    col_block = c * CHUNK // B + j
-                    scale = w_scales[:, 2 * part + h, col_block:col_block + 1]
-                    src = laced[k][:, cols].bitcast(FP8)
-                    if on_vector:
-                        nc.vector.tensor_scalar(out=wide[k][:, cols], in0=src, scalar1=scale, scalar2=None, op0=MULT)
-                    else:
-                        nc.scalar.activation(out=wide[k][:, cols], in_=src, func=ACT.Copy, scale=scale)
+        def lace_w(k, blocks=range(4)):
+            tile = work.tile([P, len(blocks) * 4 * B], U8, name="w_laced", bufs=4)
+            whole = len(blocks) // 2 if blocks[0] % 2 == 0 else 0
+            if whole:
+                src = raw_columns(k)[:, blocks[0] // 2:blocks[0] // 2 + whole].rearrange("p h t (c i) -> p h c t i", i=4)
+                nc.vector.tensor_copy(out=tile[:, 0:whole * 4 * CHUNK].rearrange("p (h c i t) -> p h c t i", h=whole, i=4, t=4), in_=src)
+            for n in range(2 * whole, len(blocks)):
+                h, j = divmod(blocks[n], 2)
+                src = raw_columns(k)[:, h, :, j * B:(j + 1) * B].rearrange("p t (c i) -> p c t i", i=4)
+                nc.vector.tensor_copy(out=tile[:, n * 4 * B:(n + 1) * 4 * B].rearrange("p (c i t) -> p c t i", i=4, t=4), in_=src)
+            for n, block in enumerate(blocks):
+                laced[(k, block)] = tile[:, n * 4 * B:(n + 1) * 4 * B]
+
+        def lace_w_gpsimd(k, count):
+            slot = lent[k] = free_slots.pop()
+            tile = work.tile([P, count * 4 * B], U8, align_bytes=64, name="w_laced_late", tag="slot%d" % slot, bufs=1)
+            src = raw_columns(k)[:, 1, :, CHUNK - count * B:CHUNK]
+            nc.gpsimd.tensor_copy(out=tile[:].rearrange("p (c t) -> p c t", t=4), in_=src.rearrange("p t c -> p c t"))
+            for n in range(count):
+                laced[(k, 4 - count + n)] = tile[:, n * 4 * B:(n + 1) * 4 * B]
+
+        def widen_w(k, blocks=range(4), part="scalar"):
+            c, w_part = divmod(k, PARTS)
+            if k not in wide:
+                slot = free_slots.pop(0)
+                wide[k] = (work.tile([P, UNIT], BF16, align_bytes=64, name="w_wide", tag="slot%d" % slot, bufs=1), slot)
+            for block in blocks:
+                h, j = divmod(block, 2)
+                col_block = c * CHUNK // B + j
+                scale = w_scales[:, 2 * w_part + h, col_block:col_block + 1]
+                src = laced[(k, block)].bitcast(FP8)
+                dst = wide[k][0][:, 4 * B * block:4 * B * (block + 1)]
+                if part == "vector":
+                    nc.vector.tensor_scalar(out=dst, in0=src, scalar1=scale, scalar2=None, op0=MULT)
+                else:
+                    nc.scalar.activation(out=dst, in_=src, func=ACT.Copy, scale=scale)
+            if part == "scalar" and k in lent:
+                free_slots.append(lent[k])
 
         def quantise(src, name, bufs):
             codes = work.tile([P, 512], U32, align_bytes=64, name=name + "_codes", bufs=bufs)
@@ -150,7 +177,8 @@ def tile_drafter_feature_fusion_d2_kernel(tc, e, f_bytes, f_scale, w_bytes, w_sc
             return codes, scales
 
         def quant_w(k):
-            w_mx[k] = quantise(wide[k], "w", 8)
+            w_mx[k] = quantise(wide[k][0], "w", 9)
+            free_slots.append(wide[k][1])
 
         f_wide = {}
         natural = {}
@@ -198,7 +226,7 @@ def tile_drafter_feature_fusion_d2_kernel(tc, e, f_bytes, f_scale, w_bytes, w_sc
         def quant_f(m):
             x_mx[("f", m)] = quantise(turned[("f", m)], "f", TILES)
 
-        def passes(acc, x, x_first, c, parts):
+        def passes(acc, x, x_first, c, parts, start=True, stop=True):
             steps = [(part, h) for part in parts for h in range(2)]
             for i, (part, h) in enumerate(steps):
                 x_cols = slice((x_first + i) * P, (x_first + i + 1) * P)
@@ -206,7 +234,7 @@ def tile_drafter_feature_fusion_d2_kernel(tc, e, f_bytes, f_scale, w_bytes, w_sc
                 w = w_mx[c * PARTS + part]
                 nc.tensor.matmul_mx(out=acc, lhsT=x[0][:, x_cols].bitcast(FP8X4), lhsT_scale=x[1][:, x_cols],
                                     rhs=w[0][:, w_cols].bitcast(FP8X4), rhs_scale=w[1][:, w_cols],
-                                    start=(i == 0), stop=(i == len(steps) - 1))
+                                    start=(start and i == 0), stop=(stop and i == len(steps) - 1))
 
         a_bank = {}
         c_bank = {}
@@ -220,7 +248,7 @@ def tile_drafter_feature_fusion_d2_kernel(tc, e, f_bytes, f_scale, w_bytes, w_sc
 
         def add_b(s):
             c = s // PAIRS
-            a_plus_b[s] = work.tile([P, 2, CHUNK], F32, name="a_plus_b", bufs=8)
+            a_plus_b[s] = work.tile([P, 2, CHUNK], F32, name="a_plus_b", bufs=12)
             row = bias[:, c * CHUNK:(c + 1) * CHUNK].unsqueeze(1).to_broadcast([P, 2, CHUNK])
             nc.vector.tensor_tensor(out=a_plus_b[s][:], in0=a_bank[s][1][:], in1=row, op=ADD)
             free_banks.append(a_bank[s][0])
@@ -230,6 +258,14 @@ def tile_drafter_feature_fusion_d2_kernel(tc, e, f_bytes, f_scale, w_bytes, w_sc
             c_bank[s] = take_bank([P, 2, CHUNK])
             for i in range(2):
                 passes(c_bank[s][1][:, i, :], x_mx[("f", 2 * pair + i)], 0, c, [1, 2])
+
+        def mm_c_half(s, part):
+            c, pair = divmod(s, PAIRS)
+            if part == 1:
+                c_bank[s] = take_bank([P, 2, CHUNK])
+            for i in range(2):
+                passes(c_bank[s][1][:, i, :], x_mx[("f", 2 * pair + i)], 2 * (part - 1), c, [part],
+                       start=(part == 1 and i == 0), stop=(part == 2 and i == 1))
 
         sums = {}
 
@@ -248,9 +284,11 @@ def tile_drafter_feature_fusion_d2_kernel(tc, e, f_bytes, f_scale, w_bytes, w_sc
             nc.scalar.activation(out=res[:], in_=sums[s][:], func=ACT.Silu)
             nc.sync.dma_start(out=o_v[:, 2 * pair:2 * pair + 2, c * CHUNK:(c + 1) * CHUNK], in_=res[:])
 
-        lace_w(0)
+        lace_w(0, range(2))
         scale_f(0, F_PASSES, "scalar")
-        widen_w(0, on_vector=True)
+        widen_w(0, range(2), "vector")
+        lace_w(0, range(2, 4))
+        widen_w(0, range(2, 4), "vector")
         turn_e(0)
         scale_f(1, 0, "vector")
         turn_f(0)
@@ -260,7 +298,6 @@ def tile_drafter_feature_fusion_d2_kernel(tc, e, f_bytes, f_scale, w_bytes, w_sc
         quant_e(0)
         lace_w(2)
         mm_a(0)
-        lace_w(3)
         for m in range(TILES):
             pair, odd = divmod(m, 2)
             k = PARTS + pair - 1
@@ -271,8 +308,8 @@ def tile_drafter_feature_fusion_d2_kernel(tc, e, f_bytes, f_scale, w_bytes, w_sc
             if not odd and pair > 0:
                 mm_c(pair - 1)
                 mm_a(pair)
-            if m >= PAIRS:
-                mm_a(m)
+            if m - PAIRS + A_LEAD >= PAIRS:
+                mm_a(m - PAIRS + A_LEAD)
             if not odd:
                 widen_w(k)
             quant_f(m)
@@ -290,33 +327,46 @@ def tile_drafter_feature_fusion_d2_kernel(tc, e, f_bytes, f_scale, w_bytes, w_sc
             else:
                 if pair + 1 < PAIRS:
                     turn_e(pair + 1)
-                lace_w(k + 2)
+                lace_w(k + 1)
                 if pair > 1:
                     finish(pair - 2)
-            if m > PAIRS:
-                add_b(m - 1)
+            if m - PAIRS + A_LEAD - A_LAG >= PAIRS:
+                add_b(m - PAIRS + A_LEAD - A_LAG)
         mm_c(PAIRS - 1)
         widen_w(2 * PARTS)
-        add_b(TILES - 1)
         finish(PAIRS - 2)
-        lace_w(2 * PARTS + 2)
+        lace_w(2 * PARTS + 1)
         last = CHUNKS * PAIRS
-        for s in range(PAIRS, last + C_LAG + 1):
-            c, pair = divmod(s, PAIRS)
-            k = (c + 1) * PARTS + pair
-            if s - C_LAG - 1 >= PAIRS - 1:
-                finish(s - C_LAG - 1)
-            if PAIRS - 1 <= s - C_LAG < last:
-                join(s - C_LAG)
-            if s < last:
-                mm_c(s)
-            if pair < PARTS and k + 1 < UNITS:
-                widen_w(k + 1)
-            if TILES <= s + A_LEAD - A_LAG < last:
-                add_b(s + A_LEAD - A_LAG)
-            if TILES <= s + A_LEAD < last:
-                mm_a(s + A_LEAD)
-            if pair < PARTS and k < UNITS:
+
+        def empty(i):
+            s = PAIRS + i // 2
+            if i % 2 == 0:
+                if PAIRS - 1 <= s - C_LAG - 1 < last:
+                    finish(s - C_LAG - 1)
+                if PAIRS - 1 <= s - C_LAG < last:
+                    join(s - C_LAG)
+                if s < last:
+                    mm_c(s)
+            else:
+                if PAIRS <= s + A_LEAD - A_LAG < last:
+                    add_b(s + A_LEAD - A_LAG)
+                if PAIRS <= s + A_LEAD < last:
+                    mm_a(s + A_LEAD)
+
+        for k in range(2 * PARTS, UNITS + 2 * PARTS):
+            beat = k - 2 * PARTS
+            run = range(2 * PAIRS * beat // PARTS, 2 * PAIRS * (beat + 1) // PARTS)
+            late = min(G_BLOCKS, len(run) - 1)
+            on_vector = W_ON_VECTOR * (beat % PARTS == 0)
+            if k + 1 < UNITS:
+                widen_w(k + 1, range(on_vector, 4))
+            if k < UNITS:
                 quant_w(k)
-            if pair < PARTS and k + 3 < UNITS:
-                lace_w(k + 3)
+            if k + 2 < UNITS and late:
+                lace_w_gpsimd(k + 2, late)
+            for i in run:
+                empty(i)
+            if k + 1 < UNITS:
+                widen_w(k + 1, range(on_vector), "vector")
+            if k + 2 < UNITS:
+                lace_w(k + 2, range(4 - late))

@@ -36,7 +36,7 @@ A_LEAD = 2
 A_LAG = 2
 G_BLOCKS = 2
 W_ON_VECTOR = 0
-F_PASSES_ON_SCALAR = 1
+F_PASSES_ON_SCALAR = 0
 
 
 def tile_drafter_feature_fusion_d2_kernel(tc, e, f_bytes, f_scale, w_bytes, w_scale, trust, b, out):

@@ -32,8 +32,8 @@ UNITS = CHUNKS * PARTS
 UNIT = 2 * 4 * CHUNK
 EARLY = 512
 C_LAG = 2
-A_LEAD = 2
-A_LAG = 2
+A_LEAD = 3
+A_LAG = 1
 G_BLOCKS = 2
 W_ON_VECTOR = 0
 F_PASSES_ON_SCALAR = 0
@@ -84,11 +84,10 @@ def tile_drafter_feature_fusion_d2_kernel(tc, e, f_bytes, f_scale, w_bytes, w_sc
             nc.sync.dma_start(out=raw[:], in_=f_v[:, m, :])
             f_raw[m] = raw
 
-        load_w(0, 0, [0])
         load_f(0)
-        load_w(0, 0, [1])
-        load_e(0)
+        load_w(0, 0)
         load_f(1)
+        load_e(0)
         load_w(1, 0)
         load_w(2, 0)
         bias = once.tile([P, N], BF16)
@@ -114,10 +113,12 @@ def tile_drafter_feature_fusion_d2_kernel(tc, e, f_bytes, f_scale, w_bytes, w_sc
         make_identity(nc, ident[:])
 
         w_scales = once.tile([P, PASSES, W_BLOCKS], F32)
-        number, bank = take_bank([P, PASSES * W_BLOCKS])
-        nc.tensor.matmul(bank[:], lhsT=quadrants[:], rhs=w_scale_rows[:].rearrange("p g j -> p (g j)"), start=True, stop=True)
-        nc.scalar.copy(out=w_scales[:].rearrange("p g j -> p (g j)"), in_=bank[:])
-        free_banks.append(number)
+
+        def spread_w_scale():
+            number, bank = take_bank([P, PASSES * W_BLOCKS])
+            nc.tensor.matmul(bank[:], lhsT=quadrants[:], rhs=w_scale_rows[:].rearrange("p g j -> p (g j)"), start=True, stop=True)
+            nc.scalar.copy(out=w_scales[:].rearrange("p g j -> p (g j)"), in_=bank[:])
+            free_banks.append(number)
 
         laced = {}
         wide = {}
@@ -281,17 +282,21 @@ def tile_drafter_feature_fusion_d2_kernel(tc, e, f_bytes, f_scale, w_bytes, w_sc
         def finish(s):
             c, pair = divmod(s, PAIRS)
             res = work.tile([P, 2, CHUNK], F32, name="res", bufs=5)
-            nc.scalar.activation(out=res[:], in_=sums[s][:], func=ACT.Silu)
-            nc.sync.dma_start(out=o_v[:, 2 * pair:2 * pair + 2, c * CHUNK:(c + 1) * CHUNK], in_=res[:])
+            pieces = [slice(0, 1), slice(1, 2)] if s == CHUNKS * PAIRS - 1 else [slice(0, 2)]
+            for tiles in pieces:
+                nc.scalar.activation(out=res[:, tiles], in_=sums[s][:, tiles], func=ACT.Silu)
+                nc.sync.dma_start(out=o_v[:, 2 * pair + tiles.start:2 * pair + tiles.stop, c * CHUNK:(c + 1) * CHUNK], in_=res[:, tiles])
 
+        scale_f(0, 2, "scalar")
+        scale_f(0, 2, "vector")
+        spread_w_scale()
         lace_w(0, range(2))
-        scale_f(0, F_PASSES, "scalar")
-        widen_w(0, range(2), "vector")
+        widen_w(0, range(2))
         lace_w(0, range(2, 4))
-        widen_w(0, range(2, 4), "vector")
-        turn_e(0)
         scale_f(1, 0, "vector")
+        widen_w(0, range(2, 4))
         turn_f(0)
+        turn_e(0)
         quant_w(0)
         lace_w(1)
         widen_w(1)
@@ -319,23 +324,26 @@ def tile_drafter_feature_fusion_d2_kernel(tc, e, f_bytes, f_scale, w_bytes, w_sc
                 quant_w(1)
             if odd:
                 quant_w(k)
+                if pair > 0:
+                    lace_w_gpsimd(k + 2, min(pair, G_BLOCKS))
                 add_b(pair)
                 if pair > 0:
                     join(pair - 1)
+                for j in range(m - 1, m + 1):
+                    if j - PAIRS + A_LEAD - A_LAG >= PAIRS:
+                        add_b(j - PAIRS + A_LEAD - A_LAG)
                 if pair + 1 < PAIRS:
                     quant_e(pair + 1)
             else:
                 if pair + 1 < PAIRS:
                     turn_e(pair + 1)
-                lace_w(k + 1)
+                lace_w(k + 1, range(4 - min(max(pair - 1, 0), G_BLOCKS)))
                 if pair > 1:
                     finish(pair - 2)
-            if m - PAIRS + A_LEAD - A_LAG >= PAIRS:
-                add_b(m - PAIRS + A_LEAD - A_LAG)
         mm_c(PAIRS - 1)
         widen_w(2 * PARTS)
         finish(PAIRS - 2)
-        lace_w(2 * PARTS + 1)
+        lace_w(2 * PARTS + 1, range(4 - G_BLOCKS))
         last = CHUNKS * PAIRS
 
         def empty(i):
@@ -353,20 +361,26 @@ def tile_drafter_feature_fusion_d2_kernel(tc, e, f_bytes, f_scale, w_bytes, w_sc
                 if PAIRS <= s + A_LEAD < last:
                     mm_a(s + A_LEAD)
 
+        def run(beat):
+            return range(2 * PAIRS * beat // PARTS, 2 * PAIRS * (beat + 1) // PARTS)
+
+        def late(beat):
+            reads = [i for i in run(beat) if i % 2 or PAIRS + i // 2 - C_LAG >= PAIRS - 1]
+            return min(G_BLOCKS, len(reads) - 1)
+
+        lace_w(2 * PARTS + 2, range(4 - late(0)))
         for k in range(2 * PARTS, UNITS + 2 * PARTS):
             beat = k - 2 * PARTS
-            run = range(2 * PAIRS * beat // PARTS, 2 * PAIRS * (beat + 1) // PARTS)
-            late = min(G_BLOCKS, len(run) - 1)
             on_vector = W_ON_VECTOR * (beat % PARTS == 0)
             if k + 1 < UNITS:
                 widen_w(k + 1, range(on_vector, 4))
             if k < UNITS:
                 quant_w(k)
-            if k + 2 < UNITS and late:
-                lace_w_gpsimd(k + 2, late)
-            for i in run:
+            if k + 2 < UNITS and late(beat):
+                lace_w_gpsimd(k + 2, late(beat))
+            for i in run(beat):
                 empty(i)
             if k + 1 < UNITS:
                 widen_w(k + 1, range(on_vector), "vector")
-            if k + 2 < UNITS:
-                lace_w(k + 2, range(4 - late))
+            if k + 3 < UNITS:
+                lace_w(k + 3, range(4 - late(beat + 1)))

@@ -35,8 +35,10 @@ C_LAG = 2
 A_LEAD = 3
 A_LAG = 1
 G_BLOCKS = 2
-W_ON_VECTOR = 0
-F_PASSES_ON_SCALAR = 0
+W_ON_VECTOR = 1
+F_FROM = 6
+GROUPS = [slice(0, CHUNK), slice(CHUNK, 2 * CHUNK), slice(2 * CHUNK, N)]
+F_PASSES_ON_SCALAR = 1
 
 
 def tile_drafter_feature_fusion_d2_kernel(tc, e, f_bytes, f_scale, w_bytes, w_scale, trust, b, out):
@@ -46,7 +48,9 @@ def tile_drafter_feature_fusion_d2_kernel(tc, e, f_bytes, f_scale, w_bytes, w_sc
         work = ctx.enter_context(tc.tile_pool(name="work", bufs=3))
         psum = ctx.enter_context(tc.psum_pool(name="psum", bufs=1))
         w_scale_rows = once.tile([P, PASSES, W_BLOCKS], F32)
-        nc.gpsimd.memset(w_scale_rows[:], 0.0)
+        nc.vector.memset(w_scale_rows[:], 0.0)
+        zero = once.tile([P, 1], F32)
+        nc.vector.memset(zero[:], 0.0)
         quadrants = once.tile([P, P], F32)
         make_block_diagonal(nc, quadrants[:], 32)
         ctx.enter_context(tc.manual_schedule())
@@ -61,18 +65,18 @@ def tile_drafter_feature_fusion_d2_kernel(tc, e, f_bytes, f_scale, w_bytes, w_sc
         nc.scalar.dma_start(out=w_scale_rows[0:P:32], in_=w_scale.rearrange("(g q) j -> q g j", q=4))
 
         warm = once.tile([P, 1], F32)
-        nc.scalar.activation(out=warm[:], in_=quadrants[:, 0:1], func=ACT.Silu)
+        nc.scalar.activation(out=warm[:], in_=zero[:], func=ACT.Silu)
 
         w_raw = {}
         e_raw = {}
         f_raw = {}
 
-        def load_w(part, late, halves=(0, 1)):
-            cols = slice(EARLY, N) if late else slice(0, EARLY)
-            if (part, late) not in w_raw:
-                w_raw[(part, late)] = once.tile([P, 2, 4, cols.stop - cols.start], U8, name="w_raw%d_%d" % (part, late))
-            for h in halves:
-                nc.sync.dma_start(out=w_raw[(part, late)][:, h], in_=w_v[:, 2 * part + h, :, cols])
+        def load_w(part, group):
+            cols = GROUPS[group]
+            raw = once.tile([P, 2, 4, cols.stop - cols.start], U8, name="w_raw%d_%d" % (part, group))
+            for h in range(2):
+                nc.sync.dma_start(out=raw[:, h], in_=w_v[:, 2 * part + h, :, cols])
+            w_raw[(part, group)] = raw
 
         def load_e(pair):
             raw = once.tile([P, 2 * E], BF16, name="e_raw%d" % pair)
@@ -81,7 +85,8 @@ def tile_drafter_feature_fusion_d2_kernel(tc, e, f_bytes, f_scale, w_bytes, w_sc
 
         def load_f(m):
             raw = once.tile([P, D], U8, name="f_raw%d" % m)
-            nc.sync.dma_start(out=raw[:], in_=f_v[:, m, :])
+            for cols in ([slice(D // 2, D), slice(0, D // 2)] if m == 0 else [slice(0, D)]):
+                nc.sync.dma_start(out=raw[:, cols], in_=f_v[:, m, cols])
             f_raw[m] = raw
 
         load_f(0)
@@ -94,13 +99,14 @@ def tile_drafter_feature_fusion_d2_kernel(tc, e, f_bytes, f_scale, w_bytes, w_sc
         trusts = once.tile([P, TILES], BF16)
         for pair in range(1, PAIRS):
             load_f(2 * pair)
+            load_w(pair - 1, 1)
             load_e(pair)
             load_f(2 * pair + 1)
             if pair == 1:
                 nc.sync.dma_start(out=bias[:, 0:EARLY], in_=b[0:EARLY].partition_broadcast(P))
                 nc.sync.dma_start(out=trusts[:], in_=trust.rearrange("(p m) o -> p (m o)", m=TILES))
         for part in range(PARTS):
-            load_w(part, 1)
+            load_w(part, 2)
         nc.sync.dma_start(out=bias[:, EARLY:N], in_=b[EARLY:N].partition_broadcast(P))
 
         free_banks = list(range(8))
@@ -128,9 +134,9 @@ def tile_drafter_feature_fusion_d2_kernel(tc, e, f_bytes, f_scale, w_bytes, w_sc
 
         def raw_columns(k):
             c, part = divmod(k, PARTS)
-            late = int(c * CHUNK >= EARLY)
-            n0 = c * CHUNK - late * EARLY
-            return w_raw[(part, late)][:, :, :, n0:n0 + CHUNK]
+            group = min(c, 2)
+            n0 = c * CHUNK - GROUPS[group].start
+            return w_raw[(part, group)][:, :, :, n0:n0 + CHUNK]
 
         def lace_w(k, blocks=range(4)):
             tile = work.tile([P, len(blocks) * 4 * B], U8, name="w_laced", bufs=4)
@@ -294,20 +300,23 @@ def tile_drafter_feature_fusion_d2_kernel(tc, e, f_bytes, f_scale, w_bytes, w_sc
         widen_w(0, range(2))
         lace_w(0, range(2, 4))
         scale_f(1, 0, "vector")
-        widen_w(0, range(2, 4))
         turn_f(0)
         turn_e(0)
-        quant_w(0)
+        widen_w(0, range(2, 4), "vector")
         lace_w(1)
+        quant_w(0)
         widen_w(1)
         quant_e(0)
         lace_w(2)
         mm_a(0)
+        def early_share(pair):
+            return 0 if pair < 1 else G_BLOCKS if pair == PAIRS - 1 else 1
+
         for m in range(TILES):
             pair, odd = divmod(m, 2)
             k = PARTS + pair - 1
             if m + 2 < TILES:
-                scale_f(m + 2, F_PASSES_ON_SCALAR, "scalar")
+                scale_f(m + 2, F_PASSES_ON_SCALAR * (m + 2 >= F_FROM), "scalar")
             if m + 1 < TILES:
                 turn_f(m + 1)
             if not odd and pair > 0:
@@ -319,13 +328,13 @@ def tile_drafter_feature_fusion_d2_kernel(tc, e, f_bytes, f_scale, w_bytes, w_sc
                 widen_w(k)
             quant_f(m)
             if m + 2 < TILES:
-                scale_f(m + 2, F_PASSES_ON_SCALAR, "vector")
+                scale_f(m + 2, F_PASSES_ON_SCALAR * (m + 2 >= F_FROM), "vector")
             if m == 0:
                 quant_w(1)
             if odd:
                 quant_w(k)
                 if pair > 0:
-                    lace_w_gpsimd(k + 2, min(pair, G_BLOCKS))
+                    lace_w_gpsimd(k + 2, early_share(pair))
                 add_b(pair)
                 if pair > 0:
                     join(pair - 1)
@@ -337,7 +346,7 @@ def tile_drafter_feature_fusion_d2_kernel(tc, e, f_bytes, f_scale, w_bytes, w_sc
             else:
                 if pair + 1 < PAIRS:
                     turn_e(pair + 1)
-                lace_w(k + 1, range(4 - min(max(pair - 1, 0), G_BLOCKS)))
+                lace_w(k + 1, range(4 - early_share(pair - 1)))
                 if pair > 1:
                     finish(pair - 2)
         mm_c(PAIRS - 1)
@@ -371,16 +380,16 @@ def tile_drafter_feature_fusion_d2_kernel(tc, e, f_bytes, f_scale, w_bytes, w_sc
         lace_w(2 * PARTS + 2, range(4 - late(0)))
         for k in range(2 * PARTS, UNITS + 2 * PARTS):
             beat = k - 2 * PARTS
-            on_vector = W_ON_VECTOR * (beat % PARTS == 0)
+            on_vector = W_ON_VECTOR * (k + 2 == UNITS)
             if k + 1 < UNITS:
                 widen_w(k + 1, range(on_vector, 4))
             if k < UNITS:
                 quant_w(k)
             if k + 2 < UNITS and late(beat):
                 lace_w_gpsimd(k + 2, late(beat))
+            if on_vector:
+                widen_w(k + 1, range(on_vector), "vector")
             for i in run(beat):
                 empty(i)
-            if k + 1 < UNITS:
-                widen_w(k + 1, range(on_vector), "vector")
             if k + 3 < UNITS:
                 lace_w(k + 3, range(4 - late(beat + 1)))

@@ -36,7 +36,7 @@ A_LEAD = 3
 A_LAG = 1
 G_BLOCKS = 2
 W_ON_VECTOR = 1
-F_FROM = 6
+F_FROM = 8
 GROUPS = [slice(0, CHUNK), slice(CHUNK, 2 * CHUNK), slice(2 * CHUNK, N)]
 F_PASSES_ON_SCALAR = 1
 
@@ -377,19 +377,18 @@ def tile_drafter_feature_fusion_d2_kernel(tc, e, f_bytes, f_scale, w_bytes, w_sc
             reads = [i for i in run(beat) if i % 2 or PAIRS + i // 2 - C_LAG >= PAIRS - 1]
             return min(G_BLOCKS, len(reads) - 1)
 
-        lace_w(2 * PARTS + 2, range(4 - late(0)))
         for k in range(2 * PARTS, UNITS + 2 * PARTS):
             beat = k - 2 * PARTS
-            on_vector = W_ON_VECTOR * (k + 2 == UNITS)
+            on_vector = int(beat % PARTS < W_ON_VECTOR)
             if k + 1 < UNITS:
                 widen_w(k + 1, range(on_vector, 4))
             if k < UNITS:
                 quant_w(k)
+            if k + 2 < UNITS:
+                lace_w(k + 2, range(4 - late(beat)))
             if k + 2 < UNITS and late(beat):
                 lace_w_gpsimd(k + 2, late(beat))
-            if on_vector:
+            if on_vector and k + 1 < UNITS:
                 widen_w(k + 1, range(on_vector), "vector")
             for i in run(beat):
                 empty(i)
-            if k + 3 < UNITS:
-                lace_w(k + 3, range(4 - late(beat + 1)))

@@ -31,7 +31,7 @@ PARTS = PASSES // 2
 UNITS = CHUNKS * PARTS
 UNIT = 2 * 4 * CHUNK
 EARLY = 512
-C_LAG = 2
+C_LAG = 1
 A_LEAD = 3
 A_LAG = 1
 G_BLOCKS = 2
@@ -178,8 +178,8 @@ def tile_drafter_feature_fusion_d2_kernel(tc, e, f_bytes, f_scale, w_bytes, w_sc
                 free_slots.append(lent[k])
 
         def quantise(src, name, bufs):
-            codes = work.tile([P, 512], U32, align_bytes=64, name=name + "_codes", bufs=bufs)
-            scales = work.tile([P, 512], U8, align_bytes=64, name=name + "_scales", bufs=bufs)
+            codes = work.tile([P, 512], U32, align_bytes=256, name=name + "_codes", bufs=bufs)
+            scales = work.tile([P, 512], U8, align_bytes=256, name=name + "_scales", bufs=bufs)
             nc.vector.quantize_mx(out=codes[:].bitcast(FP8X4), scales=scales[:], in_=src[:])
             return codes, scales
 
@@ -310,7 +310,7 @@ def tile_drafter_feature_fusion_d2_kernel(tc, e, f_bytes, f_scale, w_bytes, w_sc
         lace_w(2)
         mm_a(0)
         def early_share(pair):
-            return 0 if pair < 1 else G_BLOCKS if pair == PAIRS - 1 else 1
+            return max(0, min(pair, G_BLOCKS))
 
         for m in range(TILES):
             pair, odd = divmod(m, 2)
@@ -322,8 +322,10 @@ def tile_drafter_feature_fusion_d2_kernel(tc, e, f_bytes, f_scale, w_bytes, w_sc
             if not odd and pair > 0:
                 mm_c(pair - 1)
                 mm_a(pair)
-            if m - PAIRS + A_LEAD >= PAIRS:
-                mm_a(m - PAIRS + A_LEAD)
+            if m == PAIRS:
+                mm_a(PAIRS)
+            if PAIRS <= m < TILES - 1:
+                mm_a(m + 1)
             if not odd:
                 widen_w(k)
             quant_f(m)
@@ -338,9 +340,9 @@ def tile_drafter_feature_fusion_d2_kernel(tc, e, f_bytes, f_scale, w_bytes, w_sc
                 add_b(pair)
                 if pair > 0:
                     join(pair - 1)
-                for j in range(m - 1, m + 1):
-                    if j - PAIRS + A_LEAD - A_LAG >= PAIRS:
-                        add_b(j - PAIRS + A_LEAD - A_LAG)
+                if m > PAIRS:
+                    add_b(m - 1)
+                    add_b(m)
                 if pair + 1 < PAIRS:
                     quant_e(pair + 1)
             else:
@@ -365,17 +367,17 @@ def tile_drafter_feature_fusion_d2_kernel(tc, e, f_bytes, f_scale, w_bytes, w_sc
                 if s < last:
                     mm_c(s)
             else:
-                if PAIRS <= s + A_LEAD - A_LAG < last:
+                if TILES <= s + A_LEAD - A_LAG < last:
                     add_b(s + A_LEAD - A_LAG)
-                if PAIRS <= s + A_LEAD < last:
+                if TILES <= s + A_LEAD < last:
                     mm_a(s + A_LEAD)
 
         def run(beat):
             return range(2 * PAIRS * beat // PARTS, 2 * PAIRS * (beat + 1) // PARTS)
 
         def late(beat):
-            reads = [i for i in run(beat) if i % 2 or PAIRS + i // 2 - C_LAG >= PAIRS - 1]
-            return min(G_BLOCKS, len(reads) - 1)
+            reads = [i for i in run(beat) if PAIRS + i // 2 >= (TILES - A_LEAD + A_LAG if i % 2 else PAIRS - 1 + C_LAG)]
+            return max(0, min(G_BLOCKS, len(reads) - 1))
 
         for k in range(2 * PARTS, UNITS + 2 * PARTS):
             beat = k - 2 * PARTS

@@ -92,16 +92,18 @@ def tile_drafter_feature_fusion_d2_kernel(tc, e, f_bytes, f_scale, w_bytes, w_sc
         load_f(0)
         load_w(0, 0)
         load_f(1)
-        load_e(0)
         load_w(1, 0)
+        load_f(2)
         load_w(2, 0)
+        load_e(0)
         bias = once.tile([P, N], BF16)
         trusts = once.tile([P, TILES], BF16)
         for pair in range(1, PAIRS):
-            load_f(2 * pair)
+            if pair > 1:
+                load_f(2 * pair)
             load_w(pair - 1, 1)
-            load_e(pair)
             load_f(2 * pair + 1)
+            load_e(pair)
             if pair == 1:
                 nc.sync.dma_start(out=bias[:, 0:EARLY], in_=b[0:EARLY].partition_broadcast(P))
                 nc.sync.dma_start(out=trusts[:], in_=trust.rearrange("(p m) o -> p (m o)", m=TILES))
@@ -262,9 +264,10 @@ def tile_drafter_feature_fusion_d2_kernel(tc, e, f_bytes, f_scale, w_bytes, w_sc
 
         def mm_c(s):
             c, pair = divmod(s, PAIRS)
-            c_bank[s] = take_bank([P, 2, CHUNK])
+            first = take_bank([P, 2, CHUNK])
+            c_bank[s] = [first, take_bank([P, 2, CHUNK]) if s == CHUNKS * PAIRS - 1 else first]
             for i in range(2):
-                passes(c_bank[s][1][:, i, :], x_mx[("f", 2 * pair + i)], 0, c, [1, 2])
+                passes(c_bank[s][i][1][:, i, :], x_mx[("f", 2 * pair + i)], 0, c, [1, 2])
 
         def mm_c_half(s, part):
             c, pair = divmod(s, PAIRS)
@@ -281,9 +284,9 @@ def tile_drafter_feature_fusion_d2_kernel(tc, e, f_bytes, f_scale, w_bytes, w_sc
             z = sums[s] = work.tile([P, 2, CHUNK], F32, name="z", bufs=4)
             for i in range(2):
                 m = 2 * pair + i
-                nc.vector.scalar_tensor_tensor(out=z[:, i, :], in0=c_bank[s][1][:, i, :], scalar=trusts[:, m:m + 1],
+                nc.vector.scalar_tensor_tensor(out=z[:, i, :], in0=c_bank[s][i][1][:, i, :], scalar=trusts[:, m:m + 1],
                                                in1=a_plus_b[s][:, i, :], op0=MULT, op1=ADD)
-            free_banks.append(c_bank[s][0])
+            free_banks.append(c_bank[s][0][0])
 
         def finish(s):
             c, pair = divmod(s, PAIRS)
@@ -301,14 +304,12 @@ def tile_drafter_feature_fusion_d2_kernel(tc, e, f_bytes, f_scale, w_bytes, w_sc
         lace_w(0, range(2, 4))
         scale_f(1, 0, "vector")
         turn_f(0)
-        turn_e(0)
         widen_w(0, range(2, 4), "vector")
         lace_w(1)
-        quant_w(0)
+        turn_f(1)
         widen_w(1)
-        quant_e(0)
-        lace_w(2)
-        mm_a(0)
+        quant_w(0)
+
         def early_share(pair):
             return max(0, min(pair, G_BLOCKS))
 
@@ -317,8 +318,10 @@ def tile_drafter_feature_fusion_d2_kernel(tc, e, f_bytes, f_scale, w_bytes, w_sc
             k = PARTS + pair - 1
             if m + 2 < TILES:
                 scale_f(m + 2, F_PASSES_ON_SCALAR * (m + 2 >= F_FROM), "scalar")
-            if m + 1 < TILES:
+            if 0 < m < TILES - 1:
                 turn_f(m + 1)
+            if m == 1:
+                turn_e(1)
             if not odd and pair > 0:
                 mm_c(pair - 1)
                 mm_a(pair)
@@ -326,19 +329,27 @@ def tile_drafter_feature_fusion_d2_kernel(tc, e, f_bytes, f_scale, w_bytes, w_sc
                 mm_a(PAIRS)
             if PAIRS <= m < TILES - 1:
                 mm_a(m + 1)
-            if not odd:
+            if m > 0 and not odd:
                 widen_w(k)
             quant_f(m)
             if m + 2 < TILES:
                 scale_f(m + 2, F_PASSES_ON_SCALAR * (m + 2 >= F_FROM), "vector")
             if m == 0:
+                lace_w(2)
+                turn_e(0)
+                widen_w(2)
                 quant_w(1)
+            if m == 1:
+                quant_e(0)
+                mm_a(0)
             if odd:
                 quant_w(k)
                 if pair > 0:
                     lace_w_gpsimd(k + 2, early_share(pair))
-                add_b(pair)
+                if pair == 1:
+                    add_b(0)
                 if pair > 0:
+                    add_b(pair)
                     join(pair - 1)
                 if m > PAIRS:
                     add_b(m - 1)
@@ -346,7 +357,7 @@ def tile_drafter_feature_fusion_d2_kernel(tc, e, f_bytes, f_scale, w_bytes, w_sc
                 if pair + 1 < PAIRS:
                     quant_e(pair + 1)
             else:
-                if pair + 1 < PAIRS:
+                if 0 < pair < PAIRS - 1:
                     turn_e(pair + 1)
                 lace_w(k + 1, range(4 - early_share(pair - 1)))
                 if pair > 1:

@@ -101,12 +101,15 @@ def tile_drafter_feature_fusion_d2_kernel(tc, e, f_bytes, f_scale, w_bytes, w_sc
         for pair in range(1, PAIRS):
             if pair > 1:
                 load_f(2 * pair)
-            load_w(pair - 1, 1)
+            if pair == 2:
+                nc.sync.dma_start(out=bias[:, 0:EARLY], in_=b[0:EARLY].partition_broadcast(P))
+                nc.sync.dma_start(out=trusts[:], in_=trust.rearrange("(p m) o -> p (m o)", m=TILES))
+            if pair > 1:
+                load_w(pair - 1, 1)
             load_f(2 * pair + 1)
             load_e(pair)
             if pair == 1:
-                nc.sync.dma_start(out=bias[:, 0:EARLY], in_=b[0:EARLY].partition_broadcast(P))
-                nc.sync.dma_start(out=trusts[:], in_=trust.rearrange("(p m) o -> p (m o)", m=TILES))
+                load_w(0, 1)
         for part in range(PARTS):
             load_w(part, 2)
         nc.sync.dma_start(out=bias[:, EARLY:N], in_=b[EARLY:N].partition_broadcast(P))
@@ -354,12 +357,15 @@ def tile_drafter_feature_fusion_d2_kernel(tc, e, f_bytes, f_scale, w_bytes, w_sc
                 if m > PAIRS:
                     add_b(m - 1)
                     add_b(m)
+                if pair == 0:
+                    lace_w(k + 1)
                 if pair + 1 < PAIRS:
                     quant_e(pair + 1)
             else:
                 if 0 < pair < PAIRS - 1:
                     turn_e(pair + 1)
-                lace_w(k + 1, range(4 - early_share(pair - 1)))
+                if pair > 0:
+                    lace_w(k + 1, range(4 - early_share(pair - 1)))
                 if pair > 1:
                     finish(pair - 2)
         mm_c(PAIRS - 1)

@@ -22,23 +22,33 @@ K_PASS = 512
 TILES = T // P
 PAIRS = TILES // 2
 PASSES = (E + D) // K_PASS
-F_PASSES = D // K_PASS
+E_PASSES = E // K_PASS
 F_BLOCKS = D // B
 W_BLOCKS = N // B
-CHUNK = 256
-CHUNKS = N // CHUNK
-PARTS = PASSES // 2
-UNITS = CHUNKS * PARTS
-UNIT = 2 * 4 * CHUNK
-EARLY = 512
-C_LAG = 1
-A_LEAD = 3
-A_LAG = 1
-G_BLOCKS = 2
-W_ON_VECTOR = 1
-F_FROM = 8
-GROUPS = [slice(0, CHUNK), slice(CHUNK, 2 * CHUNK), slice(2 * CHUNK, N)]
-F_PASSES_ON_SCALAR = 1
+HALF = 256
+WIDE = 512
+G_BLOCKS = 3
+F0_ON_SCALAR = 2
+SLOTS = 6
+LAST_HALF = N // HALF - 1
+F_LATE = 8
+BACKLOG = 4
+
+
+def a_unit(h):
+    return ("a", h * HALF, HALF, [0, 1])
+
+
+def c_wide(c):
+    return [("c", c * WIDE, WIDE, [g]) for g in range(E_PASSES, PASSES)]
+
+
+def c_half(h):
+    return [("c", h * HALF, HALF, [g, g + 1]) for g in range(E_PASSES, PASSES, 2)]
+
+
+UNITS = ([a_unit(0), a_unit(1)] + c_wide(0) + [a_unit(2), a_unit(3)] + c_half(2) + c_half(3)
+         + [a_unit(4)] + c_half(4) + c_half(5) + [a_unit(5)])
 
 
 def tile_drafter_feature_fusion_d2_kernel(tc, e, f_bytes, f_scale, w_bytes, w_scale, trust, b, out):
@@ -71,12 +81,12 @@ def tile_drafter_feature_fusion_d2_kernel(tc, e, f_bytes, f_scale, w_bytes, w_sc
         e_raw = {}
         f_raw = {}
 
-        def load_w(part, group):
-            cols = GROUPS[group]
-            raw = once.tile([P, 2, 4, cols.stop - cols.start], U8, name="w_raw%d_%d" % (part, group))
-            for h in range(2):
-                nc.sync.dma_start(out=raw[:, h], in_=w_v[:, 2 * part + h, :, cols])
-            w_raw[(part, group)] = raw
+        def load_w(k):
+            kind, n0, width, gs = UNITS[k]
+            raw = once.tile([P, 4, WIDE], U8, name="w_raw%d" % k)
+            for h, g in enumerate(gs):
+                nc.sync.dma_start(out=raw[:, :, h * width:(h + 1) * width], in_=w_v[:, g, :, n0:n0 + width])
+            w_raw[k] = raw
 
         def load_e(pair):
             raw = once.tile([P, 2 * E], BF16, name="e_raw%d" % pair)
@@ -89,30 +99,27 @@ def tile_drafter_feature_fusion_d2_kernel(tc, e, f_bytes, f_scale, w_bytes, w_sc
                 nc.sync.dma_start(out=raw[:, cols], in_=f_v[:, m, cols])
             f_raw[m] = raw
 
-        load_f(0)
-        load_w(0, 0)
-        load_f(1)
-        load_w(1, 0)
-        load_f(2)
-        load_w(2, 0)
-        load_e(0)
         bias = once.tile([P, N], BF16)
         trusts = once.tile([P, TILES], BF16)
-        for pair in range(1, PAIRS):
-            if pair > 1:
-                load_f(2 * pair)
-            if pair == 2:
-                nc.sync.dma_start(out=bias[:, 0:EARLY], in_=b[0:EARLY].partition_broadcast(P))
-                nc.sync.dma_start(out=trusts[:], in_=trust.rearrange("(p m) o -> p (m o)", m=TILES))
-            if pair > 1:
-                load_w(pair - 1, 1)
-            load_f(2 * pair + 1)
-            load_e(pair)
-            if pair == 1:
-                load_w(0, 1)
-        for part in range(PARTS):
-            load_w(part, 2)
-        nc.sync.dma_start(out=bias[:, EARLY:N], in_=b[EARLY:N].partition_broadcast(P))
+        load_f(0)
+        load_w(0)
+        load_w(1)
+        load_f(1)
+        load_e(0)
+        load_w(2)
+        load_f(2)
+        load_e(1)
+        for m in range(3, TILES):
+            load_w(m)
+            load_f(m)
+            if m - 1 < PAIRS:
+                load_e(m - 1)
+            if m == PAIRS:
+                nc.sync.dma_start(out=bias[:, 0:WIDE], in_=b[0:WIDE].partition_broadcast(P))
+        nc.sync.dma_start(out=trusts[:], in_=trust.rearrange("(p m) o -> p (m o)", m=TILES))
+        nc.sync.dma_start(out=bias[:, WIDE:N], in_=b[WIDE:N].partition_broadcast(P))
+        for k in range(TILES, len(UNITS)):
+            load_w(k)
 
         free_banks = list(range(8))
 
@@ -135,44 +142,35 @@ def tile_drafter_feature_fusion_d2_kernel(tc, e, f_bytes, f_scale, w_bytes, w_sc
         wide = {}
         w_mx = {}
         lent = {}
-        free_slots = list(range(5))
+        free_slots = list(range(SLOTS))
 
-        def raw_columns(k):
-            c, part = divmod(k, PARTS)
-            group = min(c, 2)
-            n0 = c * CHUNK - GROUPS[group].start
-            return w_raw[(part, group)][:, :, :, n0:n0 + CHUNK]
+        def block_of(k, block):
+            kind, n0, width, gs = UNITS[k]
+            return divmod(block, width // B)
 
-        def lace_w(k, blocks=range(4)):
+        def lace_w(k, blocks):
             tile = work.tile([P, len(blocks) * 4 * B], U8, name="w_laced", bufs=4)
-            whole = len(blocks) // 2 if blocks[0] % 2 == 0 else 0
-            if whole:
-                src = raw_columns(k)[:, blocks[0] // 2:blocks[0] // 2 + whole].rearrange("p h t (c i) -> p h c t i", i=4)
-                nc.vector.tensor_copy(out=tile[:, 0:whole * 4 * CHUNK].rearrange("p (h c i t) -> p h c t i", h=whole, i=4, t=4), in_=src)
-            for n in range(2 * whole, len(blocks)):
-                h, j = divmod(blocks[n], 2)
-                src = raw_columns(k)[:, h, :, j * B:(j + 1) * B].rearrange("p t (c i) -> p c t i", i=4)
-                nc.vector.tensor_copy(out=tile[:, n * 4 * B:(n + 1) * 4 * B].rearrange("p (c i t) -> p c t i", i=4, t=4), in_=src)
+            src = w_raw[k][:, :, blocks.start * B:blocks.stop * B].rearrange("p t (c i) -> p c t i", i=4)
+            nc.vector.tensor_copy(out=tile[:].rearrange("p (c i t) -> p c t i", i=4, t=4), in_=src)
             for n, block in enumerate(blocks):
                 laced[(k, block)] = tile[:, n * 4 * B:(n + 1) * 4 * B]
 
-        def lace_w_gpsimd(k, count):
+        def lace_w_gpsimd(k, blocks):
             slot = lent[k] = free_slots.pop()
-            tile = work.tile([P, count * 4 * B], U8, align_bytes=64, name="w_laced_late", tag="slot%d" % slot, bufs=1)
-            src = raw_columns(k)[:, 1, :, CHUNK - count * B:CHUNK]
+            tile = work.tile([P, len(blocks) * 4 * B], U8, align_bytes=64, name="w_laced_late", tag="slot%d" % slot, bufs=1)
+            src = w_raw[k][:, :, blocks.start * B:blocks.stop * B]
             nc.gpsimd.tensor_copy(out=tile[:].rearrange("p (c t) -> p c t", t=4), in_=src.rearrange("p t c -> p c t"))
-            for n in range(count):
-                laced[(k, 4 - count + n)] = tile[:, n * 4 * B:(n + 1) * 4 * B]
+            for n, block in enumerate(blocks):
+                laced[(k, block)] = tile[:, n * 4 * B:(n + 1) * 4 * B]
 
-        def widen_w(k, blocks=range(4), part="scalar"):
-            c, w_part = divmod(k, PARTS)
+        def widen_w(k, blocks, part="scalar"):
+            kind, n0, width, gs = UNITS[k]
             if k not in wide:
                 slot = free_slots.pop(0)
-                wide[k] = (work.tile([P, UNIT], BF16, align_bytes=64, name="w_wide", tag="slot%d" % slot, bufs=1), slot)
+                wide[k] = (work.tile([P, 2048], BF16, align_bytes=64, name="w_wide", tag="slot%d" % slot, bufs=1), slot)
             for block in blocks:
-                h, j = divmod(block, 2)
-                col_block = c * CHUNK // B + j
-                scale = w_scales[:, 2 * w_part + h, col_block:col_block + 1]
+                h, j = block_of(k, block)
+                scale = w_scales[:, gs[h], n0 // B + j:n0 // B + j + 1]
                 src = laced[(k, block)].bitcast(FP8)
                 dst = wide[k][0][:, 4 * B * block:4 * B * (block + 1)]
                 if part == "vector":
@@ -189,18 +187,19 @@ def tile_drafter_feature_fusion_d2_kernel(tc, e, f_bytes, f_scale, w_bytes, w_sc
             return codes, scales
 
         def quant_w(k):
-            w_mx[k] = quantise(wide[k][0], "w", 9)
+            kind, n0, width, gs = UNITS[k]
+            codes, scales = quantise(wide[k][0], "w", 9)
+            for h, g in enumerate(gs):
+                w_mx[(g, n0)] = (codes[:, h * width:(h + 1) * width], scales[:, h * width:(h + 1) * width])
             free_slots.append(wide[k][1])
 
         f_wide = {}
-        natural = {}
         turned = {}
         x_mx = {}
 
         def scale_f(m, on_scalar, part):
             if m not in f_wide:
                 f_wide[m] = work.tile([P, D], BF16, name="f_wide")
-            natural[m] = on_scalar
             for j in (range(4 * on_scalar) if part == "scalar" else range(4 * on_scalar, F_BLOCKS)):
                 g, q = divmod(j, 4)
                 src = f_raw[m][:, j * B:(j + 1) * B].bitcast(FP8)
@@ -230,7 +229,7 @@ def tile_drafter_feature_fusion_d2_kernel(tc, e, f_bytes, f_scale, w_bytes, w_sc
             turn(e_raw[pair], ("e", pair), 4)
 
         def turn_f(m):
-            turn(f_wide[m], ("f", m), natural[m])
+            turn(f_wide[m], ("f", m), f_share(m))
 
         def quant_e(pair):
             x_mx[("e", pair)] = quantise(turned[("e", pair)], "e", PAIRS)
@@ -238,176 +237,135 @@ def tile_drafter_feature_fusion_d2_kernel(tc, e, f_bytes, f_scale, w_bytes, w_sc
         def quant_f(m):
             x_mx[("f", m)] = quantise(turned[("f", m)], "f", TILES)
 
-        def passes(acc, x, x_first, c, parts, start=True, stop=True):
-            steps = [(part, h) for part in parts for h in range(2)]
-            for i, (part, h) in enumerate(steps):
-                x_cols = slice((x_first + i) * P, (x_first + i + 1) * P)
-                w_cols = slice(h * CHUNK, (h + 1) * CHUNK)
-                w = w_mx[c * PARTS + part]
-                nc.tensor.matmul_mx(out=acc, lhsT=x[0][:, x_cols].bitcast(FP8X4), lhsT_scale=x[1][:, x_cols],
-                                    rhs=w[0][:, w_cols].bitcast(FP8X4), rhs_scale=w[1][:, w_cols],
-                                    start=(start and i == 0), stop=(stop and i == len(steps) - 1))
+        banks = {}
+        first_sum = {}
+        sums = []
 
-        a_bank = {}
-        c_bank = {}
-        a_plus_b = {}
+        def multiply(product, part=None):
+            kind, n0, width, m0 = product
+            count = WIDE // width
+            gs = list(range(E_PASSES) if kind == "a" else range(E_PASSES, PASSES))
+            first = gs[0]
+            if part != 1:
+                banks[product] = take_bank([P, count, width])
+            if part is not None:
+                gs = gs[2 * part:2 * part + 2]
+            for i in range(count):
+                m = m0 + i
+                x = x_mx[("e", m // 2)] if kind == "a" else x_mx[("f", m)]
+                x_first = 2 * (m % 2) if kind == "a" else 0
+                for g in gs:
+                    x_cols = slice((x_first + g - first) * P, (x_first + g - first + 1) * P)
+                    w = w_mx[(g, n0)]
+                    if part is None:
+                        start, stop = g == gs[0], g == gs[-1]
+                    else:
+                        start, stop = (part, i, g) == (0, 0, gs[0]), (part, i, g) == (1, count - 1, gs[-1])
+                    nc.tensor.matmul_mx(out=banks[product][1][:, i, :], lhsT=x[0][:, x_cols].bitcast(FP8X4), lhsT_scale=x[1][:, x_cols],
+                                        rhs=w[0].bitcast(FP8X4), rhs_scale=w[1], start=start, stop=stop)
 
-        def mm_a(s):
-            c, pair = divmod(s, PAIRS)
-            a_bank[s] = take_bank([P, 2, CHUNK])
-            for i in range(2):
-                passes(a_bank[s][1][:, i, :], x_mx[("e", pair)], 2 * i, c, [0])
+        def empty(product):
+            kind, n0, width, m0 = product
+            number, bank = banks[product]
+            count = WIDE // width
+            half, pair = n0 // HALF, m0 // 2
+            opens = (kind == "a") == (half < LAST_HALF)
+            if opens and half < 2 and pair not in first_sum:
+                first_sum[pair] = work.tile([P, 2, WIDE], F32, name="first_wide", bufs=PAIRS)
+            if opens and half >= 2 and pair % 2 == 0:
+                first_sum[(half, pair // 2)] = once.tile([P, 2, 2, HALF], F32, name="first_half", tag="e_raw%d" % (2 * (half % 2) + pair // 2))
+            if half < 2:
+                part = first_sum[pair][:, m0 % 2:m0 % 2 + count, n0:n0 + width]
+            else:
+                part = first_sum[(half, pair // 2)][:, pair % 2]
+            if opens:
+                dst = part
+            else:
+                dst = work.tile([P, count, width], F32, name="z", bufs=9)[:]
+                sums.append((dst, product))
+            if kind == "a":
+                other = bias[:, n0:n0 + width].unsqueeze(1).to_broadcast([P, 2, width]) if opens else part
+                nc.vector.tensor_tensor(out=dst, in0=bank[:], in1=other, op=ADD)
+            else:
+                for i in range(count):
+                    other = bias[:, n0:n0 + width] if opens else part[:, i, :]
+                    nc.vector.scalar_tensor_tensor(out=dst[:, i, :], in0=bank[:, i, :], scalar=trusts[:, m0 + i:m0 + i + 1],
+                                                   in1=other, op0=MULT, op1=ADD)
+            free_banks.append(number)
 
-        def add_b(s):
-            c = s // PAIRS
-            a_plus_b[s] = work.tile([P, 2, CHUNK], F32, name="a_plus_b", bufs=12)
-            row = bias[:, c * CHUNK:(c + 1) * CHUNK].unsqueeze(1).to_broadcast([P, 2, CHUNK])
-            nc.vector.tensor_tensor(out=a_plus_b[s][:], in0=a_bank[s][1][:], in1=row, op=ADD)
-            free_banks.append(a_bank[s][0])
+        def finish():
+            z, (kind, n0, width, m0) = sums.pop(0)
+            count = WIDE // width
+            res = work.tile([P, count, width], F32, name="res", bufs=5)
+            very_last = (kind, n0 // HALF, m0 // 2) == ("a", LAST_HALF, PAIRS - 1)
+            for tiles in ([slice(0, 1), slice(1, 2)] if very_last else [slice(0, count)]):
+                nc.scalar.activation(out=res[:, tiles], in_=z[:, tiles], func=ACT.Silu)
+                nc.sync.dma_start(out=o_v[:, m0 + tiles.start:m0 + tiles.stop, n0:n0 + width], in_=res[:, tiles])
 
-        def mm_c(s):
-            c, pair = divmod(s, PAIRS)
-            first = take_bank([P, 2, CHUNK])
-            c_bank[s] = [first, take_bank([P, 2, CHUNK]) if s == CHUNKS * PAIRS - 1 else first]
-            for i in range(2):
-                passes(c_bank[s][i][1][:, i, :], x_mx[("f", 2 * pair + i)], 0, c, [1, 2])
+        def halves(kind, h):
+            return [(kind, h * HALF, HALF, 2 * pair) for pair in range(PAIRS)]
 
-        def mm_c_half(s, part):
-            c, pair = divmod(s, PAIRS)
-            if part == 1:
-                c_bank[s] = take_bank([P, 2, CHUNK])
-            for i in range(2):
-                passes(c_bank[s][1][:, i, :], x_mx[("f", 2 * pair + i)], 2 * (part - 1), c, [part],
-                       start=(part == 1 and i == 0), stop=(part == 2 and i == 1))
+        def wides(c, first):
+            return [("c", c * WIDE, WIDE, m) for m in range(first, first + 4)]
 
-        sums = {}
+        windows = {5: halves("a", 0), 6: halves("a", 1), 7: wides(0, 0), 8: halves("a", 2), 9: wides(0, 4), 10: halves("a", 3),
+                   11: halves("c", 2), 12: halves("c", 3), 13: halves("a", 4), 15: halves("c", 4), 17: halves("c", 5), 18: halves("a", 5)}
+        last = len(UNITS)
+        on_vector = {14: 1, 16: 2}
 
-        def join(s):
-            pair = s % PAIRS
-            z = sums[s] = work.tile([P, 2, CHUNK], F32, name="z", bufs=4)
-            for i in range(2):
-                m = 2 * pair + i
-                nc.vector.scalar_tensor_tensor(out=z[:, i, :], in0=c_bank[s][i][1][:, i, :], scalar=trusts[:, m:m + 1],
-                                               in1=a_plus_b[s][:, i, :], op0=MULT, op1=ADD)
-            free_banks.append(c_bank[s][0][0])
+        def f_share(m):
+            return F0_ON_SCALAR if m == 0 else int(m >= F_LATE)
 
-        def finish(s):
-            c, pair = divmod(s, PAIRS)
-            res = work.tile([P, 2, CHUNK], F32, name="res", bufs=5)
-            pieces = [slice(0, 1), slice(1, 2)] if s == CHUNKS * PAIRS - 1 else [slice(0, 2)]
-            for tiles in pieces:
-                nc.scalar.activation(out=res[:, tiles], in_=sums[s][:, tiles], func=ACT.Silu)
-                nc.sync.dma_start(out=o_v[:, 2 * pair + tiles.start:2 * pair + tiles.stop, c * CHUNK:(c + 1) * CHUNK], in_=res[:, tiles])
-
-        scale_f(0, 2, "scalar")
-        scale_f(0, 2, "vector")
+        scale_f(0, F0_ON_SCALAR, "scalar")
+        scale_f(0, F0_ON_SCALAR, "vector")
         spread_w_scale()
         lace_w(0, range(2))
         widen_w(0, range(2))
         lace_w(0, range(2, 4))
-        scale_f(1, 0, "vector")
         turn_f(0)
+        lace_w(1, range(4))
         widen_w(0, range(2, 4), "vector")
-        lace_w(1)
-        turn_f(1)
-        widen_w(1)
-        quant_w(0)
+        scale_f(1, 0, "vector")
 
-        def early_share(pair):
-            return max(0, min(pair, G_BLOCKS))
-
-        for m in range(TILES):
-            pair, odd = divmod(m, 2)
-            k = PARTS + pair - 1
-            if m + 2 < TILES:
-                scale_f(m + 2, F_PASSES_ON_SCALAR * (m + 2 >= F_FROM), "scalar")
-            if 0 < m < TILES - 1:
-                turn_f(m + 1)
-            if m == 1:
-                turn_e(1)
-            if not odd and pair > 0:
-                mm_c(pair - 1)
-                mm_a(pair)
-            if m == PAIRS:
-                mm_a(PAIRS)
-            if PAIRS <= m < TILES - 1:
-                mm_a(m + 1)
-            if m > 0 and not odd:
-                widen_w(k)
-            quant_f(m)
-            if m + 2 < TILES:
-                scale_f(m + 2, F_PASSES_ON_SCALAR * (m + 2 >= F_FROM), "vector")
-            if m == 0:
-                lace_w(2)
-                turn_e(0)
-                widen_w(2)
-                quant_w(1)
-            if m == 1:
-                quant_e(0)
-                mm_a(0)
-            if odd:
+        for k in range(last + 1):
+            window = windows.get(k, [])
+            share = G_BLOCKS if window else 0
+            mine = on_vector.get(k, 0)
+            if k + 1 < last:
+                widen_w(k + 1, range(mine, 4))
+            if k < last:
                 quant_w(k)
-                if pair > 0:
-                    lace_w_gpsimd(k + 2, early_share(pair))
-                if pair == 1:
-                    add_b(0)
-                if pair > 0:
-                    add_b(pair)
-                    join(pair - 1)
-                if m > PAIRS:
-                    add_b(m - 1)
-                    add_b(m)
-                if pair == 0:
-                    lace_w(k + 1)
-                if pair + 1 < PAIRS:
-                    quant_e(pair + 1)
-            else:
-                if 0 < pair < PAIRS - 1:
-                    turn_e(pair + 1)
-                if pair > 0:
-                    lace_w(k + 1, range(4 - early_share(pair - 1)))
-                if pair > 1:
-                    finish(pair - 2)
-        mm_c(PAIRS - 1)
-        widen_w(2 * PARTS)
-        finish(PAIRS - 2)
-        lace_w(2 * PARTS + 1, range(4 - G_BLOCKS))
-        last = CHUNKS * PAIRS
-
-        def empty(i):
-            s = PAIRS + i // 2
-            if i % 2 == 0:
-                if PAIRS - 1 <= s - C_LAG - 1 < last:
-                    finish(s - C_LAG - 1)
-                if PAIRS - 1 <= s - C_LAG < last:
-                    join(s - C_LAG)
-                if s < last:
-                    mm_c(s)
-            else:
-                if TILES <= s + A_LEAD - A_LAG < last:
-                    add_b(s + A_LEAD - A_LAG)
-                if TILES <= s + A_LEAD < last:
-                    mm_a(s + A_LEAD)
-
-        def run(beat):
-            return range(2 * PAIRS * beat // PARTS, 2 * PAIRS * (beat + 1) // PARTS)
-
-        def late(beat):
-            reads = [i for i in run(beat) if PAIRS + i // 2 >= (TILES - A_LEAD + A_LAG if i % 2 else PAIRS - 1 + C_LAG)]
-            return max(0, min(G_BLOCKS, len(reads) - 1))
-
-        for k in range(2 * PARTS, UNITS + 2 * PARTS):
-            beat = k - 2 * PARTS
-            on_vector = int(beat % PARTS < W_ON_VECTOR)
-            if k + 1 < UNITS:
-                widen_w(k + 1, range(on_vector, 4))
-            if k < UNITS:
-                quant_w(k)
-            if k + 2 < UNITS:
-                lace_w(k + 2, range(4 - late(beat)))
-            if k + 2 < UNITS and late(beat):
-                lace_w_gpsimd(k + 2, late(beat))
-            if on_vector and k + 1 < UNITS:
-                widen_w(k + 1, range(on_vector), "vector")
-            for i in run(beat):
-                empty(i)
+            if k >= last - 5 and k < last:
+                kind, n0, width, gs = UNITS[k]
+                for product in halves(kind, n0 // HALF):
+                    multiply(product, None if kind == "a" else (gs[0] - E_PASSES) // 2)
+            if k + 2 < last:
+                lace_w(k + 2, range(4 - share))
+                if share:
+                    lace_w_gpsimd(k + 2, range(4 - share, 4))
+            if k + 2 < TILES:
+                scale_f(k + 2, f_share(k + 2), "scalar")
+            for product in window:
+                if len(sums) > BACKLOG * (last - 7 <= k < last - 1):
+                    finish()
+                empty(product)
+            if mine:
+                widen_w(k + 1, range(mine), "vector")
+            if 0 < k <= PAIRS:
+                quant_e(k - 1)
+            if k + 2 < TILES:
+                scale_f(k + 2, f_share(k + 2), "vector")
+            if k < TILES:
+                quant_f(k)
+            if k + 1 < TILES:
+                turn_f(k + 1)
+            if k < PAIRS:
+                turn_e(k)
+            if not window:
+                while len(sums) > BACKLOG * (last - 7 <= k < last - 1):
+                    finish()
+            if k < last - 5:
+                for product in windows.get(k + 1, []):
+                    multiply(product)
+        while sums:
+            finish()

@@ -27,12 +27,11 @@ F_BLOCKS = D // B
 W_BLOCKS = N // B
 HALF = 256
 WIDE = 512
-G_BLOCKS = 3
+G_COLUMNS = {"a": 352, "c": 384}
 F0_ON_SCALAR = 2
 SLOTS = 6
 LAST_HALF = N // HALF - 1
-F_LATE = 8
-BACKLOG = 4
+F_LATE = 5
 
 
 def a_unit(h):
@@ -104,17 +103,17 @@ def tile_drafter_feature_fusion_d2_kernel(tc, e, f_bytes, f_scale, w_bytes, w_sc
         load_f(0)
         load_w(0)
         load_w(1)
-        load_f(1)
         load_e(0)
+        load_f(1)
         load_w(2)
-        load_f(2)
         load_e(1)
+        load_f(2)
         for m in range(3, TILES):
             load_w(m)
-            load_f(m)
             if m - 1 < PAIRS:
                 load_e(m - 1)
-            if m == PAIRS:
+            load_f(m)
+            if m == 3:
                 nc.sync.dma_start(out=bias[:, 0:WIDE], in_=b[0:WIDE].partition_broadcast(P))
         nc.sync.dma_start(out=trusts[:], in_=trust.rearrange("(p m) o -> p (m o)", m=TILES))
         nc.sync.dma_start(out=bias[:, WIDE:N], in_=b[WIDE:N].partition_broadcast(P))
@@ -148,20 +147,17 @@ def tile_drafter_feature_fusion_d2_kernel(tc, e, f_bytes, f_scale, w_bytes, w_sc
             kind, n0, width, gs = UNITS[k]
             return divmod(block, width // B)
 
-        def lace_w(k, blocks):
-            tile = work.tile([P, len(blocks) * 4 * B], U8, name="w_laced", bufs=4)
-            src = w_raw[k][:, :, blocks.start * B:blocks.stop * B].rearrange("p t (c i) -> p c t i", i=4)
+        def lace_w(k, first, stop):
+            tile = work.tile([P, (stop - first) * 4], U8, name="w_laced", bufs=4)
+            src = w_raw[k][:, :, first:stop].rearrange("p t (c i) -> p c t i", i=4)
             nc.vector.tensor_copy(out=tile[:].rearrange("p (c i t) -> p c t i", i=4, t=4), in_=src)
-            for n, block in enumerate(blocks):
-                laced[(k, block)] = tile[:, n * 4 * B:(n + 1) * 4 * B]
+            laced.setdefault(k, []).append((tile, first, stop))
 
-        def lace_w_gpsimd(k, blocks):
+        def lace_w_gpsimd(k, first, stop):
             slot = lent[k] = free_slots.pop()
-            tile = work.tile([P, len(blocks) * 4 * B], U8, align_bytes=64, name="w_laced_late", tag="slot%d" % slot, bufs=1)
-            src = w_raw[k][:, :, blocks.start * B:blocks.stop * B]
-            nc.gpsimd.tensor_copy(out=tile[:].rearrange("p (c t) -> p c t", t=4), in_=src.rearrange("p t c -> p c t"))
-            for n, block in enumerate(blocks):
-                laced[(k, block)] = tile[:, n * 4 * B:(n + 1) * 4 * B]
+            tile = work.tile([P, (stop - first) * 4], U8, align_bytes=64, name="w_laced_late", tag="slot%d" % slot, bufs=1)
+            nc.gpsimd.tensor_copy(out=tile[:].rearrange("p (c t) -> p c t", t=4), in_=w_raw[k][:, :, first:stop].rearrange("p t c -> p c t"))
+            laced[k].append((tile, first, stop))
 
         def widen_w(k, blocks, part="scalar"):
             kind, n0, width, gs = UNITS[k]
@@ -171,12 +167,15 @@ def tile_drafter_feature_fusion_d2_kernel(tc, e, f_bytes, f_scale, w_bytes, w_sc
             for block in blocks:
                 h, j = block_of(k, block)
                 scale = w_scales[:, gs[h], n0 // B + j:n0 // B + j + 1]
-                src = laced[(k, block)].bitcast(FP8)
-                dst = wide[k][0][:, 4 * B * block:4 * B * (block + 1)]
-                if part == "vector":
-                    nc.vector.tensor_scalar(out=dst, in0=src, scalar1=scale, scalar2=None, op0=MULT)
-                else:
-                    nc.scalar.activation(out=dst, in_=src, func=ACT.Copy, scale=scale)
+                for tile, first, stop in laced[k]:
+                    c0, c1 = max(first, block * B), min(stop, (block + 1) * B)
+                    if c0 < c1:
+                        src = tile[:, 4 * (c0 - first):4 * (c1 - first)].bitcast(FP8)
+                        dst = wide[k][0][:, 4 * c0:4 * c1]
+                        if part == "vector":
+                            nc.vector.tensor_scalar(out=dst, in0=src, scalar1=scale, scalar2=None, op0=MULT)
+                        else:
+                            nc.scalar.activation(out=dst, in_=src, func=ACT.Copy, scale=scale)
             if part == "scalar" and k in lent:
                 free_slots.append(lent[k])
 
@@ -211,9 +210,10 @@ def tile_drafter_feature_fusion_d2_kernel(tc, e, f_bytes, f_scale, w_bytes, w_sc
                     nc.vector.tensor_scalar(out=halves[:, 32 * q:32 * q + 32], in0=src.rearrange("p (r u e) -> p r u e", u=2, e=2),
                                             scalar1=scale, scalar2=None, op0=MULT)
 
+        in_psum = []
+
         def turn(src, key, unsorted):
             words = src[:].bitcast(F32)
-            turned[key] = work.tile([P, 2048], BF16, align_bytes=64, name="turned", bufs=4)
             for half in range(2):
                 number, bank = take_bank([P, 2, 2, P])
                 for h in range(2):
@@ -221,6 +221,13 @@ def tile_drafter_feature_fusion_d2_kernel(tc, e, f_bytes, f_scale, w_bytes, w_sc
                     for u in range(2):
                         cols = slice(256 * g + u, 256 * (g + 1), 2) if g < unsorted else slice(256 * g + P * u, 256 * g + P * (u + 1))
                         nc.tensor.transpose(bank[:, h, u, :], words[:, cols], ident[:])
+                in_psum.append((key, half, number, bank))
+
+        def copy_turned():
+            while in_psum:
+                key, half, number, bank = in_psum.pop(0)
+                if half == 0:
+                    turned[key] = work.tile([P, 2048], BF16, align_bytes=64, name="turned", bufs=4)
                 dst = turned[key][:, 1024 * half:1024 * (half + 1)].bitcast(F32).rearrange("p (h r u) -> p h r u", h=2, u=2)
                 nc.scalar.copy(out=dst, in_=bank[:].rearrange("p h u r -> p h r u"))
                 free_banks.append(number)
@@ -241,28 +248,23 @@ def tile_drafter_feature_fusion_d2_kernel(tc, e, f_bytes, f_scale, w_bytes, w_sc
         first_sum = {}
         sums = []
 
-        def multiply(product, part=None):
+        def multiply(product, gs=None):
             kind, n0, width, m0 = product
             count = WIDE // width
-            gs = list(range(E_PASSES) if kind == "a" else range(E_PASSES, PASSES))
-            first = gs[0]
-            if part != 1:
+            whole = list(range(E_PASSES) if kind == "a" else range(E_PASSES, PASSES))
+            gs = gs or whole
+            if gs[0] == whole[0]:
                 banks[product] = take_bank([P, count, width])
-            if part is not None:
-                gs = gs[2 * part:2 * part + 2]
             for i in range(count):
                 m = m0 + i
                 x = x_mx[("e", m // 2)] if kind == "a" else x_mx[("f", m)]
                 x_first = 2 * (m % 2) if kind == "a" else 0
                 for g in gs:
-                    x_cols = slice((x_first + g - first) * P, (x_first + g - first + 1) * P)
+                    x_cols = slice((x_first + g - whole[0]) * P, (x_first + g - whole[0] + 1) * P)
                     w = w_mx[(g, n0)]
-                    if part is None:
-                        start, stop = g == gs[0], g == gs[-1]
-                    else:
-                        start, stop = (part, i, g) == (0, 0, gs[0]), (part, i, g) == (1, count - 1, gs[-1])
                     nc.tensor.matmul_mx(out=banks[product][1][:, i, :], lhsT=x[0][:, x_cols].bitcast(FP8X4), lhsT_scale=x[1][:, x_cols],
-                                        rhs=w[0].bitcast(FP8X4), rhs_scale=w[1], start=start, stop=stop)
+                                        rhs=w[0].bitcast(FP8X4), rhs_scale=w[1],
+                                        start=(i, g) == (0, whole[0]), stop=(i, g) == (count - 1, whole[-1]))
 
         def empty(product):
             kind, n0, width, m0 = product
@@ -308,10 +310,15 @@ def tile_drafter_feature_fusion_d2_kernel(tc, e, f_bytes, f_scale, w_bytes, w_sc
         def wides(c, first):
             return [("c", c * WIDE, WIDE, m) for m in range(first, first + 4)]
 
-        windows = {5: halves("a", 0), 6: halves("a", 1), 7: wides(0, 0), 8: halves("a", 2), 9: wides(0, 4), 10: halves("a", 3),
-                   11: halves("c", 2), 12: halves("c", 3), 13: halves("a", 4), 15: halves("c", 4), 17: halves("c", 5), 18: halves("a", 5)}
+        windows = {2: halves("a", 0)[:2] + halves("a", 1)[:2], 4: halves("a", 0)[2:] + halves("a", 1)[2:], 6: wides(0, 0),
+                   7: halves("a", 2), 8: halves("a", 3), 9: wides(0, 4), 10: halves("c", 2), 12: halves("c", 3),
+                   13: halves("a", 4), 15: halves("c", 4), 16: halves("c", 5)[:2], 17: halves("c", 5)[2:], 18: halves("a", 5)}
         last = len(UNITS)
-        on_vector = {14: 1, 16: 2}
+        follow = {k: halves(UNITS[k][0], UNITS[k][1] // HALF) for k in range(10, last)}
+        follow[5] = wides(0, 0)
+        follow[6] = halves("a", 2)
+        follow[7] = halves("a", 3)
+        on_vector = {11: 1, 14: 2, 16: 2}
 
         def f_share(m):
             return F0_ON_SCALAR if m == 0 else int(m >= F_LATE)
@@ -319,53 +326,56 @@ def tile_drafter_feature_fusion_d2_kernel(tc, e, f_bytes, f_scale, w_bytes, w_sc
         scale_f(0, F0_ON_SCALAR, "scalar")
         scale_f(0, F0_ON_SCALAR, "vector")
         spread_w_scale()
-        lace_w(0, range(2))
+        lace_w(0, 0, HALF)
         widen_w(0, range(2))
-        lace_w(0, range(2, 4))
+        lace_w(0, HALF, WIDE)
         turn_f(0)
-        lace_w(1, range(4))
+        copy_turned()
+        lace_w(1, 0, WIDE)
         widen_w(0, range(2, 4), "vector")
         scale_f(1, 0, "vector")
+        turn_e(0)
+        copy_turned()
 
         for k in range(last + 1):
             window = windows.get(k, [])
-            share = G_BLOCKS if window else 0
+            share = G_COLUMNS[window[0][0]] if window else 0
             mine = on_vector.get(k, 0)
+            if k + 1 < TILES:
+                turn_f(k + 1)
             if k + 1 < last:
                 widen_w(k + 1, range(mine, 4))
+            copy_turned()
+            for n in range(len(sums) if k == last - 1 else min(len(sums), 2 if window else 1)):
+                finish()
             if k < last:
                 quant_w(k)
-            if k >= last - 5 and k < last:
-                kind, n0, width, gs = UNITS[k]
-                for product in halves(kind, n0 // HALF):
-                    multiply(product, None if kind == "a" else (gs[0] - E_PASSES) // 2)
+            if mine:
+                widen_w(k + 1, range(mine), "vector")
+            for product in follow.get(k, []):
+                multiply(product, UNITS[k][3])
             if k + 2 < last:
-                lace_w(k + 2, range(4 - share))
+                lace_w(k + 2, 0, WIDE - share)
                 if share:
-                    lace_w_gpsimd(k + 2, range(4 - share, 4))
+                    lace_w_gpsimd(k + 2, WIDE - share, WIDE)
             if k + 2 < TILES:
                 scale_f(k + 2, f_share(k + 2), "scalar")
             for product in window:
-                if len(sums) > BACKLOG * (last - 7 <= k < last - 1):
-                    finish()
                 empty(product)
-            if mine:
-                widen_w(k + 1, range(mine), "vector")
-            if 0 < k <= PAIRS:
-                quant_e(k - 1)
+                if k == last:
+                    finish()
+            if k < PAIRS:
+                quant_e(k)
             if k + 2 < TILES:
                 scale_f(k + 2, f_share(k + 2), "vector")
             if k < TILES:
                 quant_f(k)
-            if k + 1 < TILES:
-                turn_f(k + 1)
-            if k < PAIRS:
-                turn_e(k)
-            if not window:
-                while len(sums) > BACKLOG * (last - 7 <= k < last - 1):
-                    finish()
-            if k < last - 5:
-                for product in windows.get(k + 1, []):
+            if k + 1 < PAIRS:
+                turn_e(k + 1)
+            copy_turned()
+            for product in windows.get(k + 1, []):
+                if product not in banks:
                     multiply(product)
-        while sums:
-            finish()
+            if k == 4:
+                for product in wides(0, 0):
+                    multiply(product, [2, 3, 4])

@@ -31,7 +31,9 @@ G_COLUMNS = {"a": 352, "c": 384}
 F0_ON_SCALAR = 2
 SLOTS = 6
 LAST_HALF = N // HALF - 1
-F_LATE = 5
+F_LATE = 3
+PE_UNITS = (2, 3, 5, 7)
+PE_BLOCKS = 2
 
 
 def a_unit(h):
@@ -77,15 +79,24 @@ def tile_drafter_feature_fusion_d2_kernel(tc, e, f_bytes, f_scale, w_bytes, w_sc
         nc.scalar.activation(out=warm[:], in_=zero[:], func=ACT.Silu)
 
         w_raw = {}
+        w_blocks = {}
         e_raw = {}
         f_raw = {}
 
         def load_w(k):
             kind, n0, width, gs = UNITS[k]
-            raw = once.tile([P, 4, WIDE], U8, name="w_raw%d" % k)
+            first = PE_BLOCKS * B if k in PE_UNITS else 0
+            if first:
+                w_blocks[k] = once.tile([P, PE_BLOCKS, 4, B], U8, name="w_blocks%d" % k)
+                for block in range(PE_BLOCKS):
+                    h, j = divmod(block, width // B)
+                    nc.sync.dma_start(out=w_blocks[k][:, block], in_=w_v[:, gs[h], :, n0 + j * B:n0 + (j + 1) * B])
+            raw = once.tile([P, 4, WIDE - first], U8, name="w_raw%d" % k)
             for h, g in enumerate(gs):
-                nc.sync.dma_start(out=raw[:, :, h * width:(h + 1) * width], in_=w_v[:, g, :, n0:n0 + width])
-            w_raw[k] = raw
+                c0, c1 = max(first, h * width), (h + 1) * width
+                if c0 < c1:
+                    nc.sync.dma_start(out=raw[:, :, c0 - first:c1 - first], in_=w_v[:, g, :, n0 + c0 - h * width:n0 + width])
+            w_raw[k] = (raw, first)
 
         def load_e(pair):
             raw = once.tile([P, 2 * E], BF16, name="e_raw%d" % pair)
@@ -122,12 +133,13 @@ def tile_drafter_feature_fusion_d2_kernel(tc, e, f_bytes, f_scale, w_bytes, w_sc
 
         free_banks = list(range(8))
 
-        def take_bank(shape):
+        def take_bank(shape, dtype=F32):
             number = free_banks.pop(0)
-            return number, psum.tile(shape, F32, name="bank%d" % number)
+            return number, psum.tile(shape, dtype, name="bank%d" % number)
 
         ident = once.tile([P, P], F32)
         make_identity(nc, ident[:])
+        ident16 = once.tile([P, P], BF16)
 
         w_scales = once.tile([P, PASSES, W_BLOCKS], F32)
 
@@ -149,14 +161,15 @@ def tile_drafter_feature_fusion_d2_kernel(tc, e, f_bytes, f_scale, w_bytes, w_sc
 
         def lace_w(k, first, stop):
             tile = work.tile([P, (stop - first) * 4], U8, name="w_laced", bufs=4)
-            src = w_raw[k][:, :, first:stop].rearrange("p t (c i) -> p c t i", i=4)
+            raw, origin = w_raw[k]
+            src = raw[:, :, first - origin:stop - origin].rearrange("p t (c i) -> p c t i", i=4)
             nc.vector.tensor_copy(out=tile[:].rearrange("p (c i t) -> p c t i", i=4, t=4), in_=src)
             laced.setdefault(k, []).append((tile, first, stop))
 
         def lace_w_gpsimd(k, first, stop):
             slot = lent[k] = free_slots.pop()
             tile = work.tile([P, (stop - first) * 4], U8, align_bytes=64, name="w_laced_late", tag="slot%d" % slot, bufs=1)
-            nc.gpsimd.tensor_copy(out=tile[:].rearrange("p (c t) -> p c t", t=4), in_=w_raw[k][:, :, first:stop].rearrange("p t c -> p c t"))
+            nc.gpsimd.tensor_copy(out=tile[:].rearrange("p (c t) -> p c t", t=4), in_=w_raw[k][0][:, :, first:stop].rearrange("p t c -> p c t"))
             laced[k].append((tile, first, stop))
 
         def widen_w(k, blocks, part="scalar"):
@@ -167,7 +180,7 @@ def tile_drafter_feature_fusion_d2_kernel(tc, e, f_bytes, f_scale, w_bytes, w_sc
             for block in blocks:
                 h, j = block_of(k, block)
                 scale = w_scales[:, gs[h], n0 // B + j:n0 // B + j + 1]
-                for tile, first, stop in laced[k]:
+                for tile, first, stop in laced.get(k, []):
                     c0, c1 = max(first, block * B), min(stop, (block + 1) * B)
                     if c0 < c1:
                         src = tile[:, 4 * (c0 - first):4 * (c1 - first)].bitcast(FP8)
@@ -178,6 +191,29 @@ def tile_drafter_feature_fusion_d2_kernel(tc, e, f_bytes, f_scale, w_bytes, w_sc
                             nc.scalar.activation(out=dst, in_=src, func=ACT.Copy, scale=scale)
             if part == "scalar" and k in lent:
                 free_slots.append(lent[k])
+
+        planes = {}
+        in_bank = {}
+
+        def widen_planes(k):
+            kind, n0, width, gs = UNITS[k]
+            planes[k] = work.tile([P, PE_BLOCKS, 4, B], BF16, name="w_planes", bufs=2)
+            for block in range(PE_BLOCKS):
+                h, j = block_of(k, block)
+                nc.vector.tensor_scalar(out=planes[k][:, block].rearrange("p t c -> p (t c)"),
+                                        in0=w_blocks[k][:, block].rearrange("p t c -> p (t c)").bitcast(FP8),
+                                        scalar1=w_scales[:, gs[h], n0 // B + j:n0 // B + j + 1], scalar2=None, op0=MULT)
+
+        def lace_planes(k):
+            in_bank[k] = [take_bank([P, 2, 4 * B], BF16) for half in range(PE_BLOCKS // 2)]
+            for block in range(PE_BLOCKS):
+                nc.tensor.matmul(in_bank[k][block // 2][1][:, block % 2], lhsT=ident16[:],
+                                 rhs=planes[k][:, block].rearrange("p t c -> p c t"), start=True, stop=True)
+
+        def copy_laced(k):
+            for half, (number, bank) in enumerate(in_bank[k]):
+                nc.scalar.copy(out=wide[k][0][:, 1024 * half:1024 * (half + 1)], in_=bank[:].rearrange("p b c -> p (b c)"))
+                free_banks.append(number)
 
         def quantise(src, name, bufs):
             codes = work.tile([P, 512], U32, align_bytes=256, name=name + "_codes", bufs=bufs)
@@ -287,7 +323,8 @@ def tile_drafter_feature_fusion_d2_kernel(tc, e, f_bytes, f_scale, w_bytes, w_sc
                 sums.append((dst, product))
             if kind == "a":
                 other = bias[:, n0:n0 + width].unsqueeze(1).to_broadcast([P, 2, width]) if opens else part
-                nc.vector.tensor_tensor(out=dst, in0=bank[:], in1=other, op=ADD)
+                for tiles in ([slice(0, 1), slice(1, 2)] if (half, pair) == (LAST_HALF, PAIRS - 1) else [slice(0, 2)]):
+                    nc.vector.tensor_tensor(out=dst[:, tiles], in0=bank[:, tiles], in1=other[:, tiles], op=ADD)
             else:
                 for i in range(count):
                     other = bias[:, n0:n0 + width] if opens else part[:, i, :]
@@ -298,7 +335,7 @@ def tile_drafter_feature_fusion_d2_kernel(tc, e, f_bytes, f_scale, w_bytes, w_sc
         def finish():
             z, (kind, n0, width, m0) = sums.pop(0)
             count = WIDE // width
-            res = work.tile([P, count, width], F32, name="res", bufs=5)
+            res = work.tile([P, count, width], F32, name="res", bufs=6)
             very_last = (kind, n0 // HALF, m0 // 2) == ("a", LAST_HALF, PAIRS - 1)
             for tiles in ([slice(0, 1), slice(1, 2)] if very_last else [slice(0, count)]):
                 nc.scalar.activation(out=res[:, tiles], in_=z[:, tiles], func=ACT.Silu)
@@ -312,13 +349,13 @@ def tile_drafter_feature_fusion_d2_kernel(tc, e, f_bytes, f_scale, w_bytes, w_sc
 
         windows = {2: halves("a", 0)[:2] + halves("a", 1)[:2], 4: halves("a", 0)[2:] + halves("a", 1)[2:], 6: wides(0, 0),
                    7: halves("a", 2), 8: halves("a", 3), 9: wides(0, 4), 10: halves("c", 2), 12: halves("c", 3),
-                   13: halves("a", 4), 15: halves("c", 4), 16: halves("c", 5)[:2], 17: halves("c", 5)[2:], 18: halves("a", 5)}
+                   13: halves("a", 4), 15: halves("c", 4), 17: halves("c", 5)[:3] + halves("a", 5)[:3] + halves("c", 5)[3:] + halves("a", 5)[3:]}
         last = len(UNITS)
         follow = {k: halves(UNITS[k][0], UNITS[k][1] // HALF) for k in range(10, last)}
         follow[5] = wides(0, 0)
         follow[6] = halves("a", 2)
         follow[7] = halves("a", 3)
-        on_vector = {11: 1, 14: 2, 16: 2}
+        on_vector = {11: 1, 14: 2, 16: 3}
 
         def f_share(m):
             return F0_ON_SCALAR if m == 0 else int(m >= F_LATE)
@@ -332,6 +369,7 @@ def tile_drafter_feature_fusion_d2_kernel(tc, e, f_bytes, f_scale, w_bytes, w_sc
         turn_f(0)
         copy_turned()
         lace_w(1, 0, WIDE)
+        nc.vector.tensor_copy(out=ident16[:], in_=ident[:])
         widen_w(0, range(2, 4), "vector")
         scale_f(1, 0, "vector")
         turn_e(0)
@@ -345,6 +383,8 @@ def tile_drafter_feature_fusion_d2_kernel(tc, e, f_bytes, f_scale, w_bytes, w_sc
                 turn_f(k + 1)
             if k + 1 < last:
                 widen_w(k + 1, range(mine, 4))
+            if k + 1 in PE_UNITS:
+                copy_laced(k + 1)
             copy_turned()
             for n in range(len(sums) if k == last - 1 else min(len(sums), 2 if window else 1)):
                 finish()
@@ -354,7 +394,12 @@ def tile_drafter_feature_fusion_d2_kernel(tc, e, f_bytes, f_scale, w_bytes, w_sc
                 widen_w(k + 1, range(mine), "vector")
             for product in follow.get(k, []):
                 multiply(product, UNITS[k][3])
-            if k + 2 < last:
+            if k + 2 in PE_UNITS:
+                widen_planes(k + 2)
+                lace_planes(k + 2)
+                if PE_BLOCKS < 4:
+                    lace_w(k + 2, PE_BLOCKS * B, WIDE)
+            elif k + 2 < last:
                 lace_w(k + 2, 0, WIDE - share)
                 if share:
                     lace_w_gpsimd(k + 2, WIDE - share, WIDE)
@@ -362,7 +407,7 @@ def tile_drafter_feature_fusion_d2_kernel(tc, e, f_bytes, f_scale, w_bytes, w_sc
                 scale_f(k + 2, f_share(k + 2), "scalar")
             for product in window:
                 empty(product)
-                if k == last:
+                if k >= last - 1 and product[0] == "a":
                     finish()
             if k < PAIRS:
                 quant_e(k)
@@ -374,7 +419,7 @@ def tile_drafter_feature_fusion_d2_kernel(tc, e, f_bytes, f_scale, w_bytes, w_sc
                 turn_e(k + 1)
             copy_turned()
             for product in windows.get(k + 1, []):
-                if product not in banks:
+                if product not in banks and k < 10:
                     multiply(product)
             if k == 4:
                 for product in wides(0, 0):

@@ -27,7 +27,7 @@ F_BLOCKS = D // B
 W_BLOCKS = N // B
 HALF = 256
 WIDE = 512
-G_COLUMNS = {"a": 352, "c": 384}
+G_COLUMNS = {"a": 416, "c": 448}
 F0_ON_SCALAR = 2
 SLOTS = 6
 LAST_HALF = N // HALF - 1
@@ -169,7 +169,8 @@ def tile_drafter_feature_fusion_d2_kernel(tc, e, f_bytes, f_scale, w_bytes, w_sc
         def lace_w_gpsimd(k, first, stop):
             slot = lent[k] = free_slots.pop()
             tile = work.tile([P, (stop - first) * 4], U8, align_bytes=64, name="w_laced_late", tag="slot%d" % slot, bufs=1)
-            nc.gpsimd.tensor_copy(out=tile[:].rearrange("p (c t) -> p c t", t=4), in_=w_raw[k][0][:, :, first:stop].rearrange("p t c -> p c t"))
+            nc.gpsimd.tensor_copy(out=tile[:].rearrange("p (c i t) -> p c t i", i=8, t=4),
+                                  in_=w_raw[k][0][:, :, first:stop].rearrange("p t (c i) -> p c t i", i=8))
             laced[k].append((tile, first, stop))
 
         def widen_w(k, blocks, part="scalar"):

@@ -1,7 +1,7 @@
 from contextlib import ExitStack
 
 import concourse.mybir as mybir
-from concourse.masks import make_block_diagonal, make_identity
+from concourse.masks import make_identity
 
 T, E, D, N = 1024, 1024, 2048, 1536
 FLOPS = 2 * T * (E + D) * N
@@ -27,7 +27,7 @@ F_BLOCKS = D // B
 W_BLOCKS = N // B
 HALF = 256
 WIDE = 512
-G_COLUMNS = {"a": 416, "c": 448}
+G_COLUMNS = 384
 F0_ON_SCALAR = 2
 SLOTS = 6
 LAST_HALF = N // HALF - 1
@@ -60,11 +60,16 @@ def tile_drafter_feature_fusion_d2_kernel(tc, e, f_bytes, f_scale, w_bytes, w_sc
         psum = ctx.enter_context(tc.psum_pool(name="psum", bufs=1))
         w_scale_rows = once.tile([P, PASSES, W_BLOCKS], F32)
         nc.vector.memset(w_scale_rows[:], 0.0)
+        ctx.enter_context(tc.manual_schedule())
+        ident = once.tile([P, P], F32)
+        nc.vector.memset(ident[:], 0.0)
+        make_identity(nc, ident[:], nomemset=True)
         zero = once.tile([P, 1], F32)
         nc.vector.memset(zero[:], 0.0)
         quadrants = once.tile([P, P], F32)
-        make_block_diagonal(nc, quadrants[:], 32)
-        ctx.enter_context(tc.manual_schedule())
+        nc.vector.memset(quadrants[:], 0.0)
+        for q in range(4):
+            nc.vector.memset(quadrants[32 * q:32 * (q + 1), 32 * q:32 * (q + 1)], 1.0)
 
         e_v = e.rearrange("(p m) k -> p m k", m=TILES)
         f_v = f_bytes.rearrange("(p m) k -> p m k", m=TILES)
@@ -137,8 +142,6 @@ def tile_drafter_feature_fusion_d2_kernel(tc, e, f_bytes, f_scale, w_bytes, w_sc
             number = free_banks.pop(0)
             return number, psum.tile(shape, dtype, name="bank%d" % number)
 
-        ident = once.tile([P, P], F32)
-        make_identity(nc, ident[:])
         ident16 = once.tile([P, P], BF16)
 
         w_scales = once.tile([P, PASSES, W_BLOCKS], F32)
@@ -378,7 +381,7 @@ def tile_drafter_feature_fusion_d2_kernel(tc, e, f_bytes, f_scale, w_bytes, w_sc
 
         for k in range(last + 1):
             window = windows.get(k, [])
-            share = G_COLUMNS[window[0][0]] if window else 0
+            share = G_COLUMNS if window else 0
             mine = on_vector.get(k, 0)
             if k + 1 < TILES:
                 turn_f(k + 1)

@@ -27,7 +27,7 @@ F_BLOCKS = D // B
 W_BLOCKS = N // B
 HALF = 256
 WIDE = 512
-G_COLUMNS = 384
+G_COLUMNS = {("a", WIDE): 384, ("a", HALF): 384, ("c", WIDE): 416, ("c", HALF): 448}
 F0_ON_SCALAR = 2
 SLOTS = 6
 LAST_HALF = N // HALF - 1
@@ -48,7 +48,7 @@ def c_half(h):
     return [("c", h * HALF, HALF, [g, g + 1]) for g in range(E_PASSES, PASSES, 2)]
 
 
-UNITS = ([a_unit(0), a_unit(1)] + c_wide(0) + [a_unit(2), a_unit(3)] + c_half(2) + c_half(3)
+UNITS = ([("a", 0, WIDE, [g]) for g in range(E_PASSES)] + c_wide(0) + [a_unit(2), a_unit(3)] + c_half(2) + c_half(3)
          + [a_unit(4)] + c_half(4) + c_half(5) + [a_unit(5)])
 
 
@@ -165,8 +165,8 @@ def tile_drafter_feature_fusion_d2_kernel(tc, e, f_bytes, f_scale, w_bytes, w_sc
         def lace_w(k, first, stop):
             tile = work.tile([P, (stop - first) * 4], U8, name="w_laced", bufs=4)
             raw, origin = w_raw[k]
-            src = raw[:, :, first - origin:stop - origin].rearrange("p t (c i) -> p c t i", i=4)
-            nc.vector.tensor_copy(out=tile[:].rearrange("p (c i t) -> p c t i", i=4, t=4), in_=src)
+            src = raw[:, :, first - origin:stop - origin].rearrange("p t (c i) -> p c t i", i=8)
+            nc.vector.tensor_copy(out=tile[:].rearrange("p (c i t) -> p c t i", i=8, t=4), in_=src)
             laced.setdefault(k, []).append((tile, first, stop))
 
         def lace_w_gpsimd(k, first, stop):
@@ -174,7 +174,7 @@ def tile_drafter_feature_fusion_d2_kernel(tc, e, f_bytes, f_scale, w_bytes, w_sc
             tile = work.tile([P, (stop - first) * 4], U8, align_bytes=64, name="w_laced_late", tag="slot%d" % slot, bufs=1)
             nc.gpsimd.tensor_copy(out=tile[:].rearrange("p (c i t) -> p c t i", i=8, t=4),
                                   in_=w_raw[k][0][:, :, first:stop].rearrange("p t (c i) -> p c t i", i=8))
-            laced[k].append((tile, first, stop))
+            laced.setdefault(k, []).append((tile, first, stop))
 
         def widen_w(k, blocks, part="scalar"):
             kind, n0, width, gs = UNITS[k]
@@ -326,8 +326,8 @@ def tile_drafter_feature_fusion_d2_kernel(tc, e, f_bytes, f_scale, w_bytes, w_sc
                 dst = work.tile([P, count, width], F32, name="z", bufs=9)[:]
                 sums.append((dst, product))
             if kind == "a":
-                other = bias[:, n0:n0 + width].unsqueeze(1).to_broadcast([P, 2, width]) if opens else part
-                for tiles in ([slice(0, 1), slice(1, 2)] if (half, pair) == (LAST_HALF, PAIRS - 1) else [slice(0, 2)]):
+                other = bias[:, n0:n0 + width].unsqueeze(1).to_broadcast([P, count, width]) if opens else part
+                for tiles in ([slice(0, 1), slice(1, 2)] if (half, pair) == (LAST_HALF, PAIRS - 1) else [slice(0, count)]):
                     nc.vector.tensor_tensor(out=dst[:, tiles], in0=bank[:, tiles], in1=other[:, tiles], op=ADD)
             else:
                 for i in range(count):
@@ -348,10 +348,10 @@ def tile_drafter_feature_fusion_d2_kernel(tc, e, f_bytes, f_scale, w_bytes, w_sc
         def halves(kind, h):
             return [(kind, h * HALF, HALF, 2 * pair) for pair in range(PAIRS)]
 
-        def wides(c, first):
-            return [("c", c * WIDE, WIDE, m) for m in range(first, first + 4)]
+        def wides(c, first, kind="c"):
+            return [(kind, c * WIDE, WIDE, m) for m in range(first, first + 4)]
 
-        windows = {2: halves("a", 0)[:2] + halves("a", 1)[:2], 4: halves("a", 0)[2:] + halves("a", 1)[2:], 6: wides(0, 0),
+        windows = {2: wides(0, 0, "a"), 4: wides(0, 4, "a"), 6: wides(0, 0),
                    7: halves("a", 2), 8: halves("a", 3), 9: wides(0, 4), 10: halves("c", 2), 12: halves("c", 3),
                    13: halves("a", 4), 15: halves("c", 4), 17: halves("c", 5)[:3] + halves("a", 5)[:3] + halves("c", 5)[3:] + halves("a", 5)[3:]}
         last = len(UNITS)
@@ -381,7 +381,7 @@ def tile_drafter_feature_fusion_d2_kernel(tc, e, f_bytes, f_scale, w_bytes, w_sc
 
         for k in range(last + 1):
             window = windows.get(k, [])
-            share = G_COLUMNS if window else 0
+            share = G_COLUMNS[(window[0][0], window[0][2])] if window else 0
             mine = on_vector.get(k, 0)
             if k + 1 < TILES:
                 turn_f(k + 1)
@@ -404,7 +404,8 @@ def tile_drafter_feature_fusion_d2_kernel(tc, e, f_bytes, f_scale, w_bytes, w_sc
                 if PE_BLOCKS < 4:
                     lace_w(k + 2, PE_BLOCKS * B, WIDE)
             elif k + 2 < last:
-                lace_w(k + 2, 0, WIDE - share)
+                if share < WIDE:
+                    lace_w(k + 2, 0, WIDE - share)
                 if share:
                     lace_w_gpsimd(k + 2, WIDE - share, WIDE)
             if k + 2 < TILES:

@@ -352,14 +352,14 @@ def tile_drafter_feature_fusion_d2_kernel(tc, e, f_bytes, f_scale, w_bytes, w_sc
             return [(kind, c * WIDE, WIDE, m) for m in range(first, first + 4)]
 
         windows = {2: wides(0, 0, "a"), 4: wides(0, 4, "a"), 6: wides(0, 0),
-                   7: halves("a", 2), 8: halves("a", 3), 9: wides(0, 4), 10: halves("c", 2), 12: halves("c", 3),
+                   7: halves("a", 2), 8: halves("a", 3), 9: wides(0, 4), 11: halves("c", 2), 12: halves("c", 3),
                    13: halves("a", 4), 15: halves("c", 4), 17: halves("c", 5)[:3] + halves("a", 5)[:3] + halves("c", 5)[3:] + halves("a", 5)[3:]}
         last = len(UNITS)
         follow = {k: halves(UNITS[k][0], UNITS[k][1] // HALF) for k in range(10, last)}
         follow[5] = wides(0, 0)
         follow[6] = halves("a", 2)
         follow[7] = halves("a", 3)
-        on_vector = {11: 1, 14: 2, 16: 3}
+        on_vector = {10: 1, 14: 2, 16: 3}
 
         def f_share(m):
             return F0_ON_SCALAR if m == 0 else int(m >= F_LATE)
@@ -396,6 +396,9 @@ def tile_drafter_feature_fusion_d2_kernel(tc, e, f_bytes, f_scale, w_bytes, w_sc
                 quant_w(k)
             if mine:
                 widen_w(k + 1, range(mine), "vector")
+            if k == 1:
+                for product in windows[2][:1]:
+                    multiply(product)
             for product in follow.get(k, []):
                 multiply(product, UNITS[k][3])
             if k + 2 in PE_UNITS:
@@ -426,6 +429,14 @@ def tile_drafter_feature_fusion_d2_kernel(tc, e, f_bytes, f_scale, w_bytes, w_sc
             for product in windows.get(k + 1, []):
                 if product not in banks and k < 10:
                     multiply(product)
+            if k == 2:
+                for product in windows[4][:1]:
+                    multiply(product)
+            if k == 9:
+                for product in windows[11]:
+                    multiply(product)
+            if k == 3:
+                multiply(wides(0, 0)[0], [2, 3])
             if k == 4:
                 for product in wides(0, 0):
-                    multiply(product, [2, 3, 4])
+                    multiply(product, [4] if product in banks else [2, 3, 4])

@@ -18,38 +18,84 @@ ACT = mybir.ActivationFunctionType
 
 P = 128
 B = 128
-K_PASS = 512
+ROWS = 4
+K_PASS = P * ROWS
+QUADRANT = 32
 TILES = T // P
 PAIRS = TILES // 2
 PASSES = (E + D) // K_PASS
 E_PASSES = E // K_PASS
 F_BLOCKS = D // B
 W_BLOCKS = N // B
-HALF = 256
 WIDE = 512
-G_COLUMNS = {("a", WIDE): 384, ("a", HALF): 384, ("c", WIDE): 416, ("c", HALF): 448}
-F0_ON_SCALAR = 2
-SLOTS = 6
+HALF = WIDE // 2
 LAST_HALF = N // HALF - 1
-F_LATE = 3
-PE_UNITS = (2, 3, 5, 7)
+UNIT = ROWS * WIDE
+UNIT_BLOCKS = WIDE // B
+RUN = 4
+VISIT = 8
+GPSIMD_COLUMNS = 416
+F0_ON_SCALAR = 2
+F_SHARED_FROM = 3
 PE_BLOCKS = 2
+SLOTS = 6
 
 
-def a_unit(h):
-    return ("a", h * HALF, HALF, [0, 1])
+def wide_units(kind, passes):
+    return [(kind, 0, WIDE, [g]) for g in passes]
 
 
-def c_wide(c):
-    return [("c", c * WIDE, WIDE, [g]) for g in range(E_PASSES, PASSES)]
+def a_half(h):
+    return [("a", h * HALF, HALF, list(range(E_PASSES)))]
 
 
 def c_half(h):
     return [("c", h * HALF, HALF, [g, g + 1]) for g in range(E_PASSES, PASSES, 2)]
 
 
-UNITS = ([("a", 0, WIDE, [g]) for g in range(E_PASSES)] + c_wide(0) + [a_unit(2), a_unit(3)] + c_half(2) + c_half(3)
-         + [a_unit(4)] + c_half(4) + c_half(5) + [a_unit(5)])
+def wide_products(kind, first):
+    return [(kind, 0, WIDE, m) for m in range(first, first + RUN)]
+
+
+def half_products(kind, h):
+    return [(kind, h * HALF, HALF, 2 * pair) for pair in range(PAIRS)]
+
+
+UNITS = (wide_units("a", range(E_PASSES)) + wide_units("c", range(E_PASSES, PASSES)) + a_half(2) + a_half(3)
+         + c_half(2) + c_half(3) + a_half(4) + c_half(4) + c_half(LAST_HALF) + a_half(LAST_HALF))
+STEPS = len(UNITS)
+
+
+def ready_step(product):
+    kind, n0, width, m0 = product
+    last_tile = m0 + WIDE // width - 1
+    last_unit = max(k for k in range(STEPS) if UNITS[k][:2] == (kind, n0))
+    return max(last_unit, last_tile // 2 if kind == "a" else last_tile)
+
+
+def plan_runs():
+    second_wide_c = wide_products("c", RUN)
+    groups = [wide_products("a", 0), wide_products("a", RUN), wide_products("c", 0), half_products("a", 2), half_products("a", 3),
+              second_wide_c, half_products("c", 2), half_products("c", 3), half_products("a", 4), half_products("c", 4)]
+    runs = {}
+    step = 0
+    before = None
+    for group in groups:
+        step = max(step, ready_step(group[-1])) + 1 + (before == second_wide_c)
+        runs[step] = group
+        before = group
+    c, a = half_products("c", LAST_HALF), half_products("a", LAST_HALF)
+    runs[STEPS - 1] = c[:-1] + a[:-1] + c[-1:] + a[-1:]
+    return runs
+
+
+RUNS = plan_runs()
+PE_UNITS = [k + 2 for k in range(TILES - 2) if k not in RUNS]
+WIDEN_ON_VECTOR = {k: n + 1 for n, k in enumerate(k for k in range(TILES, STEPS) if k not in RUNS)}
+
+
+def f_passes_on_scalar(m):
+    return F0_ON_SCALAR if m == 0 else int(m >= F_SHARED_FROM)
 
 
 def tile_drafter_feature_fusion_d2_kernel(tc, e, f_bytes, f_scale, w_bytes, w_scale, trust, b, out):
@@ -58,6 +104,7 @@ def tile_drafter_feature_fusion_d2_kernel(tc, e, f_bytes, f_scale, w_bytes, w_sc
         once = ctx.enter_context(tc.tile_pool(name="once", bufs=1))
         work = ctx.enter_context(tc.tile_pool(name="work", bufs=3))
         psum = ctx.enter_context(tc.psum_pool(name="psum", bufs=1))
+
         w_scale_rows = once.tile([P, PASSES, W_BLOCKS], F32)
         nc.vector.memset(w_scale_rows[:], 0.0)
         ctx.enter_context(tc.manual_schedule())
@@ -68,17 +115,17 @@ def tile_drafter_feature_fusion_d2_kernel(tc, e, f_bytes, f_scale, w_bytes, w_sc
         nc.vector.memset(zero[:], 0.0)
         quadrants = once.tile([P, P], F32)
         nc.vector.memset(quadrants[:], 0.0)
-        for q in range(4):
-            nc.vector.memset(quadrants[32 * q:32 * (q + 1), 32 * q:32 * (q + 1)], 1.0)
+        for q in range(P // QUADRANT):
+            nc.vector.memset(quadrants[QUADRANT * q:QUADRANT * (q + 1), QUADRANT * q:QUADRANT * (q + 1)], 1.0)
 
         e_v = e.rearrange("(p m) k -> p m k", m=TILES)
         f_v = f_bytes.rearrange("(p m) k -> p m k", m=TILES)
         o_v = out.rearrange("(p m) n -> p m n", m=TILES)
-        w_v = w_bytes.rearrange("(g p t) n -> p g t n", p=P, t=4)
+        w_v = w_bytes.rearrange("(g p t) n -> p g t n", p=P, t=ROWS)
 
         f_scales = once.tile([P, TILES * F_BLOCKS], F32)
         nc.scalar.dma_start(out=f_scales[:], in_=f_scale.rearrange("(p m) j -> p (m j)", m=TILES))
-        nc.scalar.dma_start(out=w_scale_rows[0:P:32], in_=w_scale.rearrange("(g q) j -> q g j", q=4))
+        nc.scalar.dma_start(out=w_scale_rows[0:P:QUADRANT], in_=w_scale.rearrange("(g q) j -> q g j", q=P // QUADRANT))
 
         warm = once.tile([P, 1], F32)
         nc.scalar.activation(out=warm[:], in_=zero[:], func=ACT.Silu)
@@ -88,15 +135,20 @@ def tile_drafter_feature_fusion_d2_kernel(tc, e, f_bytes, f_scale, w_bytes, w_sc
         e_raw = {}
         f_raw = {}
 
+        def block_of(k, block):
+            kind, n0, width, gs = UNITS[k]
+            h, j = divmod(block, width // B)
+            return gs[h], n0 // B + j
+
         def load_w(k):
             kind, n0, width, gs = UNITS[k]
             first = PE_BLOCKS * B if k in PE_UNITS else 0
             if first:
-                w_blocks[k] = once.tile([P, PE_BLOCKS, 4, B], U8, name="w_blocks%d" % k)
+                w_blocks[k] = once.tile([P, PE_BLOCKS, ROWS, B], U8, name="w_blocks%d" % k)
                 for block in range(PE_BLOCKS):
-                    h, j = divmod(block, width // B)
-                    nc.sync.dma_start(out=w_blocks[k][:, block], in_=w_v[:, gs[h], :, n0 + j * B:n0 + (j + 1) * B])
-            raw = once.tile([P, 4, WIDE - first], U8, name="w_raw%d" % k)
+                    g, j = block_of(k, block)
+                    nc.sync.dma_start(out=w_blocks[k][:, block], in_=w_v[:, g, :, j * B:(j + 1) * B])
+            raw = once.tile([P, ROWS, WIDE - first], U8, name="w_raw%d" % k)
             for h, g in enumerate(gs):
                 c0, c1 = max(first, h * width), (h + 1) * width
                 if c0 < c1:
@@ -118,32 +170,25 @@ def tile_drafter_feature_fusion_d2_kernel(tc, e, f_bytes, f_scale, w_bytes, w_sc
         trusts = once.tile([P, TILES], BF16)
         load_f(0)
         load_w(0)
-        load_w(1)
-        load_e(0)
-        load_f(1)
-        load_w(2)
-        load_e(1)
-        load_f(2)
-        for m in range(3, TILES):
+        for m in range(1, TILES):
             load_w(m)
             if m - 1 < PAIRS:
                 load_e(m - 1)
             load_f(m)
-            if m == 3:
+            if m == PAIRS - 1:
                 nc.sync.dma_start(out=bias[:, 0:WIDE], in_=b[0:WIDE].partition_broadcast(P))
         nc.sync.dma_start(out=trusts[:], in_=trust.rearrange("(p m) o -> p (m o)", m=TILES))
         nc.sync.dma_start(out=bias[:, WIDE:N], in_=b[WIDE:N].partition_broadcast(P))
-        for k in range(TILES, len(UNITS)):
+        for k in range(TILES, STEPS):
             load_w(k)
 
-        free_banks = list(range(8))
+        free_banks = list(range(2 * RUN))
 
         def take_bank(shape, dtype=F32):
             number = free_banks.pop(0)
             return number, psum.tile(shape, dtype, name="bank%d" % number)
 
         ident16 = once.tile([P, P], BF16)
-
         w_scales = once.tile([P, PASSES, W_BLOCKS], F32)
 
         def spread_w_scale():
@@ -154,78 +199,70 @@ def tile_drafter_feature_fusion_d2_kernel(tc, e, f_bytes, f_scale, w_bytes, w_sc
 
         laced = {}
         wide = {}
-        w_mx = {}
         lent = {}
+        planes = {}
+        laced_bank = {}
+        w_mx = {}
         free_slots = list(range(SLOTS))
 
-        def block_of(k, block):
-            kind, n0, width, gs = UNITS[k]
-            return divmod(block, width // B)
-
-        def lace_w(k, first, stop):
-            tile = work.tile([P, (stop - first) * 4], U8, name="w_laced", bufs=4)
+        def lace(engine, tile, k, first, stop):
             raw, origin = w_raw[k]
-            src = raw[:, :, first - origin:stop - origin].rearrange("p t (c i) -> p c t i", i=8)
-            nc.vector.tensor_copy(out=tile[:].rearrange("p (c i t) -> p c t i", i=8, t=4), in_=src)
+            engine.tensor_copy(out=tile[:].rearrange("p (c i t) -> p c t i", i=VISIT, t=ROWS),
+                               in_=raw[:, :, first - origin:stop - origin].rearrange("p t (c i) -> p c t i", i=VISIT))
             laced.setdefault(k, []).append((tile, first, stop))
 
-        def lace_w_gpsimd(k, first, stop):
+        def lace_on_vector(k, first, stop):
+            lace(nc.vector, work.tile([P, (stop - first) * ROWS], U8, name="w_laced", bufs=4), k, first, stop)
+
+        def lace_on_gpsimd(k, first, stop):
             slot = lent[k] = free_slots.pop()
-            tile = work.tile([P, (stop - first) * 4], U8, align_bytes=64, name="w_laced_late", tag="slot%d" % slot, bufs=1)
-            nc.gpsimd.tensor_copy(out=tile[:].rearrange("p (c i t) -> p c t i", i=8, t=4),
-                                  in_=w_raw[k][0][:, :, first:stop].rearrange("p t (c i) -> p c t i", i=8))
-            laced.setdefault(k, []).append((tile, first, stop))
+            tile = work.tile([P, (stop - first) * ROWS], U8, align_bytes=64, name="w_laced_late", tag="slot%d" % slot, bufs=1)
+            lace(nc.gpsimd, tile, k, first, stop)
 
-        def widen_w(k, blocks, part="scalar"):
-            kind, n0, width, gs = UNITS[k]
+        def scaled(engine, dst, src, scale):
+            if engine == "vector":
+                nc.vector.tensor_scalar(out=dst, in0=src, scalar1=scale, scalar2=None, op0=MULT)
+            else:
+                nc.scalar.activation(out=dst, in_=src, func=ACT.Copy, scale=scale)
+
+        def widen_w(k, blocks, engine):
             if k not in wide:
                 slot = free_slots.pop(0)
-                wide[k] = (work.tile([P, 2048], BF16, align_bytes=64, name="w_wide", tag="slot%d" % slot, bufs=1), slot)
+                wide[k] = (work.tile([P, UNIT], BF16, align_bytes=64, name="w_wide", tag="slot%d" % slot, bufs=1), slot)
             for block in blocks:
-                h, j = block_of(k, block)
-                scale = w_scales[:, gs[h], n0 // B + j:n0 // B + j + 1]
-                for tile, first, stop in laced.get(k, []):
+                g, j = block_of(k, block)
+                for tile, first, stop in laced[k]:
                     c0, c1 = max(first, block * B), min(stop, (block + 1) * B)
                     if c0 < c1:
-                        src = tile[:, 4 * (c0 - first):4 * (c1 - first)].bitcast(FP8)
-                        dst = wide[k][0][:, 4 * c0:4 * c1]
-                        if part == "vector":
-                            nc.vector.tensor_scalar(out=dst, in0=src, scalar1=scale, scalar2=None, op0=MULT)
-                        else:
-                            nc.scalar.activation(out=dst, in_=src, func=ACT.Copy, scale=scale)
-            if part == "scalar" and k in lent:
+                        scaled(engine, wide[k][0][:, ROWS * c0:ROWS * c1],
+                               tile[:, ROWS * (c0 - first):ROWS * (c1 - first)].bitcast(FP8), w_scales[:, g, j:j + 1])
+            if engine == "scalar" and k in lent:
                 free_slots.append(lent[k])
 
-        planes = {}
-        in_bank = {}
-
         def widen_planes(k):
-            kind, n0, width, gs = UNITS[k]
-            planes[k] = work.tile([P, PE_BLOCKS, 4, B], BF16, name="w_planes", bufs=2)
+            planes[k] = work.tile([P, PE_BLOCKS, ROWS, B], BF16, name="w_planes", bufs=2)
             for block in range(PE_BLOCKS):
-                h, j = block_of(k, block)
-                nc.vector.tensor_scalar(out=planes[k][:, block].rearrange("p t c -> p (t c)"),
-                                        in0=w_blocks[k][:, block].rearrange("p t c -> p (t c)").bitcast(FP8),
-                                        scalar1=w_scales[:, gs[h], n0 // B + j:n0 // B + j + 1], scalar2=None, op0=MULT)
+                g, j = block_of(k, block)
+                scaled("vector", planes[k][:, block].rearrange("p t c -> p (t c)"),
+                       w_blocks[k][:, block].rearrange("p t c -> p (t c)").bitcast(FP8), w_scales[:, g, j:j + 1])
 
         def lace_planes(k):
-            in_bank[k] = [take_bank([P, 2, 4 * B], BF16) for half in range(PE_BLOCKS // 2)]
+            number, bank = laced_bank[k] = take_bank([P, PE_BLOCKS, ROWS * B], BF16)
             for block in range(PE_BLOCKS):
-                nc.tensor.matmul(in_bank[k][block // 2][1][:, block % 2], lhsT=ident16[:],
-                                 rhs=planes[k][:, block].rearrange("p t c -> p c t"), start=True, stop=True)
+                nc.tensor.matmul(bank[:, block], lhsT=ident16[:], rhs=planes[k][:, block].rearrange("p t c -> p c t"), start=True, stop=True)
 
         def copy_laced(k):
-            for half, (number, bank) in enumerate(in_bank[k]):
-                nc.scalar.copy(out=wide[k][0][:, 1024 * half:1024 * (half + 1)], in_=bank[:].rearrange("p b c -> p (b c)"))
-                free_banks.append(number)
+            number, bank = laced_bank[k]
+            nc.scalar.copy(out=wide[k][0][:, 0:PE_BLOCKS * ROWS * B], in_=bank[:].rearrange("p b c -> p (b c)"))
+            free_banks.append(number)
 
         def quantise(src, name, bufs):
-            codes = work.tile([P, 512], U32, align_bytes=256, name=name + "_codes", bufs=bufs)
-            scales = work.tile([P, 512], U8, align_bytes=256, name=name + "_scales", bufs=bufs)
+            codes = work.tile([P, UNIT // ROWS], U32, align_bytes=256, name=name + "_codes", bufs=bufs)
+            scales = work.tile([P, UNIT // ROWS], U8, align_bytes=256, name=name + "_scales", bufs=bufs)
             nc.vector.quantize_mx(out=codes[:].bitcast(FP8X4), scales=scales[:], in_=src[:])
             return codes, scales
 
-        def quant_w(k):
+        def quantise_w(k):
             kind, n0, width, gs = UNITS[k]
             codes, scales = quantise(wide[k][0], "w", 9)
             for h, g in enumerate(gs):
@@ -235,22 +272,22 @@ def tile_drafter_feature_fusion_d2_kernel(tc, e, f_bytes, f_scale, w_bytes, w_sc
         f_wide = {}
         turned = {}
         x_mx = {}
+        in_psum = []
+        words_a_pass = K_PASS // 2
 
-        def scale_f(m, on_scalar, part):
+        def scale_f(m, engine):
             if m not in f_wide:
                 f_wide[m] = work.tile([P, D], BF16, name="f_wide")
-            for j in (range(4 * on_scalar) if part == "scalar" else range(4 * on_scalar, F_BLOCKS)):
-                g, q = divmod(j, 4)
+            split = (K_PASS // B) * f_passes_on_scalar(m)
+            for j in (range(split) if engine == "scalar" else range(split, F_BLOCKS)):
                 src = f_raw[m][:, j * B:(j + 1) * B].bitcast(FP8)
                 scale = f_scales[:, m * F_BLOCKS + j:m * F_BLOCKS + j + 1]
-                if g < on_scalar:
-                    nc.scalar.activation(out=f_wide[m][:, j * B:(j + 1) * B], in_=src, func=ACT.Copy, scale=scale)
+                if engine == "scalar":
+                    scaled(engine, f_wide[m][:, j * B:(j + 1) * B], src, scale)
                 else:
-                    halves = f_wide[m][:, g * K_PASS:(g + 1) * K_PASS].rearrange("p (u r e) -> p r u e", u=2, e=2)
-                    nc.vector.tensor_scalar(out=halves[:, 32 * q:32 * q + 32], in0=src.rearrange("p (r u e) -> p r u e", u=2, e=2),
-                                            scalar1=scale, scalar2=None, op0=MULT)
-
-        in_psum = []
+                    g, q = divmod(j, K_PASS // B)
+                    by_parity = f_wide[m][:, g * K_PASS:(g + 1) * K_PASS].rearrange("p (u r e) -> p r u e", u=2, e=2)
+                    scaled(engine, by_parity[:, QUADRANT * q:QUADRANT * (q + 1)], src.rearrange("p (r u e) -> p r u e", u=2, e=2), scale)
 
         def turn(src, key, unsorted):
             words = src[:].bitcast(F32)
@@ -258,8 +295,9 @@ def tile_drafter_feature_fusion_d2_kernel(tc, e, f_bytes, f_scale, w_bytes, w_sc
                 number, bank = take_bank([P, 2, 2, P])
                 for h in range(2):
                     g = 2 * half + h
+                    first = words_a_pass * g
                     for u in range(2):
-                        cols = slice(256 * g + u, 256 * (g + 1), 2) if g < unsorted else slice(256 * g + P * u, 256 * g + P * (u + 1))
+                        cols = slice(first + u, first + words_a_pass, 2) if g < unsorted else slice(first + P * u, first + P * (u + 1))
                         nc.tensor.transpose(bank[:, h, u, :], words[:, cols], ident[:])
                 in_psum.append((key, half, number, bank))
 
@@ -267,44 +305,52 @@ def tile_drafter_feature_fusion_d2_kernel(tc, e, f_bytes, f_scale, w_bytes, w_sc
             while in_psum:
                 key, half, number, bank = in_psum.pop(0)
                 if half == 0:
-                    turned[key] = work.tile([P, 2048], BF16, align_bytes=64, name="turned", bufs=4)
-                dst = turned[key][:, 1024 * half:1024 * (half + 1)].bitcast(F32).rearrange("p (h r u) -> p h r u", h=2, u=2)
+                    turned[key] = work.tile([P, UNIT], BF16, align_bytes=64, name="turned", bufs=4)
+                dst = turned[key][:, UNIT // 2 * half:UNIT // 2 * (half + 1)].bitcast(F32).rearrange("p (h r u) -> p h r u", h=2, u=2)
                 nc.scalar.copy(out=dst, in_=bank[:].rearrange("p h u r -> p h r u"))
                 free_banks.append(number)
 
         def turn_e(pair):
-            turn(e_raw[pair], ("e", pair), 4)
+            turn(e_raw[pair], ("e", pair), 2 * E_PASSES)
 
         def turn_f(m):
-            turn(f_wide[m], ("f", m), f_share(m))
+            turn(f_wide[m], ("f", m), f_passes_on_scalar(m))
 
-        def quant_e(pair):
+        def quantise_e(pair):
             x_mx[("e", pair)] = quantise(turned[("e", pair)], "e", PAIRS)
 
-        def quant_f(m):
+        def quantise_f(m):
             x_mx[("f", m)] = quantise(turned[("f", m)], "f", TILES)
 
         banks = {}
+        done = {}
         first_sum = {}
         sums = []
 
-        def multiply(product, gs=None):
-            kind, n0, width, m0 = product
-            count = WIDE // width
-            whole = list(range(E_PASSES) if kind == "a" else range(E_PASSES, PASSES))
-            gs = gs or whole
-            if gs[0] == whole[0]:
-                banks[product] = take_bank([P, count, width])
-            for i in range(count):
-                m = m0 + i
-                x = x_mx[("e", m // 2)] if kind == "a" else x_mx[("f", m)]
-                x_first = 2 * (m % 2) if kind == "a" else 0
-                for g in gs:
-                    x_cols = slice((x_first + g - whole[0]) * P, (x_first + g - whole[0] + 1) * P)
-                    w = w_mx[(g, n0)]
-                    nc.tensor.matmul_mx(out=banks[product][1][:, i, :], lhsT=x[0][:, x_cols].bitcast(FP8X4), lhsT_scale=x[1][:, x_cols],
-                                        rhs=w[0].bitcast(FP8X4), rhs_scale=w[1],
-                                        start=(i, g) == (0, whole[0]), stop=(i, g) == (count - 1, whole[-1]))
+        def advance(products):
+            for product in products:
+                kind, n0, width, m0 = product
+                count = WIDE // width
+                whole = list(range(E_PASSES) if kind == "a" else range(E_PASSES, PASSES))
+                gs = [g for g in whole[done.get(product, 0):] if (g, n0) in w_mx]
+                if gs and product not in banks:
+                    banks[product] = take_bank([P, count, width])
+                done[product] = done.get(product, 0) + len(gs)
+                for i in range(count):
+                    m = m0 + i
+                    x = x_mx[("e", m // 2)] if kind == "a" else x_mx[("f", m)]
+                    x_first = E_PASSES * (m % 2) if kind == "a" else -E_PASSES
+                    for g in gs:
+                        x_cols = slice((x_first + g) * P, (x_first + g + 1) * P)
+                        w = w_mx[(g, n0)]
+                        nc.tensor.matmul_mx(out=banks[product][1][:, i, :], lhsT=x[0][:, x_cols].bitcast(FP8X4), lhsT_scale=x[1][:, x_cols],
+                                            rhs=w[0].bitcast(FP8X4), rhs_scale=w[1],
+                                            start=(i, g) == (0, whole[0]), stop=(i, g) == (count - 1, whole[-1]))
+
+        def pieces(product):
+            if product == RUNS[STEPS - 1][-1]:
+                return [slice(0, 1), slice(1, 2)]
+            return [slice(0, WIDE // product[2])]
 
         def empty(product):
             kind, n0, width, m0 = product
@@ -312,22 +358,23 @@ def tile_drafter_feature_fusion_d2_kernel(tc, e, f_bytes, f_scale, w_bytes, w_sc
             count = WIDE // width
             half, pair = n0 // HALF, m0 // 2
             opens = (kind == "a") == (half < LAST_HALF)
-            if opens and half < 2 and pair not in first_sum:
-                first_sum[pair] = work.tile([P, 2, WIDE], F32, name="first_wide", bufs=PAIRS)
-            if opens and half >= 2 and pair % 2 == 0:
-                first_sum[(half, pair // 2)] = once.tile([P, 2, 2, HALF], F32, name="first_half", tag="e_raw%d" % (2 * (half % 2) + pair // 2))
-            if half < 2:
-                part = first_sum[pair][:, m0 % 2:m0 % 2 + count, n0:n0 + width]
+            if n0 < WIDE:
+                if pair not in first_sum:
+                    first_sum[pair] = work.tile([P, 2, WIDE], F32, name="first_wide", bufs=PAIRS)
+                part = first_sum[pair][:, m0 % 2:m0 % 2 + count, :]
             else:
+                if opens and pair % 2 == 0:
+                    first_sum[(half, pair // 2)] = once.tile([P, 2, 2, HALF], F32, name="first_half",
+                                                             tag="e_raw%d" % (2 * (half % 2) + pair // 2))
                 part = first_sum[(half, pair // 2)][:, pair % 2]
             if opens:
                 dst = part
             else:
-                dst = work.tile([P, count, width], F32, name="z", bufs=9)[:]
+                dst = work.tile([P, count, width], F32, name="z", bufs=2 * RUN + 1)[:]
                 sums.append((dst, product))
             if kind == "a":
                 other = bias[:, n0:n0 + width].unsqueeze(1).to_broadcast([P, count, width]) if opens else part
-                for tiles in ([slice(0, 1), slice(1, 2)] if (half, pair) == (LAST_HALF, PAIRS - 1) else [slice(0, count)]):
+                for tiles in pieces(product):
                     nc.vector.tensor_tensor(out=dst[:, tiles], in0=bank[:, tiles], in1=other[:, tiles], op=ADD)
             else:
                 for i in range(count):
@@ -337,106 +384,84 @@ def tile_drafter_feature_fusion_d2_kernel(tc, e, f_bytes, f_scale, w_bytes, w_sc
             free_banks.append(number)
 
         def finish():
-            z, (kind, n0, width, m0) = sums.pop(0)
-            count = WIDE // width
-            res = work.tile([P, count, width], F32, name="res", bufs=6)
-            very_last = (kind, n0 // HALF, m0 // 2) == ("a", LAST_HALF, PAIRS - 1)
-            for tiles in ([slice(0, 1), slice(1, 2)] if very_last else [slice(0, count)]):
+            z, product = sums.pop(0)
+            kind, n0, width, m0 = product
+            res = work.tile([P, WIDE // width, width], F32, name="res", bufs=6)
+            for tiles in pieces(product):
                 nc.scalar.activation(out=res[:, tiles], in_=z[:, tiles], func=ACT.Silu)
                 nc.sync.dma_start(out=o_v[:, m0 + tiles.start:m0 + tiles.stop, n0:n0 + width], in_=res[:, tiles])
 
-        def halves(kind, h):
-            return [(kind, h * HALF, HALF, 2 * pair) for pair in range(PAIRS)]
+        def groups_after(k):
+            return [RUNS[step] for step in sorted(RUNS) if step > k]
 
-        def wides(c, first, kind="c"):
-            return [(kind, c * WIDE, WIDE, m) for m in range(first, first + 4)]
+        def behind_quantise(k):
+            kind, n0, width, gs = UNITS[k]
+            if k == E_PASSES - 1:
+                return groups_after(k)[0][:1]
+            if k == PASSES - 1:
+                return wide_products("c", 0)
+            if width == HALF and UNITS[k] not in c_half(2):
+                return half_products(kind, n0 // HALF)
+            return []
 
-        windows = {2: wides(0, 0, "a"), 4: wides(0, 4, "a"), 6: wides(0, 0),
-                   7: halves("a", 2), 8: halves("a", 3), 9: wides(0, 4), 11: halves("c", 2), 12: halves("c", 3),
-                   13: halves("a", 4), 15: halves("c", 4), 17: halves("c", 5)[:3] + halves("a", 5)[:3] + halves("c", 5)[3:] + halves("a", 5)[3:]}
-        last = len(UNITS)
-        follow = {k: halves(UNITS[k][0], UNITS[k][1] // HALF) for k in range(10, last)}
-        follow[5] = wides(0, 0)
-        follow[6] = halves("a", 2)
-        follow[7] = halves("a", 3)
-        on_vector = {10: 1, 14: 2, 16: 3}
-
-        def f_share(m):
-            return F0_ON_SCALAR if m == 0 else int(m >= F_LATE)
-
-        scale_f(0, F0_ON_SCALAR, "scalar")
-        scale_f(0, F0_ON_SCALAR, "vector")
+        scale_f(0, "scalar")
+        scale_f(0, "vector")
         spread_w_scale()
-        lace_w(0, 0, HALF)
-        widen_w(0, range(2))
-        lace_w(0, HALF, WIDE)
+        lace_on_vector(0, 0, HALF)
+        widen_w(0, range(UNIT_BLOCKS // 2), "scalar")
+        lace_on_vector(0, HALF, WIDE)
         turn_f(0)
         copy_turned()
-        lace_w(1, 0, WIDE)
+        lace_on_vector(1, 0, WIDE)
         nc.vector.tensor_copy(out=ident16[:], in_=ident[:])
-        widen_w(0, range(2, 4), "vector")
-        scale_f(1, 0, "vector")
+        widen_w(0, range(UNIT_BLOCKS // 2, UNIT_BLOCKS), "vector")
+        scale_f(1, "vector")
         turn_e(0)
         copy_turned()
 
-        for k in range(last + 1):
-            window = windows.get(k, [])
-            share = G_COLUMNS[(window[0][0], window[0][2])] if window else 0
-            mine = on_vector.get(k, 0)
+        for k in range(STEPS):
+            run = RUNS.get(k, [])
+            on_vector = WIDEN_ON_VECTOR.get(k, 0)
+            last = k == STEPS - 1
             if k + 1 < TILES:
                 turn_f(k + 1)
-            if k + 1 < last:
-                widen_w(k + 1, range(mine, 4))
+            if not last:
+                widen_w(k + 1, range(on_vector, UNIT_BLOCKS), "scalar")
             if k + 1 in PE_UNITS:
                 copy_laced(k + 1)
             copy_turned()
-            for n in range(len(sums) if k == last - 1 else min(len(sums), 2 if window else 1)):
+            for n in range(len(sums) if last else min(len(sums), 2 if run else 1)):
                 finish()
-            if k < last:
-                quant_w(k)
-            if mine:
-                widen_w(k + 1, range(mine), "vector")
-            if k == 1:
-                for product in windows[2][:1]:
-                    multiply(product)
-            for product in follow.get(k, []):
-                multiply(product, UNITS[k][3])
+            quantise_w(k)
+            if on_vector:
+                widen_w(k + 1, range(on_vector), "vector")
+            advance(behind_quantise(k))
             if k + 2 in PE_UNITS:
                 widen_planes(k + 2)
                 lace_planes(k + 2)
-                if PE_BLOCKS < 4:
-                    lace_w(k + 2, PE_BLOCKS * B, WIDE)
-            elif k + 2 < last:
-                if share < WIDE:
-                    lace_w(k + 2, 0, WIDE - share)
+                lace_on_vector(k + 2, PE_BLOCKS * B, WIDE)
+            elif k + 2 < STEPS:
+                share = GPSIMD_COLUMNS if run else 0
+                lace_on_vector(k + 2, 0, WIDE - share)
                 if share:
-                    lace_w_gpsimd(k + 2, WIDE - share, WIDE)
+                    lace_on_gpsimd(k + 2, WIDE - share, WIDE)
             if k + 2 < TILES:
-                scale_f(k + 2, f_share(k + 2), "scalar")
-            for product in window:
+                scale_f(k + 2, "scalar")
+            for product in run:
                 empty(product)
-                if k >= last - 1 and product[0] == "a":
+                if last and product[0] == "a":
                     finish()
             if k < PAIRS:
-                quant_e(k)
+                quantise_e(k)
             if k + 2 < TILES:
-                scale_f(k + 2, f_share(k + 2), "vector")
+                scale_f(k + 2, "vector")
             if k < TILES:
-                quant_f(k)
+                quantise_f(k)
             if k + 1 < PAIRS:
                 turn_e(k + 1)
             copy_turned()
-            for product in windows.get(k + 1, []):
-                if product not in banks and k < 10:
-                    multiply(product)
-            if k == 2:
-                for product in windows[4][:1]:
-                    multiply(product)
-            if k == 9:
-                for product in windows[11]:
-                    multiply(product)
-            if k == 3:
-                multiply(wides(0, 0)[0], [2, 3])
-            if k == 4:
-                for product in wides(0, 0):
-                    multiply(product, [4] if product in banks else [2, 3, 4])
+            if 0 < k < STEPS - 1:
+                ahead = groups_after(k)
+                advance(ahead[0][:1] if k == PAIRS - 2 else ahead[0])
+                if k == PAIRS - 1:
+                    advance(ahead[1][:1])

@@ -35,9 +35,8 @@ UNIT_BLOCKS = WIDE // B
 RUN = 4
 VISIT = 8
 GPSIMD_COLUMNS = 416
-F0_ON_SCALAR = 2
-F_SHARED_FROM = 3
-PE_BLOCKS = 2
+F_ON_SCALAR = [1, 0] + [2] * (TILES - 2)
+LACE = 4
 SLOTS = 6
 
 
@@ -90,12 +89,12 @@ def plan_runs():
 
 
 RUNS = plan_runs()
-PE_UNITS = [k + 2 for k in range(TILES - 2) if k not in RUNS]
-WIDEN_ON_VECTOR = {k: n + 1 for n, k in enumerate(k for k in range(TILES, STEPS) if k not in RUNS)}
+PLAIN_UNITS = [k for k in range(STEPS) if k - 2 not in RUNS]
+WIDEN_ON_VECTOR = {k: 1 for k in range(TILES, STEPS) if k not in RUNS}
 
 
 def f_passes_on_scalar(m):
-    return F0_ON_SCALAR if m == 0 else int(m >= F_SHARED_FROM)
+    return F_ON_SCALAR[m]
 
 
 def tile_drafter_feature_fusion_d2_kernel(tc, e, f_bytes, f_scale, w_bytes, w_scale, trust, b, out):
@@ -131,7 +130,6 @@ def tile_drafter_feature_fusion_d2_kernel(tc, e, f_bytes, f_scale, w_bytes, w_sc
         nc.scalar.activation(out=warm[:], in_=zero[:], func=ACT.Silu)
 
         w_raw = {}
-        w_blocks = {}
         e_raw = {}
         f_raw = {}
 
@@ -142,18 +140,10 @@ def tile_drafter_feature_fusion_d2_kernel(tc, e, f_bytes, f_scale, w_bytes, w_sc
 
         def load_w(k):
             kind, n0, width, gs = UNITS[k]
-            first = PE_BLOCKS * B if k in PE_UNITS else 0
-            if first:
-                w_blocks[k] = once.tile([P, PE_BLOCKS, ROWS, B], U8, name="w_blocks%d" % k)
-                for block in range(PE_BLOCKS):
-                    g, j = block_of(k, block)
-                    nc.sync.dma_start(out=w_blocks[k][:, block], in_=w_v[:, g, :, j * B:(j + 1) * B])
-            raw = once.tile([P, ROWS, WIDE - first], U8, name="w_raw%d" % k)
+            raw = once.tile([P, ROWS, WIDE], U8, name="w_raw%d" % k)
             for h, g in enumerate(gs):
-                c0, c1 = max(first, h * width), (h + 1) * width
-                if c0 < c1:
-                    nc.sync.dma_start(out=raw[:, :, c0 - first:c1 - first], in_=w_v[:, g, :, n0 + c0 - h * width:n0 + width])
-            w_raw[k] = (raw, first)
+                nc.sync.dma_start(out=raw[:, :, h * width:(h + 1) * width], in_=w_v[:, g, :, n0:n0 + width])
+            w_raw[k] = raw
 
         def load_e(pair):
             raw = once.tile([P, 2 * E], BF16, name="e_raw%d" % pair)
@@ -188,7 +178,6 @@ def tile_drafter_feature_fusion_d2_kernel(tc, e, f_bytes, f_scale, w_bytes, w_sc
             number = free_banks.pop(0)
             return number, psum.tile(shape, dtype, name="bank%d" % number)
 
-        ident16 = once.tile([P, P], BF16)
         w_scales = once.tile([P, PASSES, W_BLOCKS], F32)
 
         def spread_w_scale():
@@ -201,14 +190,13 @@ def tile_drafter_feature_fusion_d2_kernel(tc, e, f_bytes, f_scale, w_bytes, w_sc
         wide = {}
         lent = {}
         planes = {}
-        laced_bank = {}
         w_mx = {}
         free_slots = list(range(SLOTS))
 
         def lace(engine, tile, k, first, stop):
-            raw, origin = w_raw[k]
+            raw = w_raw[k]
             engine.tensor_copy(out=tile[:].rearrange("p (c i t) -> p c t i", i=VISIT, t=ROWS),
-                               in_=raw[:, :, first - origin:stop - origin].rearrange("p t (c i) -> p c t i", i=VISIT))
+                               in_=raw[:, :, first:stop].rearrange("p t (c i) -> p c t i", i=VISIT))
             laced.setdefault(k, []).append((tile, first, stop))
 
         def lace_on_vector(k, first, stop):
@@ -225,10 +213,13 @@ def tile_drafter_feature_fusion_d2_kernel(tc, e, f_bytes, f_scale, w_bytes, w_sc
             else:
                 nc.scalar.activation(out=dst, in_=src, func=ACT.Copy, scale=scale)
 
-        def widen_w(k, blocks, engine):
+        def take_wide(k):
             if k not in wide:
                 slot = free_slots.pop(0)
                 wide[k] = (work.tile([P, UNIT], BF16, align_bytes=64, name="w_wide", tag="slot%d" % slot, bufs=1), slot)
+
+        def widen_w(k, blocks, engine):
+            take_wide(k)
             for block in blocks:
                 g, j = block_of(k, block)
                 for tile, first, stop in laced[k]:
@@ -240,21 +231,16 @@ def tile_drafter_feature_fusion_d2_kernel(tc, e, f_bytes, f_scale, w_bytes, w_sc
                 free_slots.append(lent[k])
 
         def widen_planes(k):
-            planes[k] = work.tile([P, PE_BLOCKS, ROWS, B], BF16, name="w_planes", bufs=2)
-            for block in range(PE_BLOCKS):
-                g, j = block_of(k, block)
-                scaled("vector", planes[k][:, block].rearrange("p t c -> p (t c)"),
-                       w_blocks[k][:, block].rearrange("p t c -> p (t c)").bitcast(FP8), w_scales[:, g, j:j + 1])
+            planes[k] = work.tile([P, ROWS, WIDE], BF16, name="w_planes")
+            nc.scalar.copy(out=planes[k][:].rearrange("p t c -> p (t c)"), in_=w_raw[k][:].rearrange("p t c -> p (t c)").bitcast(FP8))
 
         def lace_planes(k):
-            number, bank = laced_bank[k] = take_bank([P, PE_BLOCKS, ROWS * B], BF16)
-            for block in range(PE_BLOCKS):
-                nc.tensor.matmul(bank[:, block], lhsT=ident16[:], rhs=planes[k][:, block].rearrange("p t c -> p c t"), start=True, stop=True)
-
-        def copy_laced(k):
-            number, bank = laced_bank[k]
-            nc.scalar.copy(out=wide[k][0][:, 0:PE_BLOCKS * ROWS * B], in_=bank[:].rearrange("p b c -> p (b c)"))
-            free_banks.append(number)
+            take_wide(k)
+            for block in range(UNIT_BLOCKS):
+                g, j = block_of(k, block)
+                dst = wide[k][0][:, ROWS * B * block:ROWS * B * (block + 1)].rearrange("p (c i t) -> p c t i", i=LACE, t=ROWS)
+                src = planes[k][:, :, B * block:B * (block + 1)].rearrange("p t (c i) -> p c t i", i=LACE)
+                scaled("vector", dst, src, w_scales[:, g, j:j + 1])
 
         def quantise(src, name, bufs):
             codes = work.tile([P, UNIT // ROWS], U32, align_bytes=256, name=name + "_codes", bufs=bufs)
@@ -279,7 +265,7 @@ def tile_drafter_feature_fusion_d2_kernel(tc, e, f_bytes, f_scale, w_bytes, w_sc
             if m not in f_wide:
                 f_wide[m] = work.tile([P, D], BF16, name="f_wide")
             split = (K_PASS // B) * f_passes_on_scalar(m)
-            for j in (range(split) if engine == "scalar" else range(split, F_BLOCKS)):
+            for j in (range(split) if engine == "scalar" else reversed(range(split, F_BLOCKS))):
                 src = f_raw[m][:, j * B:(j + 1) * B].bitcast(FP8)
                 scale = f_scales[:, m * F_BLOCKS + j:m * F_BLOCKS + j + 1]
                 if engine == "scalar":
@@ -404,17 +390,14 @@ def tile_drafter_feature_fusion_d2_kernel(tc, e, f_bytes, f_scale, w_bytes, w_sc
                 return half_products(kind, n0 // HALF)
             return []
 
+        spread_w_scale()
         scale_f(0, "scalar")
         scale_f(0, "vector")
-        spread_w_scale()
-        lace_on_vector(0, 0, HALF)
-        widen_w(0, range(UNIT_BLOCKS // 2), "scalar")
-        lace_on_vector(0, HALF, WIDE)
+        widen_planes(0)
         turn_f(0)
         copy_turned()
-        lace_on_vector(1, 0, WIDE)
-        nc.vector.tensor_copy(out=ident16[:], in_=ident[:])
-        widen_w(0, range(UNIT_BLOCKS // 2, UNIT_BLOCKS), "vector")
+        lace_planes(0)
+        widen_planes(1)
         scale_f(1, "vector")
         turn_e(0)
         copy_turned()
@@ -425,26 +408,22 @@ def tile_drafter_feature_fusion_d2_kernel(tc, e, f_bytes, f_scale, w_bytes, w_sc
             last = k == STEPS - 1
             if k + 1 < TILES:
                 turn_f(k + 1)
-            if not last:
+            if k + 1 in PLAIN_UNITS:
+                lace_planes(k + 1)
+            elif not last:
                 widen_w(k + 1, range(on_vector, UNIT_BLOCKS), "scalar")
-            if k + 1 in PE_UNITS:
-                copy_laced(k + 1)
             copy_turned()
+            if k + 2 in PLAIN_UNITS:
+                widen_planes(k + 2)
             for n in range(len(sums) if last else min(len(sums), 2 if run else 1)):
                 finish()
             quantise_w(k)
             if on_vector:
                 widen_w(k + 1, range(on_vector), "vector")
             advance(behind_quantise(k))
-            if k + 2 in PE_UNITS:
-                widen_planes(k + 2)
-                lace_planes(k + 2)
-                lace_on_vector(k + 2, PE_BLOCKS * B, WIDE)
-            elif k + 2 < STEPS:
-                share = GPSIMD_COLUMNS if run else 0
-                lace_on_vector(k + 2, 0, WIDE - share)
-                if share:
-                    lace_on_gpsimd(k + 2, WIDE - share, WIDE)
+            if run and k + 2 < STEPS:
+                lace_on_vector(k + 2, 0, WIDE - GPSIMD_COLUMNS)
+                lace_on_gpsimd(k + 2, WIDE - GPSIMD_COLUMNS, WIDE)
             if k + 2 < TILES:
                 scale_f(k + 2, "scalar")
             for product in run:

@@ -33,11 +33,10 @@ LAST_HALF = N // HALF - 1
 UNIT = ROWS * WIDE
 UNIT_BLOCKS = WIDE // B
 RUN = 4
-VISIT = 8
-GPSIMD_COLUMNS = 416
-F_ON_SCALAR = [1, 0] + [2] * (TILES - 2)
+GPSIMD_BLOCKS = 3
+SILUS = 3
+F_ON_SCALAR = [0, 0, 0, 0, 2, 3, 3, 3]
 LACE = 4
-SLOTS = 6
 
 
 def wide_units(kind, passes):
@@ -60,37 +59,29 @@ def half_products(kind, h):
     return [(kind, h * HALF, HALF, 2 * pair) for pair in range(PAIRS)]
 
 
-UNITS = (wide_units("a", range(E_PASSES)) + wide_units("c", range(E_PASSES, PASSES)) + a_half(2) + a_half(3)
-         + c_half(2) + c_half(3) + a_half(4) + c_half(4) + c_half(LAST_HALF) + a_half(LAST_HALF))
+HALVES = N // HALF
+UNITS = (wide_units("a", range(E_PASSES)) + [u for h in range(2, HALVES) for u in a_half(h)]
+         + [u for h in range(HALVES) for u in c_half(h)])
 STEPS = len(UNITS)
-
-
-def ready_step(product):
-    kind, n0, width, m0 = product
-    last_tile = m0 + WIDE // width - 1
-    last_unit = max(k for k in range(STEPS) if UNITS[k][:2] == (kind, n0))
-    return max(last_unit, last_tile // 2 if kind == "a" else last_tile)
+A_STEPS = HALVES
 
 
 def plan_runs():
-    second_wide_c = wide_products("c", RUN)
-    groups = [wide_products("a", 0), wide_products("a", RUN), wide_products("c", 0), half_products("a", 2), half_products("a", 3),
-              second_wide_c, half_products("c", 2), half_products("c", 3), half_products("a", 4), half_products("c", 4)]
-    runs = {}
-    step = 0
-    before = None
-    for group in groups:
-        step = max(step, ready_step(group[-1])) + 1 + (before == second_wide_c)
-        runs[step] = group
-        before = group
-    c, a = half_products("c", LAST_HALF), half_products("a", LAST_HALF)
-    runs[STEPS - 1] = c[:-1] + a[:-1] + c[-1:] + a[-1:]
+    wide = wide_products("a", 0) + wide_products("a", RUN)
+    second = half_products("a", 2)
+    groups = [wide[:4], wide[4:6] + second[:2], wide[6:] + second[2:]] + [half_products("a", h) for h in range(3, HALVES)]
+    runs = {E_PASSES + n: group for n, group in enumerate(groups)}
+    for h in range(HALVES - 2):
+        runs[A_STEPS + 2 * h + 2] = half_products("c", h)
+    runs[STEPS - 1] = half_products("c", HALVES - 2) + half_products("c", HALVES - 1)
     return runs
 
 
 RUNS = plan_runs()
-PLAIN_UNITS = [k for k in range(STEPS) if k - 2 not in RUNS]
-WIDEN_ON_VECTOR = {k: 1 for k in range(TILES, STEPS) if k not in RUNS}
+
+
+def vector_blocks(k):
+    return UNIT_BLOCKS - (GPSIMD_BLOCKS if k - 2 in RUNS else 0)
 
 
 def f_passes_on_scalar(m):
@@ -186,61 +177,30 @@ def tile_drafter_feature_fusion_d2_kernel(tc, e, f_bytes, f_scale, w_bytes, w_sc
             nc.scalar.copy(out=w_scales[:].rearrange("p g j -> p (g j)"), in_=bank[:])
             free_banks.append(number)
 
-        laced = {}
-        wide = {}
-        lent = {}
         planes = {}
+        wide = {}
         w_mx = {}
-        free_slots = list(range(SLOTS))
-
-        def lace(engine, tile, k, first, stop):
-            raw = w_raw[k]
-            engine.tensor_copy(out=tile[:].rearrange("p (c i t) -> p c t i", i=VISIT, t=ROWS),
-                               in_=raw[:, :, first:stop].rearrange("p t (c i) -> p c t i", i=VISIT))
-            laced.setdefault(k, []).append((tile, first, stop))
-
-        def lace_on_vector(k, first, stop):
-            lace(nc.vector, work.tile([P, (stop - first) * ROWS], U8, name="w_laced", bufs=4), k, first, stop)
-
-        def lace_on_gpsimd(k, first, stop):
-            slot = lent[k] = free_slots.pop()
-            tile = work.tile([P, (stop - first) * ROWS], U8, align_bytes=64, name="w_laced_late", tag="slot%d" % slot, bufs=1)
-            lace(nc.gpsimd, tile, k, first, stop)
 
         def scaled(engine, dst, src, scale):
             if engine == "vector":
                 nc.vector.tensor_scalar(out=dst, in0=src, scalar1=scale, scalar2=None, op0=MULT)
+            elif engine == "gpsimd":
+                nc.gpsimd.tensor_scalar(out=dst, in0=src, scalar1=scale, scalar2=0.0, op0=MULT, op1=ADD)
             else:
                 nc.scalar.activation(out=dst, in_=src, func=ACT.Copy, scale=scale)
 
-        def take_wide(k):
-            if k not in wide:
-                slot = free_slots.pop(0)
-                wide[k] = (work.tile([P, UNIT], BF16, align_bytes=64, name="w_wide", tag="slot%d" % slot, bufs=1), slot)
-
-        def widen_w(k, blocks, engine):
-            take_wide(k)
-            for block in blocks:
-                g, j = block_of(k, block)
-                for tile, first, stop in laced[k]:
-                    c0, c1 = max(first, block * B), min(stop, (block + 1) * B)
-                    if c0 < c1:
-                        scaled(engine, wide[k][0][:, ROWS * c0:ROWS * c1],
-                               tile[:, ROWS * (c0 - first):ROWS * (c1 - first)].bitcast(FP8), w_scales[:, g, j:j + 1])
-            if engine == "scalar" and k in lent:
-                free_slots.append(lent[k])
-
-        def widen_planes(k):
-            planes[k] = work.tile([P, ROWS, WIDE], BF16, name="w_planes")
+        def widen_w(k):
+            planes[k] = work.tile([P, ROWS, WIDE], BF16, name="w_planes", bufs=3)
             nc.scalar.copy(out=planes[k][:].rearrange("p t c -> p (t c)"), in_=w_raw[k][:].rearrange("p t c -> p (t c)").bitcast(FP8))
 
-        def lace_planes(k):
-            take_wide(k)
-            for block in range(UNIT_BLOCKS):
+        def lace(engine, k, blocks):
+            if k not in wide:
+                wide[k] = work.tile([P, UNIT], BF16, align_bytes=64, name="w_wide", bufs=2)
+            for block in blocks:
                 g, j = block_of(k, block)
-                dst = wide[k][0][:, ROWS * B * block:ROWS * B * (block + 1)].rearrange("p (c i t) -> p c t i", i=LACE, t=ROWS)
+                dst = wide[k][:, ROWS * B * block:ROWS * B * (block + 1)].rearrange("p (c i t) -> p c t i", i=LACE, t=ROWS)
                 src = planes[k][:, :, B * block:B * (block + 1)].rearrange("p t (c i) -> p c t i", i=LACE)
-                scaled("vector", dst, src, w_scales[:, g, j:j + 1])
+                scaled(engine, dst, src, w_scales[:, g, j:j + 1])
 
         def quantise(src, name, bufs):
             codes = work.tile([P, UNIT // ROWS], U32, align_bytes=256, name=name + "_codes", bufs=bufs)
@@ -250,10 +210,9 @@ def tile_drafter_feature_fusion_d2_kernel(tc, e, f_bytes, f_scale, w_bytes, w_sc
 
         def quantise_w(k):
             kind, n0, width, gs = UNITS[k]
-            codes, scales = quantise(wide[k][0], "w", 9)
+            codes, scales = quantise(wide[k], "w", 5)
             for h, g in enumerate(gs):
                 w_mx[(g, n0)] = (codes[:, h * width:(h + 1) * width], scales[:, h * width:(h + 1) * width])
-            free_slots.append(wide[k][1])
 
         f_wide = {}
         turned = {}
@@ -310,7 +269,6 @@ def tile_drafter_feature_fusion_d2_kernel(tc, e, f_bytes, f_scale, w_bytes, w_sc
 
         banks = {}
         done = {}
-        first_sum = {}
         sums = []
 
         def advance(products):
@@ -318,55 +276,42 @@ def tile_drafter_feature_fusion_d2_kernel(tc, e, f_bytes, f_scale, w_bytes, w_sc
                 kind, n0, width, m0 = product
                 count = WIDE // width
                 whole = list(range(E_PASSES) if kind == "a" else range(E_PASSES, PASSES))
-                gs = [g for g in whole[done.get(product, 0):] if (g, n0) in w_mx]
-                if gs and product not in banks:
-                    banks[product] = take_bank([P, count, width])
-                done[product] = done.get(product, 0) + len(gs)
+                made = done.setdefault(product, [])
                 for i in range(count):
                     m = m0 + i
-                    x = x_mx[("e", m // 2)] if kind == "a" else x_mx[("f", m)]
+                    key = ("e", m // 2) if kind == "a" else ("f", m)
                     x_first = E_PASSES * (m % 2) if kind == "a" else -E_PASSES
-                    for g in gs:
-                        x_cols = slice((x_first + g) * P, (x_first + g + 1) * P)
-                        w = w_mx[(g, n0)]
-                        nc.tensor.matmul_mx(out=banks[product][1][:, i, :], lhsT=x[0][:, x_cols].bitcast(FP8X4), lhsT_scale=x[1][:, x_cols],
-                                            rhs=w[0].bitcast(FP8X4), rhs_scale=w[1],
-                                            start=(i, g) == (0, whole[0]), stop=(i, g) == (count - 1, whole[-1]))
+                    for g in whole:
+                        if key in x_mx and (g, n0) in w_mx and (i, g) not in made:
+                            if product not in banks:
+                                banks[product] = take_bank([P, count, width])
+                            made.append((i, g))
+                            x_cols = slice((x_first + g) * P, (x_first + g + 1) * P)
+                            x, w = x_mx[key], w_mx[(g, n0)]
+                            nc.tensor.matmul_mx(out=banks[product][1][:, i, :], lhsT=x[0][:, x_cols].bitcast(FP8X4), lhsT_scale=x[1][:, x_cols],
+                                                rhs=w[0].bitcast(FP8X4), rhs_scale=w[1],
+                                                start=len(made) == 1, stop=len(made) == count * len(whole))
 
         def pieces(product):
             if product == RUNS[STEPS - 1][-1]:
                 return [slice(0, 1), slice(1, 2)]
             return [slice(0, WIDE // product[2])]
 
+        first_sum = once.tile([P, TILES, N], F32)
+
         def empty(product):
             kind, n0, width, m0 = product
             number, bank = banks[product]
             count = WIDE // width
-            half, pair = n0 // HALF, m0 // 2
-            opens = (kind == "a") == (half < LAST_HALF)
-            if n0 < WIDE:
-                if pair not in first_sum:
-                    first_sum[pair] = work.tile([P, 2, WIDE], F32, name="first_wide", bufs=PAIRS)
-                part = first_sum[pair][:, m0 % 2:m0 % 2 + count, :]
-            else:
-                if opens and pair % 2 == 0:
-                    first_sum[(half, pair // 2)] = once.tile([P, 2, 2, HALF], F32, name="first_half",
-                                                             tag="e_raw%d" % (2 * (half % 2) + pair // 2))
-                part = first_sum[(half, pair // 2)][:, pair % 2]
-            if opens:
-                dst = part
-            else:
-                dst = work.tile([P, count, width], F32, name="z", bufs=2 * RUN + 1)[:]
-                sums.append((dst, product))
+            part = first_sum[:, m0:m0 + count, n0:n0 + width]
             if kind == "a":
-                other = bias[:, n0:n0 + width].unsqueeze(1).to_broadcast([P, count, width]) if opens else part
-                for tiles in pieces(product):
-                    nc.vector.tensor_tensor(out=dst[:, tiles], in0=bank[:, tiles], in1=other[:, tiles], op=ADD)
+                nc.vector.tensor_tensor(out=part, in0=bank[:], in1=bias[:, n0:n0 + width].unsqueeze(1).to_broadcast([P, count, width]), op=ADD)
             else:
+                z = work.tile([P, count, width], F32, name="z", bufs=6)
+                sums.append((z[:], product))
                 for i in range(count):
-                    other = bias[:, n0:n0 + width] if opens else part[:, i, :]
-                    nc.vector.scalar_tensor_tensor(out=dst[:, i, :], in0=bank[:, i, :], scalar=trusts[:, m0 + i:m0 + i + 1],
-                                                   in1=other, op0=MULT, op1=ADD)
+                    nc.vector.scalar_tensor_tensor(out=z[:, i, :], in0=bank[:, i, :], scalar=trusts[:, m0 + i:m0 + i + 1],
+                                                   in1=part[:, i, :], op0=MULT, op1=ADD)
             free_banks.append(number)
 
         def finish():
@@ -377,58 +322,55 @@ def tile_drafter_feature_fusion_d2_kernel(tc, e, f_bytes, f_scale, w_bytes, w_sc
                 nc.scalar.activation(out=res[:, tiles], in_=z[:, tiles], func=ACT.Silu)
                 nc.sync.dma_start(out=o_v[:, m0 + tiles.start:m0 + tiles.stop, n0:n0 + width], in_=res[:, tiles])
 
-        def groups_after(k):
-            return [RUNS[step] for step in sorted(RUNS) if step > k]
+        def waiting(k):
+            return [product for step in sorted(RUNS) if step > k for product in RUNS[step]]
 
-        def behind_quantise(k):
-            kind, n0, width, gs = UNITS[k]
-            if k == E_PASSES - 1:
-                return groups_after(k)[0][:1]
-            if k == PASSES - 1:
-                return wide_products("c", 0)
-            if width == HALF and UNITS[k] not in c_half(2):
-                return half_products(kind, n0 // HALF)
-            return []
+        def ahead(k, spare):
+            for product in waiting(k):
+                if product not in banks and len(free_banks) <= spare:
+                    break
+                advance([product])
+                spare = spare + (product not in banks)
 
+        widen_w(0)
         spread_w_scale()
         scale_f(0, "scalar")
         scale_f(0, "vector")
-        widen_planes(0)
         turn_f(0)
+        widen_w(1)
         copy_turned()
-        lace_planes(0)
-        widen_planes(1)
+        lace("vector", 0, range(UNIT_BLOCKS))
         scale_f(1, "vector")
         turn_e(0)
+        widen_w(2)
         copy_turned()
 
         for k in range(STEPS):
             run = RUNS.get(k, [])
-            on_vector = WIDEN_ON_VECTOR.get(k, 0)
             last = k == STEPS - 1
             if k + 1 < TILES:
                 turn_f(k + 1)
-            if k + 1 in PLAIN_UNITS:
-                lace_planes(k + 1)
-            elif not last:
-                widen_w(k + 1, range(on_vector, UNIT_BLOCKS), "scalar")
+            if k + 3 < STEPS:
+                widen_w(k + 3)
             copy_turned()
-            if k + 2 in PLAIN_UNITS:
-                widen_planes(k + 2)
-            for n in range(len(sums) if last else min(len(sums), 2 if run else 1)):
+            advance(run)
+            for n in range(len(sums) if last else min(len(sums), SILUS)):
                 finish()
+            if not last:
+                lace("vector", k + 1, range(1, vector_blocks(k + 1)))
             quantise_w(k)
-            if on_vector:
-                widen_w(k + 1, range(on_vector), "vector")
-            advance(behind_quantise(k))
-            if run and k + 2 < STEPS:
-                lace_on_vector(k + 2, 0, WIDE - GPSIMD_COLUMNS)
-                lace_on_gpsimd(k + 2, WIDE - GPSIMD_COLUMNS, WIDE)
+            if not last:
+                lace("vector", k + 1, range(1))
+            if last:
+                advance(run)
+            ahead(k, 0)
+            if k + 2 < STEPS:
+                lace("gpsimd", k + 2, range(vector_blocks(k + 2), UNIT_BLOCKS))
             if k + 2 < TILES:
                 scale_f(k + 2, "scalar")
             for product in run:
                 empty(product)
-                if last and product[0] == "a":
+                if last:
                     finish()
             if k < PAIRS:
                 quantise_e(k)
@@ -439,8 +381,4 @@ def tile_drafter_feature_fusion_d2_kernel(tc, e, f_bytes, f_scale, w_bytes, w_sc
             if k + 1 < PAIRS:
                 turn_e(k + 1)
             copy_turned()
-            if 0 < k < STEPS - 1:
-                ahead = groups_after(k)
-                advance(ahead[0][:1] if k == PAIRS - 2 else ahead[0])
-                if k == PAIRS - 1:
-                    advance(ahead[1][:1])
+            ahead(k, 2 if k + 2 < TILES else 0)

@@ -33,9 +33,9 @@ LAST_HALF = N // HALF - 1
 UNIT = ROWS * WIDE
 UNIT_BLOCKS = WIDE // B
 RUN = 4
-GPSIMD_BLOCKS = 3
-SILUS = 3
-F_ON_SCALAR = [0, 0, 0, 0, 2, 3, 3, 3]
+GPSIMD_COLUMNS = 256
+SILUS = 2
+F_ON_SCALAR = [1, 0, 0, 0, 2, 2, 2, 2]
 LACE = 4
 
 
@@ -60,28 +60,38 @@ def half_products(kind, h):
 
 
 HALVES = N // HALF
-UNITS = (wide_units("a", range(E_PASSES)) + [u for h in range(2, HALVES) for u in a_half(h)]
-         + [u for h in range(HALVES) for u in c_half(h)])
+UNITS = (wide_units("a", range(E_PASSES)) + [u for h in range(2, LAST_HALF) for u in a_half(h)]
+         + [u for h in range(LAST_HALF) for u in c_half(h)] + c_half(LAST_HALF)[:1] + a_half(LAST_HALF) + c_half(LAST_HALF)[1:])
 STEPS = len(UNITS)
-A_STEPS = HALVES
 
 
 def plan_runs():
     wide = wide_products("a", 0) + wide_products("a", RUN)
     second = half_products("a", 2)
-    groups = [wide[:4], wide[4:6] + second[:2], wide[6:] + second[2:]] + [half_products("a", h) for h in range(3, HALVES)]
+    groups = [wide[:4], second[:2] + wide[4:6], wide[6:] + second[2:]] + [half_products("a", h) for h in range(3, LAST_HALF)]
     runs = {E_PASSES + n: group for n, group in enumerate(groups)}
-    for h in range(HALVES - 2):
-        runs[A_STEPS + 2 * h + 2] = half_products("c", h)
-    runs[STEPS - 1] = half_products("c", HALVES - 2) + half_products("c", HALVES - 1)
+    for h in range(LAST_HALF):
+        runs[max(TILES, LAST_HALF + 2 * h + 2)] = half_products("c", h)
+    runs[STEPS - 1] = half_products("a", LAST_HALF) + half_products("c", LAST_HALF)
     return runs
 
 
 RUNS = plan_runs()
 
 
-def vector_blocks(k):
-    return UNIT_BLOCKS - (GPSIMD_BLOCKS if k - 2 in RUNS else 0)
+def scalar_blocks(step):
+    if step < PAIRS - 1:
+        return 0
+    if step + 3 < TILES:
+        return 1
+    if step <= TILES or step + 3 >= STEPS:
+        return 2
+    return int(step not in RUNS)
+
+
+def shares(k):
+    scalar_end = WIDE - (GPSIMD_COLUMNS if k - 2 in RUNS else 0)
+    return scalar_end - B * scalar_blocks(k - 2), scalar_end
 
 
 def f_passes_on_scalar(m):
@@ -152,14 +162,15 @@ def tile_drafter_feature_fusion_d2_kernel(tc, e, f_bytes, f_scale, w_bytes, w_sc
         load_f(0)
         load_w(0)
         for m in range(1, TILES):
+            load_f(m)
             load_w(m)
             if m - 1 < PAIRS:
                 load_e(m - 1)
-            load_f(m)
             if m == PAIRS - 1:
                 nc.sync.dma_start(out=bias[:, 0:WIDE], in_=b[0:WIDE].partition_broadcast(P))
+            if m == PAIRS + 1:
+                nc.sync.dma_start(out=bias[:, WIDE:N], in_=b[WIDE:N].partition_broadcast(P))
         nc.sync.dma_start(out=trusts[:], in_=trust.rearrange("(p m) o -> p (m o)", m=TILES))
-        nc.sync.dma_start(out=bias[:, WIDE:N], in_=b[WIDE:N].partition_broadcast(P))
         for k in range(TILES, STEPS):
             load_w(k)
 
@@ -174,7 +185,7 @@ def tile_drafter_feature_fusion_d2_kernel(tc, e, f_bytes, f_scale, w_bytes, w_sc
         def spread_w_scale():
             number, bank = take_bank([P, PASSES * W_BLOCKS])
             nc.tensor.matmul(bank[:], lhsT=quadrants[:], rhs=w_scale_rows[:].rearrange("p g j -> p (g j)"), start=True, stop=True)
-            nc.scalar.copy(out=w_scales[:].rearrange("p g j -> p (g j)"), in_=bank[:])
+            nc.vector.tensor_copy(out=w_scales[:].rearrange("p g j -> p (g j)"), in_=bank[:])
             free_banks.append(number)
 
         planes = {}
@@ -190,17 +201,20 @@ def tile_drafter_feature_fusion_d2_kernel(tc, e, f_bytes, f_scale, w_bytes, w_sc
                 nc.scalar.activation(out=dst, in_=src, func=ACT.Copy, scale=scale)
 
         def widen_w(k):
-            planes[k] = work.tile([P, ROWS, WIDE], BF16, name="w_planes", bufs=3)
+            planes[k] = work.tile([P, ROWS, WIDE], BF16, name="w_planes", bufs=4)
             nc.scalar.copy(out=planes[k][:].rearrange("p t c -> p (t c)"), in_=w_raw[k][:].rearrange("p t c -> p (t c)").bitcast(FP8))
 
-        def lace(engine, k, blocks):
+        def lace(engine, k, first, stop):
             if k not in wide:
                 wide[k] = work.tile([P, UNIT], BF16, align_bytes=64, name="w_wide", bufs=2)
-            for block in blocks:
-                g, j = block_of(k, block)
-                dst = wide[k][:, ROWS * B * block:ROWS * B * (block + 1)].rearrange("p (c i t) -> p c t i", i=LACE, t=ROWS)
-                src = planes[k][:, :, B * block:B * (block + 1)].rearrange("p t (c i) -> p c t i", i=LACE)
-                scaled(engine, dst, src, w_scales[:, g, j:j + 1])
+            for block in range(UNIT_BLOCKS):
+                c0, c1 = max(first, B * block), min(stop, B * (block + 1))
+                if c0 < c1:
+                    g, j = block_of(k, block)
+                    visit = LACE if engine == "vector" else 1
+                    dst = wide[k][:, ROWS * c0:ROWS * c1].rearrange("p (c i t) -> p c t i", i=visit, t=ROWS)
+                    src = planes[k][:, :, c0:c1].rearrange("p t (c i) -> p c t i", i=visit)
+                    scaled(engine, dst, src, w_scales[:, g, j:j + 1])
 
         def quantise(src, name, bufs):
             codes = work.tile([P, UNIT // ROWS], U32, align_bytes=256, name=name + "_codes", bufs=bufs)
@@ -222,7 +236,7 @@ def tile_drafter_feature_fusion_d2_kernel(tc, e, f_bytes, f_scale, w_bytes, w_sc
 
         def scale_f(m, engine):
             if m not in f_wide:
-                f_wide[m] = work.tile([P, D], BF16, name="f_wide")
+                f_wide[m] = work.tile([P, D], BF16, name="f_wide", bufs=4)
             split = (K_PASS // B) * f_passes_on_scalar(m)
             for j in (range(split) if engine == "scalar" else reversed(range(split, F_BLOCKS))):
                 src = f_raw[m][:, j * B:(j + 1) * B].bitcast(FP8)
@@ -270,6 +284,8 @@ def tile_drafter_feature_fusion_d2_kernel(tc, e, f_bytes, f_scale, w_bytes, w_sc
         banks = {}
         done = {}
         sums = []
+        made_sums = []
+        z_pairs = []
 
         def advance(products):
             for product in products:
@@ -297,21 +313,29 @@ def tile_drafter_feature_fusion_d2_kernel(tc, e, f_bytes, f_scale, w_bytes, w_sc
                 return [slice(0, 1), slice(1, 2)]
             return [slice(0, WIDE // product[2])]
 
-        first_sum = once.tile([P, TILES, N], F32)
+        first_sum = once.tile([P, TILES, N - HALF], F32)
 
         def empty(product):
             kind, n0, width, m0 = product
             number, bank = banks[product]
             count = WIDE // width
-            part = first_sum[:, m0:m0 + count, n0:n0 + width]
+            kept = n0 % (N - HALF)
+            part = first_sum[:, m0:m0 + count, kept:kept + width]
             if kind == "a":
-                nc.vector.tensor_tensor(out=part, in0=bank[:], in1=bias[:, n0:n0 + width].unsqueeze(1).to_broadcast([P, count, width]), op=ADD)
+                dst, other = part, bias[:, n0:n0 + width].unsqueeze(1).to_broadcast([P, count, width])
             else:
-                z = work.tile([P, count, width], F32, name="z", bufs=6)
-                sums.append((z[:], product))
+                if len(made_sums) % 2 == 0:
+                    z_pairs.append(once.tile([P, 2, count, width], F32, name="z", tag="e_raw%d" % (len(z_pairs) % PAIRS)))
+                dst, other = z_pairs[-1][:, len(made_sums) % 2], part
+                made_sums.append(product)
+                sums.append((dst, product))
+            if kind == "a":
+                for tiles in pieces(product):
+                    nc.vector.tensor_tensor(out=dst[:, tiles], in0=bank[:, tiles], in1=other[:, tiles], op=ADD)
+            else:
                 for i in range(count):
-                    nc.vector.scalar_tensor_tensor(out=z[:, i, :], in0=bank[:, i, :], scalar=trusts[:, m0 + i:m0 + i + 1],
-                                                   in1=part[:, i, :], op0=MULT, op1=ADD)
+                    nc.vector.scalar_tensor_tensor(out=dst[:, i, :], in0=bank[:, i, :], scalar=trusts[:, m0 + i:m0 + i + 1],
+                                                   in1=other[:, i, :], op0=MULT, op1=ADD)
             free_banks.append(number)
 
         def finish():
@@ -332,53 +356,56 @@ def tile_drafter_feature_fusion_d2_kernel(tc, e, f_bytes, f_scale, w_bytes, w_sc
                 advance([product])
                 spare = spare + (product not in banks)
 
-        widen_w(0)
-        spread_w_scale()
         scale_f(0, "scalar")
+        widen_w(0)
         scale_f(0, "vector")
         turn_f(0)
+        scale_f(1, "vector")
+        spread_w_scale()
         widen_w(1)
         copy_turned()
-        lace("vector", 0, range(UNIT_BLOCKS))
-        scale_f(1, "vector")
+        lace("vector", 0, 0, WIDE)
+        turn_f(1)
         turn_e(0)
-        widen_w(2)
-        copy_turned()
 
         for k in range(STEPS):
             run = RUNS.get(k, [])
             last = k == STEPS - 1
-            if k + 1 < TILES:
-                turn_f(k + 1)
-            if k + 3 < STEPS:
+            if k < E_PASSES:
+                copy_turned()
+                widen_w(k + 2)
+            if 0 < k < STEPS - 3:
                 widen_w(k + 3)
             copy_turned()
             advance(run)
             for n in range(len(sums) if last else min(len(sums), SILUS)):
                 finish()
             if not last:
-                lace("vector", k + 1, range(1, vector_blocks(k + 1)))
+                behind = min(B, shares(k + 1)[0]) if k + 2 < STEPS else 0
+                lace("vector", k + 1, behind, shares(k + 1)[0])
             quantise_w(k)
             if not last:
-                lace("vector", k + 1, range(1))
+                lace("vector", k + 1, 0, behind)
             if last:
                 advance(run)
-            ahead(k, 0)
-            if k + 2 < STEPS:
-                lace("gpsimd", k + 2, range(vector_blocks(k + 2), UNIT_BLOCKS))
-            if k + 2 < TILES:
-                scale_f(k + 2, "scalar")
-            for product in run:
-                empty(product)
-                if last:
-                    finish()
-            if k < PAIRS:
-                quantise_e(k)
-            if k + 2 < TILES:
-                scale_f(k + 2, "vector")
-            if k < TILES:
-                quantise_f(k)
+            ahead(k, 2 if k + 1 < PAIRS else 0)
             if k + 1 < PAIRS:
                 turn_e(k + 1)
-            copy_turned()
-            ahead(k, 2 if k + 2 < TILES else 0)
+            if k + 2 < STEPS:
+                lace("gpsimd", k + 2, shares(k + 2)[1], WIDE)
+                lace("scalar", k + 2, *shares(k + 2))
+            if k + 3 < TILES:
+                scale_f(k + 3, "scalar")
+            for product in run:
+                empty(product)
+                if last and product[0] == "c":
+                    finish()
+            if k + 2 < TILES:
+                scale_f(k + 2, "vector")
+            if k < PAIRS:
+                quantise_e(k)
+            if k < TILES:
+                quantise_f(k)
+            if k + 2 < TILES:
+                turn_f(k + 2)
+            ahead(k, 0)

@@ -27,82 +27,58 @@ PASSES = (E + D) // K_PASS
 E_PASSES = E // K_PASS
 F_BLOCKS = D // B
 W_BLOCKS = N // B
-WIDE = 512
-HALF = WIDE // 2
-LAST_HALF = N // HALF - 1
-UNIT = ROWS * WIDE
-UNIT_BLOCKS = WIDE // B
-RUN = 4
-GPSIMD_COLUMNS = 256
+STRIP = 256
+STRIPS = N // STRIP
+PIECE = ROWS * STRIP
+BANKS = 8
+LACE = 4
 SILUS = 2
 F_ON_SCALAR = [1, 0, 0, 0, 2, 2, 2, 2]
-LACE = 4
+SCALAR_STEPS = [4, 5, 6, 7, 8, 10, 14]
 
 
-def wide_units(kind, passes):
-    return [(kind, 0, WIDE, [g]) for g in passes]
+def a_unit(s):
+    return [[(s, g) for g in range(E_PASSES)]]
 
 
-def a_half(h):
-    return [("a", h * HALF, HALF, list(range(E_PASSES)))]
+def c_units(s):
+    return [[(s, g), (s, g + 1)] for g in range(E_PASSES, PASSES, 2)]
 
 
-def c_half(h):
-    return [("c", h * HALF, HALF, [g, g + 1]) for g in range(E_PASSES, PASSES, 2)]
+def products(kind, s, pairs=range(PAIRS)):
+    return [(kind, s, pair) for pair in pairs]
 
 
-def wide_products(kind, first):
-    return [(kind, 0, WIDE, m) for m in range(first, first + RUN)]
-
-
-def half_products(kind, h):
-    return [(kind, h * HALF, HALF, 2 * pair) for pair in range(PAIRS)]
-
-
-HALVES = N // HALF
-UNITS = (wide_units("a", range(E_PASSES)) + [u for h in range(2, LAST_HALF) for u in a_half(h)]
-         + [u for h in range(LAST_HALF) for u in c_half(h)] + c_half(LAST_HALF)[:1] + a_half(LAST_HALF) + c_half(LAST_HALF)[1:])
+LAST = STRIPS - 1
+UNITS = ([u for s in range(LAST) for u in a_unit(s)] + [u for s in range(LAST) for u in c_units(s)]
+         + c_units(LAST)[:1] + a_unit(LAST) + c_units(LAST)[1:])
 STEPS = len(UNITS)
 
 
 def plan_runs():
-    wide = wide_products("a", 0) + wide_products("a", RUN)
-    second = half_products("a", 2)
-    groups = [wide[:4], second[:2] + wide[4:6], wide[6:] + second[2:]] + [half_products("a", h) for h in range(3, LAST_HALF)]
-    runs = {E_PASSES + n: group for n, group in enumerate(groups)}
-    for h in range(LAST_HALF):
-        runs[max(TILES, LAST_HALF + 2 * h + 2)] = half_products("c", h)
-    runs[STEPS - 1] = half_products("a", LAST_HALF) + half_products("c", LAST_HALF)
+    early, late = range(2), range(2, PAIRS)
+    groups = [products("a", 0, early) + products("a", 1, early),
+              products("a", 2, early) + products("a", 0, [2]) + products("a", 1, [2]),
+              products("a", 2, [2]) + [("a", s, 3) for s in range(3)]] + [products("a", s) for s in range(3, LAST)]
+    runs = {2 + n: group for n, group in enumerate(groups)}
+    for s in range(LAST):
+        runs[max(TILES, LAST + 2 * s + 2)] = products("c", s)
+    runs[STEPS - 1] = products("a", LAST) + products("c", LAST)
     return runs
 
 
 RUNS = plan_runs()
 
 
-def scalar_blocks(step):
-    if step < PAIRS - 1:
-        return 0
-    if step + 3 < TILES:
-        return 1
-    if step <= TILES or step + 3 >= STEPS:
-        return 2
-    return int(step not in RUNS)
-
-
-def shares(k):
-    scalar_end = WIDE - (GPSIMD_COLUMNS if k - 2 in RUNS else 0)
-    return scalar_end - B * scalar_blocks(k - 2), scalar_end
-
-
-def f_passes_on_scalar(m):
-    return F_ON_SCALAR[m]
+def lacers(k):
+    return ["scalar" if k - 2 in SCALAR_STEPS else "vector", "gpsimd" if k - 2 in RUNS else "vector"]
 
 
 def tile_drafter_feature_fusion_d2_kernel(tc, e, f_bytes, f_scale, w_bytes, w_scale, trust, b, out):
     nc = tc.nc
     with ExitStack() as ctx:
         once = ctx.enter_context(tc.tile_pool(name="once", bufs=1))
-        work = ctx.enter_context(tc.tile_pool(name="work", bufs=3))
+        work = ctx.enter_context(tc.tile_pool(name="work", bufs=4))
         psum = ctx.enter_context(tc.psum_pool(name="psum", bufs=1))
 
         w_scale_rows = once.tile([P, PASSES, W_BLOCKS], F32)
@@ -134,17 +110,10 @@ def tile_drafter_feature_fusion_d2_kernel(tc, e, f_bytes, f_scale, w_bytes, w_sc
         e_raw = {}
         f_raw = {}
 
-        def block_of(k, block):
-            kind, n0, width, gs = UNITS[k]
-            h, j = divmod(block, width // B)
-            return gs[h], n0 // B + j
-
         def load_w(k):
-            kind, n0, width, gs = UNITS[k]
-            raw = once.tile([P, ROWS, WIDE], U8, name="w_raw%d" % k)
-            for h, g in enumerate(gs):
-                nc.sync.dma_start(out=raw[:, :, h * width:(h + 1) * width], in_=w_v[:, g, :, n0:n0 + width])
-            w_raw[k] = raw
+            for s, g in UNITS[k]:
+                w_raw[(s, g)] = once.tile([P, ROWS, STRIP], U8, name="w_raw%d_%d" % (s, g))
+                nc.sync.dma_start(out=w_raw[(s, g)][:], in_=w_v[:, g, :, s * STRIP:(s + 1) * STRIP])
 
         def load_e(pair):
             raw = once.tile([P, 2 * E], BF16, name="e_raw%d" % pair)
@@ -160,36 +129,38 @@ def tile_drafter_feature_fusion_d2_kernel(tc, e, f_bytes, f_scale, w_bytes, w_sc
         bias = once.tile([P, N], BF16)
         trusts = once.tile([P, TILES], BF16)
         load_f(0)
+        load_f(1)
         load_w(0)
         for m in range(1, TILES):
-            load_f(m)
+            if m > 1:
+                load_f(m)
             load_w(m)
             if m - 1 < PAIRS:
                 load_e(m - 1)
             if m == PAIRS - 1:
-                nc.sync.dma_start(out=bias[:, 0:WIDE], in_=b[0:WIDE].partition_broadcast(P))
+                nc.sync.dma_start(out=bias[:, 0:2 * STRIP], in_=b[0:2 * STRIP].partition_broadcast(P))
             if m == PAIRS + 1:
-                nc.sync.dma_start(out=bias[:, WIDE:N], in_=b[WIDE:N].partition_broadcast(P))
+                nc.sync.dma_start(out=bias[:, 2 * STRIP:N], in_=b[2 * STRIP:N].partition_broadcast(P))
         nc.sync.dma_start(out=trusts[:], in_=trust.rearrange("(p m) o -> p (m o)", m=TILES))
         for k in range(TILES, STEPS):
             load_w(k)
 
-        free_banks = list(range(2 * RUN))
+        free_banks = list(range(BANKS))
 
-        def take_bank(shape, dtype=F32):
+        def take_bank(shape):
             number = free_banks.pop(0)
-            return number, psum.tile(shape, dtype, name="bank%d" % number)
+            return number, psum.tile(shape, F32, name="bank%d" % number)
 
         w_scales = once.tile([P, PASSES, W_BLOCKS], F32)
 
         def spread_w_scale():
             number, bank = take_bank([P, PASSES * W_BLOCKS])
             nc.tensor.matmul(bank[:], lhsT=quadrants[:], rhs=w_scale_rows[:].rearrange("p g j -> p (g j)"), start=True, stop=True)
-            nc.vector.tensor_copy(out=w_scales[:].rearrange("p g j -> p (g j)"), in_=bank[:])
+            nc.scalar.copy(out=w_scales[:].rearrange("p g j -> p (g j)"), in_=bank[:])
             free_banks.append(number)
 
         planes = {}
-        wide = {}
+        laced = {}
         w_mx = {}
 
         def scaled(engine, dst, src, scale):
@@ -201,32 +172,38 @@ def tile_drafter_feature_fusion_d2_kernel(tc, e, f_bytes, f_scale, w_bytes, w_sc
                 nc.scalar.activation(out=dst, in_=src, func=ACT.Copy, scale=scale)
 
         def widen_w(k):
-            planes[k] = work.tile([P, ROWS, WIDE], BF16, name="w_planes", bufs=4)
-            nc.scalar.copy(out=planes[k][:].rearrange("p t c -> p (t c)"), in_=w_raw[k][:].rearrange("p t c -> p (t c)").bitcast(FP8))
+            tag = "w_planes" if k < 10 else "f_wide" if k < 14 else "turned"
+            both = work.tile([P, 2, ROWS, STRIP], BF16, align_bytes=64, name="w_planes", tag=tag, bufs=5 if k < 10 else 4)
+            for h, piece in enumerate(UNITS[k]):
+                planes[piece] = both[:, h]
+                nc.scalar.copy(out=planes[piece].rearrange("p t c -> p (t c)"),
+                               in_=w_raw[piece][:].rearrange("p t c -> p (t c)").bitcast(FP8))
 
-        def lace(engine, k, first, stop):
-            if k not in wide:
-                wide[k] = work.tile([P, UNIT], BF16, align_bytes=64, name="w_wide", bufs=2)
-            for block in range(UNIT_BLOCKS):
-                c0, c1 = max(first, B * block), min(stop, B * (block + 1))
-                if c0 < c1:
-                    g, j = block_of(k, block)
+        def lace(engine, k):
+            for piece, lacer in zip(UNITS[k], lacers(k)):
+                if lacer == engine:
+                    s, g = piece
+                    if piece == UNITS[k][1] and (k in RUNS or k - 2 in RUNS):
+                        laced[piece] = once.tile([P, PIECE], BF16, align_bytes=64, name="w_laced_late", tag="late%d" % (k % 2))
+                    else:
+                        laced[piece] = work.tile([P, PIECE], BF16, align_bytes=64, name="w_laced", bufs=6)
                     visit = LACE if engine == "vector" else 1
-                    dst = wide[k][:, ROWS * c0:ROWS * c1].rearrange("p (c i t) -> p c t i", i=visit, t=ROWS)
-                    src = planes[k][:, :, c0:c1].rearrange("p t (c i) -> p c t i", i=visit)
-                    scaled(engine, dst, src, w_scales[:, g, j:j + 1])
+                    for block in range(STRIP // B):
+                        dst = laced[piece][:, ROWS * B * block:ROWS * B * (block + 1)].rearrange("p (c i t) -> p c t i", i=visit, t=ROWS)
+                        src = planes[piece][:, :, B * block:B * (block + 1)].rearrange("p t (c i) -> p c t i", i=visit)
+                        j = s * STRIP // B + block
+                        scaled(engine, dst, src, w_scales[:, g, j:j + 1])
 
         def quantise(src, name, bufs):
-            codes = work.tile([P, UNIT // ROWS], U32, align_bytes=256, name=name + "_codes", bufs=bufs)
-            scales = work.tile([P, UNIT // ROWS], U8, align_bytes=256, name=name + "_scales", bufs=bufs)
+            words = src.shape[1] // ROWS
+            codes = work.tile([P, words], U32, align_bytes=256, name=name + "_codes", bufs=bufs)
+            scales = work.tile([P, words], U8, align_bytes=256, name=name + "_scales", bufs=bufs)
             nc.vector.quantize_mx(out=codes[:].bitcast(FP8X4), scales=scales[:], in_=src[:])
             return codes, scales
 
         def quantise_w(k):
-            kind, n0, width, gs = UNITS[k]
-            codes, scales = quantise(wide[k], "w", 5)
-            for h, g in enumerate(gs):
-                w_mx[(g, n0)] = (codes[:, h * width:(h + 1) * width], scales[:, h * width:(h + 1) * width])
+            for piece in UNITS[k]:
+                w_mx[piece] = quantise(laced[piece], "w", 12)
 
         f_wide = {}
         turned = {}
@@ -236,8 +213,8 @@ def tile_drafter_feature_fusion_d2_kernel(tc, e, f_bytes, f_scale, w_bytes, w_sc
 
         def scale_f(m, engine):
             if m not in f_wide:
-                f_wide[m] = work.tile([P, D], BF16, name="f_wide", bufs=4)
-            split = (K_PASS // B) * f_passes_on_scalar(m)
+                f_wide[m] = work.tile([P, D], BF16, align_bytes=64, name="f_wide")
+            split = (K_PASS // B) * F_ON_SCALAR[m]
             for j in (range(split) if engine == "scalar" else reversed(range(split, F_BLOCKS))):
                 src = f_raw[m][:, j * B:(j + 1) * B].bitcast(FP8)
                 scale = f_scales[:, m * F_BLOCKS + j:m * F_BLOCKS + j + 1]
@@ -264,8 +241,8 @@ def tile_drafter_feature_fusion_d2_kernel(tc, e, f_bytes, f_scale, w_bytes, w_sc
             while in_psum:
                 key, half, number, bank = in_psum.pop(0)
                 if half == 0:
-                    turned[key] = work.tile([P, UNIT], BF16, align_bytes=64, name="turned", bufs=4)
-                dst = turned[key][:, UNIT // 2 * half:UNIT // 2 * (half + 1)].bitcast(F32).rearrange("p (h r u) -> p h r u", h=2, u=2)
+                    turned[key] = work.tile([P, D], BF16, align_bytes=64, name="turned")
+                dst = turned[key][:, D // 2 * half:D // 2 * (half + 1)].bitcast(F32).rearrange("p (h r u) -> p h r u", h=2, u=2)
                 nc.scalar.copy(out=dst, in_=bank[:].rearrange("p h u r -> p h r u"))
                 free_banks.append(number)
 
@@ -273,7 +250,7 @@ def tile_drafter_feature_fusion_d2_kernel(tc, e, f_bytes, f_scale, w_bytes, w_sc
             turn(e_raw[pair], ("e", pair), 2 * E_PASSES)
 
         def turn_f(m):
-            turn(f_wide[m], ("f", m), f_passes_on_scalar(m))
+            turn(f_wide[m], ("f", m), F_ON_SCALAR[m])
 
         def quantise_e(pair):
             x_mx[("e", pair)] = quantise(turned[("e", pair)], "e", PAIRS)
@@ -283,88 +260,65 @@ def tile_drafter_feature_fusion_d2_kernel(tc, e, f_bytes, f_scale, w_bytes, w_sc
 
         banks = {}
         done = {}
-        sums = []
-        made_sums = []
-        z_pairs = []
+        finished = []
+        sums = once.tile([P, STRIPS, TILES, STRIP], F32)
 
-        def advance(products):
-            for product in products:
-                kind, n0, width, m0 = product
-                count = WIDE // width
+        def advance(group):
+            for product in group:
+                kind, s, pair = product
                 whole = list(range(E_PASSES) if kind == "a" else range(E_PASSES, PASSES))
                 made = done.setdefault(product, [])
-                for i in range(count):
-                    m = m0 + i
-                    key = ("e", m // 2) if kind == "a" else ("f", m)
-                    x_first = E_PASSES * (m % 2) if kind == "a" else -E_PASSES
+                for i in range(2):
+                    key = ("e", pair) if kind == "a" else ("f", 2 * pair + i)
+                    x_first = E_PASSES * i if kind == "a" else -E_PASSES
                     for g in whole:
-                        if key in x_mx and (g, n0) in w_mx and (i, g) not in made:
+                        if key in x_mx and (s, g) in w_mx and (i, g) not in made:
                             if product not in banks:
-                                banks[product] = take_bank([P, count, width])
+                                banks[product] = take_bank([P, 2, STRIP])
                             made.append((i, g))
                             x_cols = slice((x_first + g) * P, (x_first + g + 1) * P)
-                            x, w = x_mx[key], w_mx[(g, n0)]
+                            x, w = x_mx[key], w_mx[(s, g)]
                             nc.tensor.matmul_mx(out=banks[product][1][:, i, :], lhsT=x[0][:, x_cols].bitcast(FP8X4), lhsT_scale=x[1][:, x_cols],
-                                                rhs=w[0].bitcast(FP8X4), rhs_scale=w[1],
-                                                start=len(made) == 1, stop=len(made) == count * len(whole))
-
-        def pieces(product):
-            if product == RUNS[STEPS - 1][-1]:
-                return [slice(0, 1), slice(1, 2)]
-            return [slice(0, WIDE // product[2])]
-
-        first_sum = once.tile([P, TILES, N - HALF], F32)
+                                                rhs=w[0][:].bitcast(FP8X4), rhs_scale=w[1][:],
+                                                start=len(made) == 1, stop=len(made) == 2 * len(whole))
 
         def empty(product):
-            kind, n0, width, m0 = product
+            kind, s, pair = product
             number, bank = banks[product]
-            count = WIDE // width
-            kept = n0 % (N - HALF)
-            part = first_sum[:, m0:m0 + count, kept:kept + width]
+            part = sums[:, s, 2 * pair:2 * pair + 2, :]
             if kind == "a":
-                dst, other = part, bias[:, n0:n0 + width].unsqueeze(1).to_broadcast([P, count, width])
+                nc.vector.tensor_tensor(out=part, in0=bank[:], in1=bias[:, s * STRIP:(s + 1) * STRIP].unsqueeze(1).to_broadcast([P, 2, STRIP]), op=ADD)
             else:
-                if len(made_sums) % 2 == 0:
-                    z_pairs.append(once.tile([P, 2, count, width], F32, name="z", tag="e_raw%d" % (len(z_pairs) % PAIRS)))
-                dst, other = z_pairs[-1][:, len(made_sums) % 2], part
-                made_sums.append(product)
-                sums.append((dst, product))
-            if kind == "a":
-                for tiles in pieces(product):
-                    nc.vector.tensor_tensor(out=dst[:, tiles], in0=bank[:, tiles], in1=other[:, tiles], op=ADD)
-            else:
-                for i in range(count):
-                    nc.vector.scalar_tensor_tensor(out=dst[:, i, :], in0=bank[:, i, :], scalar=trusts[:, m0 + i:m0 + i + 1],
-                                                   in1=other[:, i, :], op0=MULT, op1=ADD)
+                for i in range(2):
+                    m = 2 * pair + i
+                    nc.vector.scalar_tensor_tensor(out=part[:, i, :], in0=bank[:, i, :], scalar=trusts[:, m:m + 1],
+                                                   in1=part[:, i, :], op0=MULT, op1=ADD)
+                finished.append(product)
             free_banks.append(number)
 
         def finish():
-            z, product = sums.pop(0)
-            kind, n0, width, m0 = product
-            res = work.tile([P, WIDE // width, width], F32, name="res", bufs=6)
-            for tiles in pieces(product):
-                nc.scalar.activation(out=res[:, tiles], in_=z[:, tiles], func=ACT.Silu)
-                nc.sync.dma_start(out=o_v[:, m0 + tiles.start:m0 + tiles.stop, n0:n0 + width], in_=res[:, tiles])
-
-        def waiting(k):
-            return [product for step in sorted(RUNS) if step > k for product in RUNS[step]]
+            kind, s, pair = product = finished.pop(0)
+            first = 2 * pair
+            for tiles in ([slice(first, first + 1), slice(first + 1, first + 2)] if product == RUNS[STEPS - 1][-1] else [slice(first, first + 2)]):
+                nc.scalar.activation(out=sums[:, s, tiles, :], in_=sums[:, s, tiles, :], func=ACT.Silu)
+                nc.sync.dma_start(out=o_v[:, tiles, s * STRIP:(s + 1) * STRIP], in_=sums[:, s, tiles, :])
 
         def ahead(k, spare):
-            for product in waiting(k):
+            for product in [product for step in sorted(RUNS) if step > k for product in RUNS[step]]:
                 if product not in banks and len(free_banks) <= spare:
                     break
                 advance([product])
                 spare = spare + (product not in banks)
 
         scale_f(0, "scalar")
+        spread_w_scale()
         widen_w(0)
         scale_f(0, "vector")
         turn_f(0)
         scale_f(1, "vector")
-        spread_w_scale()
         widen_w(1)
         copy_turned()
-        lace("vector", 0, 0, WIDE)
+        lace("vector", 0)
         turn_f(1)
         turn_e(0)
 
@@ -378,22 +332,19 @@ def tile_drafter_feature_fusion_d2_kernel(tc, e, f_bytes, f_scale, w_bytes, w_sc
                 widen_w(k + 3)
             copy_turned()
             advance(run)
-            for n in range(len(sums) if last else min(len(sums), SILUS)):
+            for n in range(len(finished) if last else min(len(finished), SILUS)):
                 finish()
             if not last:
-                behind = min(B, shares(k + 1)[0]) if k + 2 < STEPS else 0
-                lace("vector", k + 1, behind, shares(k + 1)[0])
+                lace("vector", k + 1)
             quantise_w(k)
-            if not last:
-                lace("vector", k + 1, 0, behind)
             if last:
                 advance(run)
             ahead(k, 2 if k + 1 < PAIRS else 0)
             if k + 1 < PAIRS:
                 turn_e(k + 1)
             if k + 2 < STEPS:
-                lace("gpsimd", k + 2, shares(k + 2)[1], WIDE)
-                lace("scalar", k + 2, *shares(k + 2))
+                lace("gpsimd", k + 2)
+                lace("scalar", k + 2)
             if k + 3 < TILES:
                 scale_f(k + 3, "scalar")
             for product in run:

@@ -33,8 +33,9 @@ PIECE = ROWS * STRIP
 BANKS = 8
 LACE = 4
 SILUS = 2
-F_ON_SCALAR = [1, 0, 0, 0, 2, 2, 2, 2]
-SCALAR_STEPS = [4, 5, 6, 7, 8, 10, 14]
+F_ON_SCALAR = [1, 0, 0, 0, 2, 3, 3, 3]
+GPSIMD_BLOCKS = 3
+SCALAR_BLOCKS = [0] * 8 + [1, 2, 0, 0, 0, 0, 2, 0, 0, 1]
 
 
 def a_unit(s):
@@ -50,20 +51,24 @@ def products(kind, s, pairs=range(PAIRS)):
 
 
 LAST = STRIPS - 1
-UNITS = ([u for s in range(LAST) for u in a_unit(s)] + [u for s in range(LAST) for u in c_units(s)]
-         + c_units(LAST)[:1] + a_unit(LAST) + c_units(LAST)[1:])
+UNITS = ([u for s in range(LAST - 1) for u in a_unit(s)] + c_units(0) + c_units(1) + a_unit(LAST - 1)
+         + [u for s in range(2, LAST) for u in c_units(s)] + c_units(LAST)[:1] + a_unit(LAST) + c_units(LAST)[1:])
 STEPS = len(UNITS)
+LAST_A = STEPS - 2
 
 
 def plan_runs():
     early, late = range(2), range(2, PAIRS)
     groups = [products("a", 0, early) + products("a", 1, early),
               products("a", 2, early) + products("a", 0, [2]) + products("a", 1, [2]),
-              products("a", 2, [2]) + [("a", s, 3) for s in range(3)]] + [products("a", s) for s in range(3, LAST)]
+              products("a", 2, [2]) + [("a", s, 3) for s in range(3)]] + [products("a", 3)]
     runs = {2 + n: group for n, group in enumerate(groups)}
-    for s in range(LAST):
-        runs[max(TILES, LAST + 2 * s + 2)] = products("c", s)
-    runs[STEPS - 1] = products("a", LAST) + products("c", LAST)
+    for n, group in enumerate([products("c", 0), products("c", 1), products("a", LAST - 1)]):
+        runs[TILES + n] = group
+    for s in range(2, LAST):
+        runs[LAST + 2 * s + 2] = products("c", s)
+    tail = products("a", LAST)
+    runs[STEPS - 1] = tail + products("c", LAST)
     return runs
 
 
@@ -71,7 +76,9 @@ RUNS = plan_runs()
 
 
 def lacers(k):
-    return ["scalar" if k - 2 in SCALAR_STEPS else "vector", "gpsimd" if k - 2 in RUNS else "vector"]
+    gpsimd = GPSIMD_BLOCKS if k - 2 in RUNS else 0
+    scalar = min(SCALAR_BLOCKS[k], 4 - gpsimd)
+    return ["vector"] * (4 - gpsimd - scalar) + ["scalar"] * scalar + ["gpsimd"] * gpsimd
 
 
 def tile_drafter_feature_fusion_d2_kernel(tc, e, f_bytes, f_scale, w_bytes, w_scale, trust, b, out):
@@ -171,39 +178,40 @@ def tile_drafter_feature_fusion_d2_kernel(tc, e, f_bytes, f_scale, w_bytes, w_sc
             else:
                 nc.scalar.activation(out=dst, in_=src, func=ACT.Copy, scale=scale)
 
-        def widen_w(k):
+        def widen_w(k, between=None):
             tag = "w_planes" if k < 10 else "f_wide" if k < 14 else "turned"
             both = work.tile([P, 2, ROWS, STRIP], BF16, align_bytes=64, name="w_planes", tag=tag, bufs=5 if k < 10 else 4)
             for h, piece in enumerate(UNITS[k]):
                 planes[piece] = both[:, h]
                 nc.scalar.copy(out=planes[piece].rearrange("p t c -> p (t c)"),
                                in_=w_raw[piece][:].rearrange("p t c -> p (t c)").bitcast(FP8))
+                if between and h == 0:
+                    between()
 
-        def lace(engine, k):
-            for piece, lacer in zip(UNITS[k], lacers(k)):
-                if lacer == engine:
-                    s, g = piece
-                    if piece == UNITS[k][1] and (k in RUNS or k - 2 in RUNS):
-                        laced[piece] = once.tile([P, PIECE], BF16, align_bytes=64, name="w_laced_late", tag="late%d" % (k % 2))
-                    else:
-                        laced[piece] = work.tile([P, PIECE], BF16, align_bytes=64, name="w_laced", bufs=6)
-                    visit = LACE if engine == "vector" else 1
-                    for block in range(STRIP // B):
-                        dst = laced[piece][:, ROWS * B * block:ROWS * B * (block + 1)].rearrange("p (c i t) -> p c t i", i=visit, t=ROWS)
-                        src = planes[piece][:, :, B * block:B * (block + 1)].rearrange("p t (c i) -> p c t i", i=visit)
-                        j = s * STRIP // B + block
-                        scaled(engine, dst, src, w_scales[:, g, j:j + 1])
+        def lace(engine, k, part=slice(0, 4)):
+            if k not in laced:
+                laced[k] = work.tile([P, 4, ROWS * B], BF16, align_bytes=64, name="w_laced", bufs=2)
+            visit = 1 if engine == "scalar" else LACE
+            for n in [n for n, lacer in enumerate(lacers(k)) if lacer == engine and (k, n) not in laced][part]:
+                laced[(k, n)] = engine
+                h, block = divmod(n, STRIP // B)
+                s, g = UNITS[k][h]
+                dst = laced[k][:, n].rearrange("p (c i t) -> p c t i", i=visit, t=ROWS)
+                src = planes[(s, g)][:, :, B * block:B * (block + 1)].rearrange("p t (c i) -> p c t i", i=visit)
+                j = s * STRIP // B + block
+                scaled(engine, dst, src, w_scales[:, g, j:j + 1])
 
         def quantise(src, name, bufs):
-            words = src.shape[1] // ROWS
+            words = D // ROWS
             codes = work.tile([P, words], U32, align_bytes=256, name=name + "_codes", bufs=bufs)
             scales = work.tile([P, words], U8, align_bytes=256, name=name + "_scales", bufs=bufs)
-            nc.vector.quantize_mx(out=codes[:].bitcast(FP8X4), scales=scales[:], in_=src[:])
+            nc.vector.quantize_mx(out=codes[:].bitcast(FP8X4), scales=scales[:], in_=src)
             return codes, scales
 
         def quantise_w(k):
-            for piece in UNITS[k]:
-                w_mx[piece] = quantise(laced[piece], "w", 12)
+            codes, scales = quantise(laced[k][:].rearrange("p n c -> p (n c)"), "w", 6)
+            for n, piece in enumerate(UNITS[k]):
+                w_mx[piece] = (codes[:, n * STRIP:(n + 1) * STRIP], scales[:, n * STRIP:(n + 1) * STRIP])
 
         f_wide = {}
         turned = {}
@@ -253,10 +261,10 @@ def tile_drafter_feature_fusion_d2_kernel(tc, e, f_bytes, f_scale, w_bytes, w_sc
             turn(f_wide[m], ("f", m), F_ON_SCALAR[m])
 
         def quantise_e(pair):
-            x_mx[("e", pair)] = quantise(turned[("e", pair)], "e", PAIRS)
+            x_mx[("e", pair)] = quantise(turned[("e", pair)][:], "e", PAIRS)
 
         def quantise_f(m):
-            x_mx[("f", m)] = quantise(turned[("f", m)], "f", TILES)
+            x_mx[("f", m)] = quantise(turned[("f", m)][:], "f", TILES)
 
         banks = {}
         done = {}
@@ -279,7 +287,7 @@ def tile_drafter_feature_fusion_d2_kernel(tc, e, f_bytes, f_scale, w_bytes, w_sc
                             x_cols = slice((x_first + g) * P, (x_first + g + 1) * P)
                             x, w = x_mx[key], w_mx[(s, g)]
                             nc.tensor.matmul_mx(out=banks[product][1][:, i, :], lhsT=x[0][:, x_cols].bitcast(FP8X4), lhsT_scale=x[1][:, x_cols],
-                                                rhs=w[0][:].bitcast(FP8X4), rhs_scale=w[1][:],
+                                                rhs=w[0].bitcast(FP8X4), rhs_scale=w[1],
                                                 start=len(made) == 1, stop=len(made) == 2 * len(whole))
 
         def empty(product):
@@ -311,8 +319,7 @@ def tile_drafter_feature_fusion_d2_kernel(tc, e, f_bytes, f_scale, w_bytes, w_sc
                 spare = spare + (product not in banks)
 
         scale_f(0, "scalar")
-        spread_w_scale()
-        widen_w(0)
+        widen_w(0, spread_w_scale)
         scale_f(0, "vector")
         turn_f(0)
         scale_f(1, "vector")
@@ -331,15 +338,25 @@ def tile_drafter_feature_fusion_d2_kernel(tc, e, f_bytes, f_scale, w_bytes, w_sc
             if 0 < k < STEPS - 3:
                 widen_w(k + 3)
             copy_turned()
-            advance(run)
+            advance(run[:PAIRS])
             for n in range(len(finished) if last else min(len(finished), SILUS)):
                 finish()
             if not last:
-                lace("vector", k + 1)
-            quantise_w(k)
+                lace("vector", k + 1, slice(1, 4))
+            if k != LAST_A:
+                quantise_w(k)
+            if k + 1 == LAST_A:
+                quantise_w(LAST_A)
+            if not last:
+                lace("vector", k + 1, slice(0, 1))
+            if k + 2 == LAST_A:
+                lace("vector", LAST_A)
             if last:
                 advance(run)
-            ahead(k, 2 if k + 1 < PAIRS else 0)
+            if k + 1 == LAST_A:
+                advance(products("c", LAST))
+            elif run or k >= TILES:
+                ahead(k, 2 if k + 1 < PAIRS else 0)
             if k + 1 < PAIRS:
                 turn_e(k + 1)
             if k + 2 < STEPS:
@@ -349,11 +366,16 @@ def tile_drafter_feature_fusion_d2_kernel(tc, e, f_bytes, f_scale, w_bytes, w_sc
                 scale_f(k + 3, "scalar")
             for product in run:
                 empty(product)
+                if k + 1 == LAST_A and product[0] == "c":
+                    advance([("a", LAST, product[2])])
                 if last and product[0] == "c":
                     finish()
+            if run and k < PAIRS:
+                quantise_e(k)
+                advance(RUNS[k + 1][:len(free_banks) - 2])
             if k + 2 < TILES:
                 scale_f(k + 2, "vector")
-            if k < PAIRS:
+            if not run and k < PAIRS:
                 quantise_e(k)
             if k < TILES:
                 quantise_f(k)

@@ -34,8 +34,8 @@ BANKS = 8
 LACE = 4
 SILUS = 2
 F_ON_SCALAR = [1, 0, 0, 0, 2, 3, 3, 3]
-GPSIMD_BLOCKS = 3
-SCALAR_BLOCKS = [0] * 8 + [1, 2, 0, 0, 0, 0, 2, 0, 0, 1]
+GPSIMD_COLUMNS = 304
+SCALAR_BLOCKS = [0] * 8 + [2, 2, 1, 0, 0, 0, 2, 0, 0, 2]
 
 
 def a_unit(s):
@@ -75,10 +75,10 @@ def plan_runs():
 RUNS = plan_runs()
 
 
-def lacers(k):
-    gpsimd = GPSIMD_BLOCKS if k - 2 in RUNS else 0
-    scalar = min(SCALAR_BLOCKS[k], 4 - gpsimd)
-    return ["vector"] * (4 - gpsimd - scalar) + ["scalar"] * scalar + ["gpsimd"] * gpsimd
+def share(engine, k):
+    scalar_end = 2 * STRIP - (GPSIMD_COLUMNS if k - 2 in RUNS else 0)
+    vector_end = max(0, scalar_end - B * SCALAR_BLOCKS[k])
+    return {"vector": (0, vector_end), "scalar": (vector_end, scalar_end), "gpsimd": (scalar_end, 2 * STRIP)}[engine]
 
 
 def tile_drafter_feature_fusion_d2_kernel(tc, e, f_bytes, f_scale, w_bytes, w_scale, trust, b, out):
@@ -188,18 +188,20 @@ def tile_drafter_feature_fusion_d2_kernel(tc, e, f_bytes, f_scale, w_bytes, w_sc
                 if between and h == 0:
                     between()
 
-        def lace(engine, k, part=slice(0, 4)):
+        def lace(engine, k, blocks=range(4)):
             if k not in laced:
-                laced[k] = work.tile([P, 4, ROWS * B], BF16, align_bytes=64, name="w_laced", bufs=2)
+                laced[k] = work.tile([P, 2 * STRIP, ROWS], BF16, align_bytes=64, name="w_laced", bufs=2)
             visit = 1 if engine == "scalar" else LACE
-            for n in [n for n, lacer in enumerate(lacers(k)) if lacer == engine and (k, n) not in laced][part]:
-                laced[(k, n)] = engine
-                h, block = divmod(n, STRIP // B)
-                s, g = UNITS[k][h]
-                dst = laced[k][:, n].rearrange("p (c i t) -> p c t i", i=visit, t=ROWS)
-                src = planes[(s, g)][:, :, B * block:B * (block + 1)].rearrange("p t (c i) -> p c t i", i=visit)
-                j = s * STRIP // B + block
-                scaled(engine, dst, src, w_scales[:, g, j:j + 1])
+            first, stop = share(engine, k)
+            for n in blocks:
+                c0, c1 = max(first, B * n), min(stop, B * (n + 1))
+                if c0 < c1:
+                    h, block = divmod(n, STRIP // B)
+                    s, g = UNITS[k][h]
+                    dst = laced[k][:, c0:c1].rearrange("p (c i) t -> p c t i", i=visit)
+                    src = planes[(s, g)][:, :, c0 - h * STRIP:c1 - h * STRIP].rearrange("p t (c i) -> p c t i", i=visit)
+                    j = s * STRIP // B + block
+                    scaled(engine, dst, src, w_scales[:, g, j:j + 1])
 
         def quantise(src, name, bufs):
             words = D // ROWS
@@ -209,7 +211,7 @@ def tile_drafter_feature_fusion_d2_kernel(tc, e, f_bytes, f_scale, w_bytes, w_sc
             return codes, scales
 
         def quantise_w(k):
-            codes, scales = quantise(laced[k][:].rearrange("p n c -> p (n c)"), "w", 6)
+            codes, scales = quantise(laced[k][:].rearrange("p c t -> p (c t)"), "w", 6)
             for n, piece in enumerate(UNITS[k]):
                 w_mx[piece] = (codes[:, n * STRIP:(n + 1) * STRIP], scales[:, n * STRIP:(n + 1) * STRIP])
 
@@ -341,14 +343,14 @@ def tile_drafter_feature_fusion_d2_kernel(tc, e, f_bytes, f_scale, w_bytes, w_sc
             advance(run[:PAIRS])
             for n in range(len(finished) if last else min(len(finished), SILUS)):
                 finish()
-            if not last:
-                lace("vector", k + 1, slice(1, 4))
+            if k + 1 < LAST_A:
+                lace("vector", k + 1, range(1, 4))
             if k != LAST_A:
                 quantise_w(k)
             if k + 1 == LAST_A:
                 quantise_w(LAST_A)
-            if not last:
-                lace("vector", k + 1, slice(0, 1))
+            if k + 1 < LAST_A:
+                lace("vector", k + 1, range(1))
             if k + 2 == LAST_A:
                 lace("vector", LAST_A)
             if last:

@@ -27,58 +27,53 @@ PASSES = (E + D) // K_PASS
 E_PASSES = E // K_PASS
 F_BLOCKS = D // B
 W_BLOCKS = N // B
-STRIP = 256
-STRIPS = N // STRIP
-PIECE = ROWS * STRIP
+WIDE = 512
+HALF = WIDE // 2
+CHUNKS = N // WIDE
+UNIT = ROWS * WIDE
 BANKS = 8
 LACE = 4
 SILUS = 2
 F_ON_SCALAR = [1, 0, 0, 0, 2, 3, 3, 3]
 GPSIMD_COLUMNS = 304
-SCALAR_BLOCKS = [0] * 8 + [2, 2, 1, 0, 0, 0, 2, 0, 0, 2]
+SCALAR_BLOCKS = [0] * 8 + [1, 2, 1, 0, 0, 0, 1, 2, 0, 2]
 
 
-def a_unit(s):
-    return [[(s, g) for g in range(E_PASSES)]]
+def wide_units(n, passes):
+    return [[(g, n * WIDE, WIDE)] for g in passes]
 
 
-def c_units(s):
-    return [[(s, g), (s, g + 1)] for g in range(E_PASSES, PASSES, 2)]
+def half_unit(n0):
+    return [[(g, n0, HALF) for g in range(E_PASSES)]]
 
 
-def products(kind, s, pairs=range(PAIRS)):
-    return [(kind, s, pair) for pair in pairs]
+def wide_products(kind, n, tiles):
+    return [(kind, n * WIDE, WIDE, m) for m in tiles]
 
 
-LAST = STRIPS - 1
-UNITS = ([u for s in range(LAST - 1) for u in a_unit(s)] + c_units(0) + c_units(1) + a_unit(LAST - 1)
-         + [u for s in range(2, LAST) for u in c_units(s)] + c_units(LAST)[:1] + a_unit(LAST) + c_units(LAST)[1:])
+def half_products(n0, pairs):
+    return [("a", n0, HALF, 2 * pair) for pair in pairs]
+
+
+A_PASSES, C_PASSES = range(E_PASSES), range(E_PASSES, PASSES)
+UNITS = ([[(0, 0, HALF), (0, HALF, HALF)]] + wide_units(0, A_PASSES[1:]) + half_unit(WIDE) + half_unit(WIDE + HALF) + wide_units(0, C_PASSES)
+         + wide_units(2, A_PASSES) + wide_units(1, C_PASSES) + wide_units(2, C_PASSES))
 STEPS = len(UNITS)
-LAST_A = STEPS - 2
-
-
-def plan_runs():
-    early, late = range(2), range(2, PAIRS)
-    groups = [products("a", 0, early) + products("a", 1, early),
-              products("a", 2, early) + products("a", 0, [2]) + products("a", 1, [2]),
-              products("a", 2, [2]) + [("a", s, 3) for s in range(3)]] + [products("a", 3)]
-    runs = {2 + n: group for n, group in enumerate(groups)}
-    for n, group in enumerate([products("c", 0), products("c", 1), products("a", LAST - 1)]):
-        runs[TILES + n] = group
-    for s in range(2, LAST):
-        runs[LAST + 2 * s + 2] = products("c", s)
-    tail = products("a", LAST)
-    runs[STEPS - 1] = tail + products("c", LAST)
-    return runs
-
-
-RUNS = plan_runs()
+LOW, HIGH = range(PAIRS), range(PAIRS, TILES)
+RUNS = {2: wide_products("a", 0, LOW),
+        3: half_products(WIDE, [0, 1]) + wide_products("a", 0, [4, 5]),
+        4: half_products(WIDE, [2]) + wide_products("a", 0, [6, 7]) + half_products(WIDE, [3]),
+        5: half_products(WIDE + HALF, range(PAIRS)),
+        8: wide_products("c", 0, LOW), 9: wide_products("c", 0, HIGH),
+        10: wide_products("a", 2, LOW), 11: wide_products("a", 2, HIGH),
+        14: wide_products("c", 1, LOW), 15: wide_products("c", 1, HIGH),
+        17: wide_products("c", 2, range(TILES))}
 
 
 def share(engine, k):
-    scalar_end = 2 * STRIP - (GPSIMD_COLUMNS if k - 2 in RUNS else 0)
+    scalar_end = WIDE - (GPSIMD_COLUMNS if k - 2 in RUNS else 0)
     vector_end = max(0, scalar_end - B * SCALAR_BLOCKS[k])
-    return {"vector": (0, vector_end), "scalar": (vector_end, scalar_end), "gpsimd": (scalar_end, 2 * STRIP)}[engine]
+    return {"vector": (0, vector_end), "scalar": (vector_end, scalar_end), "gpsimd": (scalar_end, WIDE)}[engine]
 
 
 def tile_drafter_feature_fusion_d2_kernel(tc, e, f_bytes, f_scale, w_bytes, w_scale, trust, b, out):
@@ -118,9 +113,9 @@ def tile_drafter_feature_fusion_d2_kernel(tc, e, f_bytes, f_scale, w_bytes, w_sc
         f_raw = {}
 
         def load_w(k):
-            for s, g in UNITS[k]:
-                w_raw[(s, g)] = once.tile([P, ROWS, STRIP], U8, name="w_raw%d_%d" % (s, g))
-                nc.sync.dma_start(out=w_raw[(s, g)][:], in_=w_v[:, g, :, s * STRIP:(s + 1) * STRIP])
+            for g, n0, width in UNITS[k]:
+                w_raw[(g, n0)] = once.tile([P, ROWS, width], U8, name="w_raw%d_%d" % (g, n0))
+                nc.sync.dma_start(out=w_raw[(g, n0)][:], in_=w_v[:, g, :, n0:n0 + width])
 
         def load_e(pair):
             raw = once.tile([P, 2 * E], BF16, name="e_raw%d" % pair)
@@ -138,16 +133,22 @@ def tile_drafter_feature_fusion_d2_kernel(tc, e, f_bytes, f_scale, w_bytes, w_sc
         load_f(0)
         load_f(1)
         load_w(0)
-        for m in range(1, TILES):
-            if m > 1:
-                load_f(m)
+        load_w(1)
+        load_e(0)
+        load_f(2)
+        load_e(1)
+        load_w(2)
+        load_f(3)
+        load_w(3)
+        for m in range(4, TILES):
             load_w(m)
-            if m - 1 < PAIRS:
-                load_e(m - 1)
-            if m == PAIRS - 1:
-                nc.sync.dma_start(out=bias[:, 0:2 * STRIP], in_=b[0:2 * STRIP].partition_broadcast(P))
+            if m - 2 < PAIRS:
+                load_e(m - 2)
+            load_f(m)
+            if m == PAIRS:
+                nc.sync.dma_start(out=bias[:, 0:WIDE], in_=b[0:WIDE].partition_broadcast(P))
             if m == PAIRS + 1:
-                nc.sync.dma_start(out=bias[:, 2 * STRIP:N], in_=b[2 * STRIP:N].partition_broadcast(P))
+                nc.sync.dma_start(out=bias[:, WIDE:N], in_=b[WIDE:N].partition_broadcast(P))
         nc.sync.dma_start(out=trusts[:], in_=trust.rearrange("(p m) o -> p (m o)", m=TILES))
         for k in range(TILES, STEPS):
             load_w(k)
@@ -180,27 +181,27 @@ def tile_drafter_feature_fusion_d2_kernel(tc, e, f_bytes, f_scale, w_bytes, w_sc
 
         def widen_w(k, between=None):
             tag = "w_planes" if k < 10 else "f_wide" if k < 14 else "turned"
-            both = work.tile([P, 2, ROWS, STRIP], BF16, align_bytes=64, name="w_planes", tag=tag, bufs=5 if k < 10 else 4)
-            for h, piece in enumerate(UNITS[k]):
-                planes[piece] = both[:, h]
-                nc.scalar.copy(out=planes[piece].rearrange("p t c -> p (t c)"),
-                               in_=w_raw[piece][:].rearrange("p t c -> p (t c)").bitcast(FP8))
+            planes[k] = work.tile([P, UNIT], BF16, align_bytes=64, name="w_planes", tag=tag, bufs=5 if k < 10 else 4)
+            for h, (g, n0, width) in enumerate(UNITS[k]):
+                nc.scalar.copy(out=planes[k][:, h * ROWS * width:(h + 1) * ROWS * width],
+                               in_=w_raw[(g, n0)][:].rearrange("p t c -> p (t c)").bitcast(FP8))
                 if between and h == 0:
                     between()
 
-        def lace(engine, k, blocks=range(4)):
+        def lace(engine, k, blocks=range(WIDE // B)):
             if k not in laced:
-                laced[k] = work.tile([P, 2 * STRIP, ROWS], BF16, align_bytes=64, name="w_laced", bufs=2)
+                laced[k] = work.tile([P, WIDE, ROWS], BF16, align_bytes=64, name="w_laced", bufs=2)
             visit = 1 if engine == "scalar" else LACE
             first, stop = share(engine, k)
             for n in blocks:
                 c0, c1 = max(first, B * n), min(stop, B * (n + 1))
                 if c0 < c1:
-                    h, block = divmod(n, STRIP // B)
-                    s, g = UNITS[k][h]
+                    h = c0 // UNITS[k][0][2]
+                    g, n0, width = UNITS[k][h]
                     dst = laced[k][:, c0:c1].rearrange("p (c i) t -> p c t i", i=visit)
-                    src = planes[(s, g)][:, :, c0 - h * STRIP:c1 - h * STRIP].rearrange("p t (c i) -> p c t i", i=visit)
-                    j = s * STRIP // B + block
+                    rows = planes[k][:].rearrange("p (h t c) -> p h t c", t=ROWS, c=width)[:, h]
+                    src = rows[:, :, c0 - h * width:c1 - h * width].rearrange("p t (c i) -> p c t i", i=visit)
+                    j = (n0 + c0 - h * width) // B
                     scaled(engine, dst, src, w_scales[:, g, j:j + 1])
 
         def quantise(src, name, bufs):
@@ -211,9 +212,11 @@ def tile_drafter_feature_fusion_d2_kernel(tc, e, f_bytes, f_scale, w_bytes, w_sc
             return codes, scales
 
         def quantise_w(k):
-            codes, scales = quantise(laced[k][:].rearrange("p c t -> p (c t)"), "w", 6)
-            for n, piece in enumerate(UNITS[k]):
-                w_mx[piece] = (codes[:, n * STRIP:(n + 1) * STRIP], scales[:, n * STRIP:(n + 1) * STRIP])
+            codes, scales = quantise(laced[k][:].rearrange("p c t -> p (c t)"), "w", 8)
+            for h, (g, n0, width) in enumerate(UNITS[k]):
+                w_mx[(g, n0)] = (codes[:, h * width:(h + 1) * width], scales[:, h * width:(h + 1) * width])
+            if k == 0:
+                w_mx[(0, 0)] = (codes[:], scales[:])
 
         f_wide = {}
         turned = {}
@@ -271,47 +274,52 @@ def tile_drafter_feature_fusion_d2_kernel(tc, e, f_bytes, f_scale, w_bytes, w_sc
         banks = {}
         done = {}
         finished = []
-        sums = once.tile([P, STRIPS, TILES, STRIP], F32)
+        sums = once.tile([P, CHUNKS, TILES, WIDE], F32)
 
         def advance(group):
             for product in group:
-                kind, s, pair = product
-                whole = list(range(E_PASSES) if kind == "a" else range(E_PASSES, PASSES))
+                kind, n0, width, m0 = product
+                count = WIDE // width
+                whole = list(A_PASSES if kind == "a" else C_PASSES)
                 made = done.setdefault(product, [])
-                for i in range(2):
-                    key = ("e", pair) if kind == "a" else ("f", 2 * pair + i)
-                    x_first = E_PASSES * i if kind == "a" else -E_PASSES
+                for i in range(count):
+                    m = m0 + i
+                    key = ("e", m // 2) if kind == "a" else ("f", m)
+                    x_first = E_PASSES * (m % 2) if kind == "a" else -E_PASSES
                     for g in whole:
-                        if key in x_mx and (s, g) in w_mx and (i, g) not in made:
+                        if key in x_mx and (g, n0) in w_mx and (i, g) not in made:
                             if product not in banks:
-                                banks[product] = take_bank([P, 2, STRIP])
+                                banks[product] = take_bank([P, count, width])
                             made.append((i, g))
                             x_cols = slice((x_first + g) * P, (x_first + g + 1) * P)
-                            x, w = x_mx[key], w_mx[(s, g)]
+                            x, w = x_mx[key], w_mx[(g, n0)]
                             nc.tensor.matmul_mx(out=banks[product][1][:, i, :], lhsT=x[0][:, x_cols].bitcast(FP8X4), lhsT_scale=x[1][:, x_cols],
                                                 rhs=w[0].bitcast(FP8X4), rhs_scale=w[1],
-                                                start=len(made) == 1, stop=len(made) == 2 * len(whole))
+                                                start=len(made) == 1, stop=len(made) == count * len(whole))
+
+        def pieces(product):
+            return [slice(0, HALF), slice(HALF, WIDE)] if product == RUNS[STEPS - 1][-1] else [slice(0, WIDE)]
 
         def empty(product):
-            kind, s, pair = product
+            kind, n0, width, m0 = product
             number, bank = banks[product]
-            part = sums[:, s, 2 * pair:2 * pair + 2, :]
+            count = WIDE // width
+            part = sums[:, n0 // WIDE, m0:m0 + count, n0 % WIDE:n0 % WIDE + width]
             if kind == "a":
-                nc.vector.tensor_tensor(out=part, in0=bank[:], in1=bias[:, s * STRIP:(s + 1) * STRIP].unsqueeze(1).to_broadcast([P, 2, STRIP]), op=ADD)
+                nc.vector.tensor_tensor(out=part, in0=bank[:], in1=bias[:, n0:n0 + width].unsqueeze(1).to_broadcast([P, count, width]), op=ADD)
             else:
-                for i in range(2):
-                    m = 2 * pair + i
-                    nc.vector.scalar_tensor_tensor(out=part[:, i, :], in0=bank[:, i, :], scalar=trusts[:, m:m + 1],
-                                                   in1=part[:, i, :], op0=MULT, op1=ADD)
+                for cols in pieces(product):
+                    nc.vector.scalar_tensor_tensor(out=part[:, 0, cols], in0=bank[:, 0, cols], scalar=trusts[:, m0:m0 + 1],
+                                                   in1=part[:, 0, cols], op0=MULT, op1=ADD)
                 finished.append(product)
             free_banks.append(number)
 
         def finish():
-            kind, s, pair = product = finished.pop(0)
-            first = 2 * pair
-            for tiles in ([slice(first, first + 1), slice(first + 1, first + 2)] if product == RUNS[STEPS - 1][-1] else [slice(first, first + 2)]):
-                nc.scalar.activation(out=sums[:, s, tiles, :], in_=sums[:, s, tiles, :], func=ACT.Silu)
-                nc.sync.dma_start(out=o_v[:, tiles, s * STRIP:(s + 1) * STRIP], in_=sums[:, s, tiles, :])
+            kind, n0, width, m = product = finished.pop(0)
+            for cols in pieces(product):
+                z = sums[:, n0 // WIDE, m, cols]
+                nc.scalar.activation(out=z, in_=z, func=ACT.Silu)
+                nc.sync.dma_start(out=o_v[:, m, n0 + cols.start:n0 + cols.stop], in_=z)
 
         def ahead(k, spare):
             for product in [product for step in sorted(RUNS) if step > k for product in RUNS[step]]:
@@ -340,25 +348,21 @@ def tile_drafter_feature_fusion_d2_kernel(tc, e, f_bytes, f_scale, w_bytes, w_sc
             if 0 < k < STEPS - 3:
                 widen_w(k + 3)
             copy_turned()
-            advance(run[:PAIRS])
+            if not last:
+                advance(run)
             for n in range(len(finished) if last else min(len(finished), SILUS)):
                 finish()
-            if k + 1 < LAST_A:
-                lace("vector", k + 1, range(1, 4))
-            if k != LAST_A:
-                quantise_w(k)
-            if k + 1 == LAST_A:
-                quantise_w(LAST_A)
-            if k + 1 < LAST_A:
+            if not last:
+                lace("vector", k + 1, range(1, WIDE // B))
+            quantise_w(k)
+            if not last:
                 lace("vector", k + 1, range(1))
-            if k + 2 == LAST_A:
-                lace("vector", LAST_A)
             if last:
                 advance(run)
-            if k + 1 == LAST_A:
-                advance(products("c", LAST))
-            elif run or k >= TILES:
+            if (run or k >= TILES) and k + 2 < STEPS:
                 ahead(k, 2 if k + 1 < PAIRS else 0)
+            elif k + 1 == TILES:
+                advance(RUNS[TILES])
             if k + 1 < PAIRS:
                 turn_e(k + 1)
             if k + 2 < STEPS:
@@ -368,8 +372,6 @@ def tile_drafter_feature_fusion_d2_kernel(tc, e, f_bytes, f_scale, w_bytes, w_sc
                 scale_f(k + 3, "scalar")
             for product in run:
                 empty(product)
-                if k + 1 == LAST_A and product[0] == "c":
-                    advance([("a", LAST, product[2])])
                 if last and product[0] == "c":
                     finish()
             if run and k < PAIRS:
@@ -383,4 +385,7 @@ def tile_drafter_feature_fusion_d2_kernel(tc, e, f_bytes, f_scale, w_bytes, w_sc
                 quantise_f(k)
             if k + 2 < TILES:
                 turn_f(k + 2)
-            ahead(k, 0)
+            if k + 2 == TILES:
+                advance(RUNS[TILES])
+            elif k + 2 < STEPS:
+                ahead(k, 0)

@@ -34,40 +34,46 @@ UNIT = ROWS * WIDE
 BANKS = 8
 LACE = 4
 SILUS = 2
-F_ON_SCALAR = [1, 0, 0, 0, 2, 3, 3, 3]
+F_ON_SCALAR = [1,0,0,0,2,2,2,2]
 GPSIMD_COLUMNS = 304
-SCALAR_BLOCKS = [0] * 8 + [1, 2, 1, 0, 0, 0, 1, 2, 0, 2]
+SCALAR_BLOCKS = [0] * 7 + [2, 1, 2, 1] + [0, 0, 1, 2, 0, 0, 2]
 
 
 def wide_units(n, passes):
     return [[(g, n * WIDE, WIDE)] for g in passes]
 
 
-def half_unit(n0):
-    return [[(g, n0, HALF) for g in range(E_PASSES)]]
+def half_units(n0, passes):
+    return [[(g, n0, HALF), (g + 1, n0, HALF)] for g in passes[::2]]
 
 
 def wide_products(kind, n, tiles):
     return [(kind, n * WIDE, WIDE, m) for m in tiles]
 
 
-def half_products(n0, pairs):
-    return [("a", n0, HALF, 2 * pair) for pair in pairs]
+def half_products(kind, n0, pairs=range(PAIRS)):
+    return [(kind, n0, HALF, 2 * pair) for pair in pairs]
 
 
 A_PASSES, C_PASSES = range(E_PASSES), range(E_PASSES, PASSES)
-UNITS = ([[(0, 0, HALF), (0, HALF, HALF)]] + wide_units(0, A_PASSES[1:]) + half_unit(WIDE) + half_unit(WIDE + HALF) + wide_units(0, C_PASSES)
-         + wide_units(2, A_PASSES) + wide_units(1, C_PASSES) + wide_units(2, C_PASSES))
+LAST = N - HALF
+UNITS = ([[(0, 0, HALF), (0, HALF, HALF)]] + wide_units(0, A_PASSES[1:]) + half_units(WIDE, A_PASSES) + half_units(WIDE + HALF, A_PASSES)
+         + wide_units(0, C_PASSES) + half_units(LAST - HALF, A_PASSES) + wide_units(1, C_PASSES) + half_units(LAST - HALF, C_PASSES)
+         + half_units(LAST, C_PASSES)[:1] + half_units(LAST, A_PASSES) + half_units(LAST, C_PASSES)[1:])
 STEPS = len(UNITS)
+LAST_A = STEPS - 2
 LOW, HIGH = range(PAIRS), range(PAIRS, TILES)
 RUNS = {2: wide_products("a", 0, LOW),
-        3: half_products(WIDE, [0, 1]) + wide_products("a", 0, [4, 5]),
-        4: half_products(WIDE, [2]) + wide_products("a", 0, [6, 7]) + half_products(WIDE, [3]),
-        5: half_products(WIDE + HALF, range(PAIRS)),
-        8: wide_products("c", 0, LOW), 9: wide_products("c", 0, HIGH),
-        10: wide_products("a", 2, LOW), 11: wide_products("a", 2, HIGH),
-        14: wide_products("c", 1, LOW), 15: wide_products("c", 1, HIGH),
-        17: wide_products("c", 2, range(TILES))}
+        3: half_products("a", WIDE, [0, 1]) + wide_products("a", 0, [4, 5]),
+        4: half_products("a", WIDE, [2]) + wide_products("a", 0, [6, 7]) + half_products("a", WIDE, [3]),
+        5: half_products("a", WIDE + HALF),
+        8: wide_products("c", 0, LOW), 9: wide_products("c", 0, HIGH), 10: half_products("a", LAST - HALF),
+        13: wide_products("c", 1, LOW), 14: wide_products("c", 1, HIGH), 15: half_products("c", LAST - HALF),
+        17: half_products("a", LAST) + half_products("c", LAST)}
+
+
+def next_run(k):
+    return min(step for step in RUNS if step > k or step == STEPS - 1)
 
 
 def share(engine, k):
@@ -297,9 +303,6 @@ def tile_drafter_feature_fusion_d2_kernel(tc, e, f_bytes, f_scale, w_bytes, w_sc
                                                 rhs=w[0].bitcast(FP8X4), rhs_scale=w[1],
                                                 start=len(made) == 1, stop=len(made) == count * len(whole))
 
-        def pieces(product):
-            return [slice(0, HALF), slice(HALF, WIDE)] if product == RUNS[STEPS - 1][-1] else [slice(0, WIDE)]
-
         def empty(product):
             kind, n0, width, m0 = product
             number, bank = banks[product]
@@ -308,18 +311,19 @@ def tile_drafter_feature_fusion_d2_kernel(tc, e, f_bytes, f_scale, w_bytes, w_sc
             if kind == "a":
                 nc.vector.tensor_tensor(out=part, in0=bank[:], in1=bias[:, n0:n0 + width].unsqueeze(1).to_broadcast([P, count, width]), op=ADD)
             else:
-                for cols in pieces(product):
-                    nc.vector.scalar_tensor_tensor(out=part[:, 0, cols], in0=bank[:, 0, cols], scalar=trusts[:, m0:m0 + 1],
-                                                   in1=part[:, 0, cols], op0=MULT, op1=ADD)
+                for i in range(count):
+                    nc.vector.scalar_tensor_tensor(out=part[:, i, :], in0=bank[:, i, :], scalar=trusts[:, m0 + i:m0 + i + 1],
+                                                   in1=part[:, i, :], op0=MULT, op1=ADD)
                 finished.append(product)
             free_banks.append(number)
 
         def finish():
-            kind, n0, width, m = product = finished.pop(0)
-            for cols in pieces(product):
-                z = sums[:, n0 // WIDE, m, cols]
+            kind, n0, width, m0 = product = finished.pop(0)
+            stop = m0 + WIDE // width
+            for tiles in ([slice(m0, m0 + 1), slice(m0 + 1, stop)] if product == RUNS[STEPS - 1][-1] else [slice(m0, stop)]):
+                z = sums[:, n0 // WIDE, tiles, n0 % WIDE:n0 % WIDE + width]
                 nc.scalar.activation(out=z, in_=z, func=ACT.Silu)
-                nc.sync.dma_start(out=o_v[:, m, n0 + cols.start:n0 + cols.stop], in_=z)
+                nc.sync.dma_start(out=o_v[:, tiles, n0:n0 + width], in_=z)
 
         def ahead(k, spare):
             for product in [product for step in sorted(RUNS) if step > k for product in RUNS[step]]:
@@ -352,18 +356,27 @@ def tile_drafter_feature_fusion_d2_kernel(tc, e, f_bytes, f_scale, w_bytes, w_sc
                 advance(run)
             for n in range(len(finished) if last else min(len(finished), SILUS)):
                 finish()
-            if not last:
+            if k + 1 == LAST_A:
+                lace("vector", LAST_A)
+            elif not last:
                 lace("vector", k + 1, range(1, WIDE // B))
-            quantise_w(k)
-            if not last:
+            if k != LAST_A:
+                quantise_w(k)
+            if k + 1 == LAST_A:
+                quantise_w(LAST_A)
+                advance(half_products("c", LAST))
+            elif not last:
                 lace("vector", k + 1, range(1))
             if last:
                 advance(run)
-            if (run or k >= TILES) and k + 2 < STEPS:
-                ahead(k, 2 if k + 1 < PAIRS else 0)
-            elif k + 1 == TILES:
-                advance(RUNS[TILES])
-            if k + 1 < PAIRS:
+            elif run and k + 1 < LAST_A:
+                ahead(k, 0)
+            elif not run and k != LAST_A:
+                advance(RUNS[next_run(k)])
+            if k == 1:
+                quantise_e(k)
+                advance(RUNS[k + 1])
+            if k == 0:
                 turn_e(k + 1)
             if k + 2 < STEPS:
                 lace("gpsimd", k + 2)
@@ -372,20 +385,24 @@ def tile_drafter_feature_fusion_d2_kernel(tc, e, f_bytes, f_scale, w_bytes, w_sc
                 scale_f(k + 3, "scalar")
             for product in run:
                 empty(product)
+                if k + 1 == LAST_A:
+                    advance([("a", LAST, HALF, product[3])])
                 if last and product[0] == "c":
                     finish()
             if run and k < PAIRS:
                 quantise_e(k)
-                advance(RUNS[k + 1][:len(free_banks) - 2])
+                advance(RUNS[k + 1])
             if k + 2 < TILES:
                 scale_f(k + 2, "vector")
-            if not run and k < PAIRS:
+            if k == 0:
                 quantise_e(k)
             if k < TILES:
                 quantise_f(k)
+            if 0 < k < PAIRS - 1:
+                turn_e(k + 1)
             if k + 2 < TILES:
                 turn_f(k + 2)
-            if k + 2 == TILES:
-                advance(RUNS[TILES])
-            elif k + 2 < STEPS:
+            if next_run(k) == k + 2 and not run:
+                advance(RUNS[k + 2])
+            elif k + 1 < LAST_A:
                 ahead(k, 0)

@@ -32,11 +32,14 @@ HALF = WIDE // 2
 CHUNKS = N // WIDE
 UNIT = ROWS * WIDE
 BANKS = 8
-LACE = 4
+WORK_BUFFERS = 4
+GPSIMD_COLUMNS = 320
+COVER = 64
+F_SHARE = 2
 SILUS = 2
-F_ON_SCALAR = [1,0,0,0,2,2,2,2]
-GPSIMD_COLUMNS = 304
-SCALAR_BLOCKS = [0] * 7 + [2, 1, 2, 1] + [0, 0, 1, 2, 0, 0, 2]
+VISIT = {"vector": 2, "scalar": 2, "gpsimd": 4}
+PLANE_BUFFERS = 5
+W_BUFFERS = 8
 
 
 def wide_units(n, passes):
@@ -57,28 +60,54 @@ def half_products(kind, n0, pairs=range(PAIRS)):
 
 A_PASSES, C_PASSES = range(E_PASSES), range(E_PASSES, PASSES)
 LAST = N - HALF
-UNITS = ([[(0, 0, HALF), (0, HALF, HALF)]] + wide_units(0, A_PASSES[1:]) + half_units(WIDE, A_PASSES) + half_units(WIDE + HALF, A_PASSES)
+LOW, HIGH = range(PAIRS), range(PAIRS, TILES)
+UNITS = ([[(g, 0, HALF), (g, HALF, HALF)] for g in A_PASSES] + half_units(WIDE, A_PASSES) + half_units(WIDE + HALF, A_PASSES)
          + wide_units(0, C_PASSES) + half_units(LAST - HALF, A_PASSES) + wide_units(1, C_PASSES) + half_units(LAST - HALF, C_PASSES)
          + half_units(LAST, C_PASSES)[:1] + half_units(LAST, A_PASSES) + half_units(LAST, C_PASSES)[1:])
 STEPS = len(UNITS)
 LAST_A = STEPS - 2
-LOW, HIGH = range(PAIRS), range(PAIRS, TILES)
-RUNS = {2: wide_products("a", 0, LOW),
-        3: half_products("a", WIDE, [0, 1]) + wide_products("a", 0, [4, 5]),
-        4: half_products("a", WIDE, [2]) + wide_products("a", 0, [6, 7]) + half_products("a", WIDE, [3]),
-        5: half_products("a", WIDE + HALF),
-        8: wide_products("c", 0, LOW), 9: wide_products("c", 0, HIGH), 10: half_products("a", LAST - HALF),
-        13: wide_products("c", 1, LOW), 14: wide_products("c", 1, HIGH), 15: half_products("c", LAST - HALF),
-        17: half_products("a", LAST) + half_products("c", LAST)}
 
 
-def next_run(k):
-    return min(step for step in RUNS if step > k or step == STEPS - 1)
+def ready(product):
+    kind, n0, width, m0 = product
+    passes = A_PASSES if kind == "a" else C_PASSES
+    last_tile = m0 + WIDE // width - 1
+    return max([k for k, unit in enumerate(UNITS) for g, first, _ in unit if g in passes and first == n0]
+               + [last_tile // 2 if kind == "a" else last_tile])
+
+
+def plan_runs():
+    groups = [wide_products("a", 0, LOW),
+              half_products("a", WIDE, [0, 1]) + wide_products("a", 0, HIGH[:2]),
+              half_products("a", WIDE, [2]) + wide_products("a", 0, HIGH[2:]) + half_products("a", WIDE, [3]),
+              half_products("a", WIDE + HALF), wide_products("c", 0, LOW), wide_products("c", 0, HIGH),
+              half_products("a", LAST - HALF), wide_products("c", 1, LOW), wide_products("c", 1, HIGH),
+              half_products("c", LAST - HALF)]
+    runs = {}
+    step = 0
+    for group in groups:
+        step = 1 + max([step] + [ready(product) for product in group])
+        runs[step] = group
+    runs[STEPS - 1] = half_products("a", LAST) + half_products("c", LAST)
+    return runs
+
+
+RUNS = plan_runs()
+FIRST_C_RUN = min(step for step, group in RUNS.items() if group[0][0] == "c")
+
+
+def f_passes_on_scalar(m):
+    if m < PAIRS:
+        return int(m == 0)
+    return F_SHARE + (PAIRS < m < TILES - 1)
 
 
 def share(engine, k):
-    scalar_end = WIDE - (GPSIMD_COLUMNS if k - 2 in RUNS else 0)
-    vector_end = max(0, scalar_end - B * SCALAR_BLOCKS[k])
+    step = k - 2
+    scalar_end = WIDE - (GPSIMD_COLUMNS if step in RUNS else 0)
+    vector_end = scalar_end
+    if step + 3 >= TILES and (step <= FIRST_C_RUN or step not in RUNS or step + 3 >= STEPS):
+        vector_end = max(COVER if k - 1 in RUNS else 0, scalar_end - (WIDE - GPSIMD_COLUMNS))
     return {"vector": (0, vector_end), "scalar": (vector_end, scalar_end), "gpsimd": (scalar_end, WIDE)}[engine]
 
 
@@ -86,7 +115,7 @@ def tile_drafter_feature_fusion_d2_kernel(tc, e, f_bytes, f_scale, w_bytes, w_sc
     nc = tc.nc
     with ExitStack() as ctx:
         once = ctx.enter_context(tc.tile_pool(name="once", bufs=1))
-        work = ctx.enter_context(tc.tile_pool(name="work", bufs=4))
+        work = ctx.enter_context(tc.tile_pool(name="work", bufs=WORK_BUFFERS))
         psum = ctx.enter_context(tc.psum_pool(name="psum", bufs=1))
 
         w_scale_rows = once.tile([P, PASSES, W_BLOCKS], F32)
@@ -140,21 +169,20 @@ def tile_drafter_feature_fusion_d2_kernel(tc, e, f_bytes, f_scale, w_bytes, w_sc
         load_f(1)
         load_w(0)
         load_w(1)
-        load_e(0)
-        load_f(2)
-        load_e(1)
-        load_w(2)
-        load_f(3)
+        for pair in range(2):
+            load_e(pair)
+            if pair == 1:
+                load_w(2)
+            load_f(pair + 2)
         load_w(3)
-        for m in range(4, TILES):
+        for m in range(PAIRS, TILES):
             load_w(m)
             if m - 2 < PAIRS:
                 load_e(m - 2)
             load_f(m)
-            if m == PAIRS:
-                nc.sync.dma_start(out=bias[:, 0:WIDE], in_=b[0:WIDE].partition_broadcast(P))
-            if m == PAIRS + 1:
-                nc.sync.dma_start(out=bias[:, WIDE:N], in_=b[WIDE:N].partition_broadcast(P))
+            if m - PAIRS < 2:
+                cols = slice(0, WIDE) if m == PAIRS else slice(WIDE, N)
+                nc.sync.dma_start(out=bias[:, cols], in_=b[cols].partition_broadcast(P))
         nc.sync.dma_start(out=trusts[:], in_=trust.rearrange("(p m) o -> p (m o)", m=TILES))
         for k in range(TILES, STEPS):
             load_w(k)
@@ -186,8 +214,11 @@ def tile_drafter_feature_fusion_d2_kernel(tc, e, f_bytes, f_scale, w_bytes, w_sc
                 nc.scalar.activation(out=dst, in_=src, func=ACT.Copy, scale=scale)
 
         def widen_w(k, between=None):
-            tag = "w_planes" if k < 10 else "f_wide" if k < 14 else "turned"
-            planes[k] = work.tile([P, UNIT], BF16, align_bytes=64, name="w_planes", tag=tag, bufs=5 if k < 10 else 4)
+            spent = k - 2 * PLANE_BUFFERS
+            if spent < 0:
+                planes[k] = work.tile([P, UNIT], BF16, align_bytes=64, name="w_planes", bufs=PLANE_BUFFERS)
+            else:
+                planes[k] = work.tile([P, UNIT], BF16, align_bytes=64, name="w_planes", tag="f_wide" if spent < WORK_BUFFERS else "turned")
             for h, (g, n0, width) in enumerate(UNITS[k]):
                 nc.scalar.copy(out=planes[k][:, h * ROWS * width:(h + 1) * ROWS * width],
                                in_=w_raw[(g, n0)][:].rearrange("p t c -> p (t c)").bitcast(FP8))
@@ -197,32 +228,31 @@ def tile_drafter_feature_fusion_d2_kernel(tc, e, f_bytes, f_scale, w_bytes, w_sc
         def lace(engine, k, blocks=range(WIDE // B)):
             if k not in laced:
                 laced[k] = work.tile([P, WIDE, ROWS], BF16, align_bytes=64, name="w_laced", bufs=2)
-            visit = 1 if engine == "scalar" else LACE
             first, stop = share(engine, k)
             for n in blocks:
                 c0, c1 = max(first, B * n), min(stop, B * (n + 1))
                 if c0 < c1:
                     h = c0 // UNITS[k][0][2]
                     g, n0, width = UNITS[k][h]
-                    dst = laced[k][:, c0:c1].rearrange("p (c i) t -> p c t i", i=visit)
+                    dst = laced[k][:, c0:c1].rearrange("p (c i) t -> p c t i", i=VISIT[engine])
                     rows = planes[k][:].rearrange("p (h t c) -> p h t c", t=ROWS, c=width)[:, h]
-                    src = rows[:, :, c0 - h * width:c1 - h * width].rearrange("p t (c i) -> p c t i", i=visit)
+                    src = rows[:, :, c0 - h * width:c1 - h * width].rearrange("p t (c i) -> p c t i", i=VISIT[engine])
                     j = (n0 + c0 - h * width) // B
                     scaled(engine, dst, src, w_scales[:, g, j:j + 1])
 
         def quantise(src, name, bufs):
-            words = D // ROWS
+            words = UNIT // ROWS
             codes = work.tile([P, words], U32, align_bytes=256, name=name + "_codes", bufs=bufs)
             scales = work.tile([P, words], U8, align_bytes=256, name=name + "_scales", bufs=bufs)
             nc.vector.quantize_mx(out=codes[:].bitcast(FP8X4), scales=scales[:], in_=src)
             return codes, scales
 
         def quantise_w(k):
-            codes, scales = quantise(laced[k][:].rearrange("p c t -> p (c t)"), "w", 8)
+            codes, scales = quantise(laced[k][:].rearrange("p c t -> p (c t)"), "w", W_BUFFERS)
             for h, (g, n0, width) in enumerate(UNITS[k]):
                 w_mx[(g, n0)] = (codes[:, h * width:(h + 1) * width], scales[:, h * width:(h + 1) * width])
-            if k == 0:
-                w_mx[(0, 0)] = (codes[:], scales[:])
+            if k < E_PASSES:
+                w_mx[(k, 0)] = (codes[:], scales[:])
 
         f_wide = {}
         turned = {}
@@ -233,7 +263,7 @@ def tile_drafter_feature_fusion_d2_kernel(tc, e, f_bytes, f_scale, w_bytes, w_sc
         def scale_f(m, engine):
             if m not in f_wide:
                 f_wide[m] = work.tile([P, D], BF16, align_bytes=64, name="f_wide")
-            split = (K_PASS // B) * F_ON_SCALAR[m]
+            split = (K_PASS // B) * f_passes_on_scalar(m)
             for j in (range(split) if engine == "scalar" else reversed(range(split, F_BLOCKS))):
                 src = f_raw[m][:, j * B:(j + 1) * B].bitcast(FP8)
                 scale = f_scales[:, m * F_BLOCKS + j:m * F_BLOCKS + j + 1]
@@ -269,7 +299,7 @@ def tile_drafter_feature_fusion_d2_kernel(tc, e, f_bytes, f_scale, w_bytes, w_sc
             turn(e_raw[pair], ("e", pair), 2 * E_PASSES)
 
         def turn_f(m):
-            turn(f_wide[m], ("f", m), F_ON_SCALAR[m])
+            turn(f_wide[m], ("f", m), f_passes_on_scalar(m))
 
         def quantise_e(pair):
             x_mx[("e", pair)] = quantise(turned[("e", pair)][:], "e", PAIRS)
@@ -325,7 +355,8 @@ def tile_drafter_feature_fusion_d2_kernel(tc, e, f_bytes, f_scale, w_bytes, w_sc
                 nc.scalar.activation(out=z, in_=z, func=ACT.Silu)
                 nc.sync.dma_start(out=o_v[:, tiles, n0:n0 + width], in_=z)
 
-        def ahead(k, spare):
+        def ahead(k):
+            spare = 0
             for product in [product for step in sorted(RUNS) if step > k for product in RUNS[step]]:
                 if product not in banks and len(free_banks) <= spare:
                     break
@@ -343,55 +374,38 @@ def tile_drafter_feature_fusion_d2_kernel(tc, e, f_bytes, f_scale, w_bytes, w_sc
         turn_f(1)
         turn_e(0)
 
-        for k in range(STEPS):
+        for k in range(LAST_A - 1):
             run = RUNS.get(k, [])
-            last = k == STEPS - 1
+            next_run = RUNS[min(step for step in RUNS if step > k)]
             if k < E_PASSES:
                 copy_turned()
                 widen_w(k + 2)
-            if 0 < k < STEPS - 3:
+            if k > 0:
                 widen_w(k + 3)
             copy_turned()
-            if not last:
-                advance(run)
-            for n in range(len(finished) if last else min(len(finished), SILUS)):
+            for n in range(min(len(finished), SILUS)):
                 finish()
-            if k + 1 == LAST_A:
-                lace("vector", LAST_A)
-            elif not last:
-                lace("vector", k + 1, range(1, WIDE // B))
-            if k != LAST_A:
-                quantise_w(k)
-            if k + 1 == LAST_A:
-                quantise_w(LAST_A)
-                advance(half_products("c", LAST))
-            elif not last:
-                lace("vector", k + 1, range(1))
-            if last:
-                advance(run)
-            elif run and k + 1 < LAST_A:
-                ahead(k, 0)
-            elif not run and k != LAST_A:
-                advance(RUNS[next_run(k)])
+            lace("vector", k + 1, range(1, WIDE // B))
+            quantise_w(k)
+            lace("vector", k + 1, range(1))
+            if run:
+                ahead(k)
+            else:
+                advance(next_run)
+            if k == 0:
+                turn_e(1)
             if k == 1:
                 quantise_e(k)
-                advance(RUNS[k + 1])
-            if k == 0:
-                turn_e(k + 1)
-            if k + 2 < STEPS:
-                lace("gpsimd", k + 2)
-                lace("scalar", k + 2)
+                advance(next_run)
+            lace("gpsimd", k + 2)
+            lace("scalar", k + 2)
             if k + 3 < TILES:
                 scale_f(k + 3, "scalar")
             for product in run:
                 empty(product)
-                if k + 1 == LAST_A:
-                    advance([("a", LAST, HALF, product[3])])
-                if last and product[0] == "c":
-                    finish()
-            if run and k < PAIRS:
+            if 1 < k < PAIRS:
                 quantise_e(k)
-                advance(RUNS[k + 1])
+                advance(next_run)
             if k + 2 < TILES:
                 scale_f(k + 2, "vector")
             if k == 0:
@@ -402,7 +416,27 @@ def tile_drafter_feature_fusion_d2_kernel(tc, e, f_bytes, f_scale, w_bytes, w_sc
                 turn_e(k + 1)
             if k + 2 < TILES:
                 turn_f(k + 2)
-            if next_run(k) == k + 2 and not run:
-                advance(RUNS[k + 2])
-            elif k + 1 < LAST_A:
-                ahead(k, 0)
+            if run or k + 1 in RUNS:
+                ahead(k)
+            else:
+                advance(next_run)
+
+        for n in range(SILUS):
+            finish()
+        lace("vector", LAST_A)
+        quantise_w(LAST_A - 1)
+        quantise_w(LAST_A)
+        advance(half_products("c", LAST))
+        lace("gpsimd", STEPS - 1)
+        lace("scalar", STEPS - 1)
+        for product, following in zip(RUNS[LAST_A - 1], half_products("a", LAST)):
+            empty(product)
+            advance([following])
+        while finished:
+            finish()
+        quantise_w(STEPS - 1)
+        advance(RUNS[STEPS - 1])
+        for product in RUNS[STEPS - 1]:
+            empty(product)
+            if finished:
+                finish()

@@ -33,9 +33,9 @@ CHUNKS = N // WIDE
 UNIT = ROWS * WIDE
 BANKS = 8
 WORK_BUFFERS = 4
-GPSIMD_COLUMNS = 320
-COVER = 64
-F_SHARE = 2
+GPSIMD_COLUMNS = 304
+COVER = 96
+F_SHARE = 1
 SILUS = 2
 VISIT = {"vector": 2, "scalar": 2, "gpsimd": 4}
 PLANE_BUFFERS = 5
@@ -106,7 +106,7 @@ def share(engine, k):
     step = k - 2
     scalar_end = WIDE - (GPSIMD_COLUMNS if step in RUNS else 0)
     vector_end = scalar_end
-    if step + 3 >= TILES and (step <= FIRST_C_RUN or step not in RUNS or step + 3 >= STEPS):
+    if min(RUNS) <= step <= FIRST_C_RUN or (step > FIRST_C_RUN and (step not in RUNS or step + 3 >= STEPS)):
         vector_end = max(COVER if k - 1 in RUNS else 0, scalar_end - (WIDE - GPSIMD_COLUMNS))
     return {"vector": (0, vector_end), "scalar": (vector_end, scalar_end), "gpsimd": (scalar_end, WIDE)}[engine]
 
@@ -408,10 +408,10 @@ def tile_drafter_feature_fusion_d2_kernel(tc, e, f_bytes, f_scale, w_bytes, w_sc
                 advance(next_run)
             if k + 2 < TILES:
                 scale_f(k + 2, "vector")
-            if k == 0:
-                quantise_e(k)
             if k < TILES:
                 quantise_f(k)
+            if k == 0:
+                quantise_e(k)
             if 0 < k < PAIRS - 1:
                 turn_e(k + 1)
             if k + 2 < TILES:

@@ -33,10 +33,9 @@ CHUNKS = N // WIDE
 UNIT = ROWS * WIDE
 BANKS = 8
 WORK_BUFFERS = 4
-GPSIMD_COLUMNS = 304
-COVER = 96
+GPSIMD_COLUMNS = 288
 F_SHARE = 1
-SILUS = 2
+SILUS = 3
 VISIT = {"vector": 2, "scalar": 2, "gpsimd": 4}
 PLANE_BUFFERS = 5
 W_BUFFERS = 8
@@ -61,54 +60,49 @@ def half_products(kind, n0, pairs=range(PAIRS)):
 A_PASSES, C_PASSES = range(E_PASSES), range(E_PASSES, PASSES)
 LAST = N - HALF
 LOW, HIGH = range(PAIRS), range(PAIRS, TILES)
-UNITS = ([[(g, 0, HALF), (g, HALF, HALF)] for g in A_PASSES] + half_units(WIDE, A_PASSES) + half_units(WIDE + HALF, A_PASSES)
-         + wide_units(0, C_PASSES) + half_units(LAST - HALF, A_PASSES) + wide_units(1, C_PASSES) + half_units(LAST - HALF, C_PASSES)
-         + half_units(LAST, C_PASSES)[:1] + half_units(LAST, A_PASSES) + half_units(LAST, C_PASSES)[1:])
+UNITS = ([[(g, 0, HALF), (g, HALF, HALF)] for g in A_PASSES] + half_units(WIDE, A_PASSES) + wide_units(0, C_PASSES)
+         + half_units(WIDE + HALF, A_PASSES) + wide_units(1, C_PASSES) + wide_units(2, A_PASSES)
+         + half_units(LAST - HALF, C_PASSES) + half_units(LAST, C_PASSES))
 STEPS = len(UNITS)
-LAST_A = STEPS - 2
+RUNS = [wide_products("a", 0, LOW),
+        half_products("a", WIDE, [0, 1]) + wide_products("a", 0, HIGH[:2]),
+        half_products("a", WIDE, [2]) + wide_products("a", 0, HIGH[2:]) + half_products("a", WIDE, [3]),
+        wide_products("c", 0, LOW), wide_products("c", 0, HIGH), half_products("a", WIDE + HALF),
+        wide_products("c", 1, LOW), wide_products("c", 1, HIGH), wide_products("a", 2, LOW), wide_products("a", 2, HIGH),
+        half_products("c", LAST - HALF), half_products("c", LAST)]
+FIRST_C = min(n for n, run in enumerate(RUNS) if run[0][0] == "c")
+BANK = {product: j + BANKS // 2 * (max(0, n - FIRST_C) % 2) for n, run in enumerate(RUNS) for j, product in enumerate(run)}
 
 
-def ready(product):
+def last_unit(product):
     kind, n0, width, m0 = product
-    passes = A_PASSES if kind == "a" else C_PASSES
-    last_tile = m0 + WIDE // width - 1
-    return max([k for k, unit in enumerate(UNITS) for g, first, _ in unit if g in passes and first == n0]
-               + [last_tile // 2 if kind == "a" else last_tile])
+    return max(k for k, unit in enumerate(UNITS) for g, first, _ in unit if g in (A_PASSES if kind == "a" else C_PASSES) and first == n0)
 
 
-def plan_runs():
-    groups = [wide_products("a", 0, LOW),
-              half_products("a", WIDE, [0, 1]) + wide_products("a", 0, HIGH[:2]),
-              half_products("a", WIDE, [2]) + wide_products("a", 0, HIGH[2:]) + half_products("a", WIDE, [3]),
-              half_products("a", WIDE + HALF), wide_products("c", 0, LOW), wide_products("c", 0, HIGH),
-              half_products("a", LAST - HALF), wide_products("c", 1, LOW), wide_products("c", 1, HIGH),
-              half_products("c", LAST - HALF)]
-    runs = {}
-    step = 0
-    for group in groups:
-        step = 1 + max([step] + [ready(product) for product in group])
-        runs[step] = group
-    runs[STEPS - 1] = half_products("a", LAST) + half_products("c", LAST)
-    return runs
+def plan_beats():
+    beats = []
+    stop = 0
+    for run in RUNS:
+        first, stop = stop, min(STEPS, max([stop + 1] + [last_unit(product) + 2 for product in run]))
+        beats.append(range(first, stop))
+    return beats
 
 
-RUNS = plan_runs()
-FIRST_C_RUN = min(step for step, group in RUNS.items() if group[0][0] == "c")
+BEATS = plan_beats()
+HELPED = [beat[0] for beat in BEATS[1:]]
+GATED = HELPED + [k - 1 for k in HELPED]
+SCALAR_FROM = BEATS[2][0]
+KEPT = 1
 
 
 def f_passes_on_scalar(m):
-    if m < PAIRS:
-        return int(m == 0)
-    return F_SHARE + (PAIRS < m < TILES - 1)
+    return int(m == 0) if m < PAIRS else F_SHARE
 
 
 def share(engine, k):
-    step = k - 2
-    scalar_end = WIDE - (GPSIMD_COLUMNS if step in RUNS else 0)
-    vector_end = scalar_end
-    if min(RUNS) <= step <= FIRST_C_RUN or (step > FIRST_C_RUN and (step not in RUNS or step + 3 >= STEPS)):
-        vector_end = max(COVER if k - 1 in RUNS else 0, scalar_end - (WIDE - GPSIMD_COLUMNS))
-    return {"vector": (0, vector_end), "scalar": (vector_end, scalar_end), "gpsimd": (scalar_end, WIDE)}[engine]
+    gpsimd_first = WIDE - (0 if k not in HELPED else GPSIMD_COLUMNS if k < STEPS - 1 else HALF)
+    scalar_end = 0 if k < SCALAR_FROM else B if k in HELPED or k < TILES else HALF
+    return {"scalar": (0, scalar_end), "vector": (scalar_end, gpsimd_first), "gpsimd": (gpsimd_first, WIDE)}[engine]
 
 
 def tile_drafter_feature_fusion_d2_kernel(tc, e, f_bytes, f_scale, w_bytes, w_scale, trust, b, out):
@@ -188,15 +182,16 @@ def tile_drafter_feature_fusion_d2_kernel(tc, e, f_bytes, f_scale, w_bytes, w_sc
             load_w(k)
 
         free_banks = list(range(BANKS))
+        to_turn = list(range(PAIRS + TILES))
 
-        def take_bank(shape):
-            number = free_banks.pop(0)
+        def take_bank(shape, number):
+            free_banks.remove(number)
             return number, psum.tile(shape, F32, name="bank%d" % number)
 
         w_scales = once.tile([P, PASSES, W_BLOCKS], F32)
 
         def spread_w_scale():
-            number, bank = take_bank([P, PASSES * W_BLOCKS])
+            number, bank = take_bank([P, PASSES * W_BLOCKS], 0)
             nc.tensor.matmul(bank[:], lhsT=quadrants[:], rhs=w_scale_rows[:].rearrange("p g j -> p (g j)"), start=True, stop=True)
             nc.scalar.copy(out=w_scales[:].rearrange("p g j -> p (g j)"), in_=bank[:])
             free_banks.append(number)
@@ -226,29 +221,38 @@ def tile_drafter_feature_fusion_d2_kernel(tc, e, f_bytes, f_scale, w_bytes, w_sc
                     between()
 
         def lace(engine, k, blocks=range(WIDE // B)):
-            if k not in laced:
-                laced[k] = work.tile([P, WIDE, ROWS], BF16, align_bytes=64, name="w_laced", bufs=2)
             first, stop = share(engine, k)
-            for n in blocks:
+            for n in ([3, 1, 2] if engine == "gpsimd" else range(WIDE // B) if k < E_PASSES else reversed(range(WIDE // B))):
                 c0, c1 = max(first, B * n), min(stop, B * (n + 1))
-                if c0 < c1:
+                if c0 < c1 and n in blocks:
+                    half = c0 // HALF
+                    if (k, half) not in laced:
+                        name, bufs = ("w_low", 3) if half == 0 else ("w_gate", 1) if k in GATED else ("w_high", 2)
+                        laced[(k, half)] = work.tile([P, HALF, ROWS], BF16, align_bytes=64, name=name, bufs=bufs)
                     h = c0 // UNITS[k][0][2]
                     g, n0, width = UNITS[k][h]
-                    dst = laced[k][:, c0:c1].rearrange("p (c i) t -> p c t i", i=VISIT[engine])
+                    dst = laced[(k, half)][:, c0 - half * HALF:c1 - half * HALF].rearrange("p (c i) t -> p c t i", i=VISIT[engine])
                     rows = planes[k][:].rearrange("p (h t c) -> p h t c", t=ROWS, c=width)[:, h]
                     src = rows[:, :, c0 - h * width:c1 - h * width].rearrange("p t (c i) -> p c t i", i=VISIT[engine])
                     j = (n0 + c0 - h * width) // B
                     scaled(engine, dst, src, w_scales[:, g, j:j + 1])
 
+        def mx_tiles(name, bufs):
+            codes = work.tile([P, WIDE], U32, align_bytes=256, name=name + "_codes", bufs=bufs)
+            scales = work.tile([P, WIDE], U8, align_bytes=256, name=name + "_scales", bufs=bufs)
+            return codes, scales
+
         def quantise(src, name, bufs):
-            words = UNIT // ROWS
-            codes = work.tile([P, words], U32, align_bytes=256, name=name + "_codes", bufs=bufs)
-            scales = work.tile([P, words], U8, align_bytes=256, name=name + "_scales", bufs=bufs)
+            codes, scales = mx_tiles(name, bufs)
             nc.vector.quantize_mx(out=codes[:].bitcast(FP8X4), scales=scales[:], in_=src)
             return codes, scales
 
         def quantise_w(k):
-            codes, scales = quantise(laced[k][:].rearrange("p c t -> p (c t)"), "w", W_BUFFERS)
+            codes, scales = mx_tiles("w", W_BUFFERS)
+            for half in range(2):
+                cols = slice(half * HALF, (half + 1) * HALF)
+                nc.vector.quantize_mx(out=codes[:, cols].bitcast(FP8X4), scales=scales[:, cols],
+                                      in_=laced[(k, half)][:].rearrange("p c t -> p (c t)"))
             for h, (g, n0, width) in enumerate(UNITS[k]):
                 w_mx[(g, n0)] = (codes[:, h * width:(h + 1) * width], scales[:, h * width:(h + 1) * width])
             if k < E_PASSES:
@@ -276,8 +280,9 @@ def tile_drafter_feature_fusion_d2_kernel(tc, e, f_bytes, f_scale, w_bytes, w_sc
 
         def turn(src, key, unsorted):
             words = src[:].bitcast(F32)
+            first_bank = BANKS // 2 + 2 * (to_turn.pop(0) % 2)
             for half in range(2):
-                number, bank = take_bank([P, 2, 2, P])
+                number, bank = take_bank([P, 2, 2, P], first_bank + half)
                 for h in range(2):
                     g = 2 * half + h
                     first = words_a_pass * g
@@ -310,9 +315,10 @@ def tile_drafter_feature_fusion_d2_kernel(tc, e, f_bytes, f_scale, w_bytes, w_sc
         banks = {}
         done = {}
         finished = []
+        emptied = []
         sums = once.tile([P, CHUNKS, TILES, WIDE], F32)
 
-        def advance(group):
+        def advance(group, stop=PASSES):
             for product in group:
                 kind, n0, width, m0 = product
                 count = WIDE // width
@@ -323,9 +329,9 @@ def tile_drafter_feature_fusion_d2_kernel(tc, e, f_bytes, f_scale, w_bytes, w_sc
                     key = ("e", m // 2) if kind == "a" else ("f", m)
                     x_first = E_PASSES * (m % 2) if kind == "a" else -E_PASSES
                     for g in whole:
-                        if key in x_mx and (g, n0) in w_mx and (i, g) not in made:
+                        if key in x_mx and (g, n0) in w_mx and (i, g) not in made and g < stop:
                             if product not in banks:
-                                banks[product] = take_bank([P, count, width])
+                                banks[product] = take_bank([P, count, width], BANK[product])
                             made.append((i, g))
                             x_cols = slice((x_first + g) * P, (x_first + g + 1) * P)
                             x, w = x_mx[key], w_mx[(g, n0)]
@@ -336,6 +342,7 @@ def tile_drafter_feature_fusion_d2_kernel(tc, e, f_bytes, f_scale, w_bytes, w_sc
         def empty(product):
             kind, n0, width, m0 = product
             number, bank = banks[product]
+            emptied.append(product)
             count = WIDE // width
             part = sums[:, n0 // WIDE, m0:m0 + count, n0 % WIDE:n0 % WIDE + width]
             if kind == "a":
@@ -350,18 +357,22 @@ def tile_drafter_feature_fusion_d2_kernel(tc, e, f_bytes, f_scale, w_bytes, w_sc
         def finish():
             kind, n0, width, m0 = product = finished.pop(0)
             stop = m0 + WIDE // width
-            for tiles in ([slice(m0, m0 + 1), slice(m0 + 1, stop)] if product == RUNS[STEPS - 1][-1] else [slice(m0, stop)]):
+            for tiles in ([slice(m0, m0 + 1), slice(m0 + 1, stop)] if product == RUNS[-1][-1] else [slice(m0, stop)]):
                 z = sums[:, n0 // WIDE, tiles, n0 % WIDE:n0 % WIDE + width]
                 nc.scalar.activation(out=z, in_=z, func=ACT.Silu)
                 nc.sync.dma_start(out=o_v[:, tiles, n0:n0 + width], in_=z)
 
-        def ahead(k):
-            spare = 0
-            for product in [product for step in sorted(RUNS) if step > k for product in RUNS[step]]:
-                if product not in banks and len(free_banks) <= spare:
+        def ahead():
+            for product in [product for run in RUNS for product in run if product not in emptied]:
+                kind, n0, width, m0 = product
+                number = BANK[product]
+                turns_to_come = [n for n in to_turn if BANKS // 2 + 2 * (n % 2) == number - number % 2]
+                if product not in banks and (number not in free_banks or turns_to_come):
                     break
-                advance([product])
-                spare = spare + (product not in banks)
+                waits = kind == "c" and width == WIDE and m0 in HIGH and (PASSES - 1, n0) not in w_mx
+                advance([product], PASSES - 2 if waits else PASSES)
+                if product not in banks:
+                    break
 
         scale_f(0, "scalar")
         widen_w(0, spread_w_scale)
@@ -373,70 +384,85 @@ def tile_drafter_feature_fusion_d2_kernel(tc, e, f_bytes, f_scale, w_bytes, w_sc
         lace("vector", 0)
         turn_f(1)
         turn_e(0)
+        copy_turned()
+        widen_w(2)
+        lace("vector", 1)
+        quantise_w(0)
+        turn_e(1)
+        scale_f(2, "vector")
+        quantise_w(1)
+        quantise_f(0)
+        quantise_e(0)
+        copy_turned()
+        turn_f(2)
+        ahead()
+        widen_w(3)
+        scale_f(3, "vector")
+        lace("vector", 2)
+        quantise_e(1)
+        ahead()
+        copy_turned()
+        turn_e(2)
+        turn_f(3)
+        widen_w(4)
+        scale_f(PAIRS, "scalar")
+        lace("vector", HELPED[0], range(1))
+        quantise_f(1)
 
-        for k in range(LAST_A - 1):
-            run = RUNS.get(k, [])
-            next_run = RUNS[min(step for step in RUNS if step > k)]
-            if k < E_PASSES:
+        late_f = [HIGH[:1], HIGH[1:3], HIGH[3:]]
+        to_widen = list(range(5, STEPS))
+        to_lace = list(range(SCALAR_FROM, STEPS))
+        to_quantise = list(range(2, TILES))
+
+        def scalar_prepares(k):
+            while to_widen and to_widen[0] <= k + 1:
+                widen_w(to_widen.pop(0))
+            while to_lace and to_lace[0] <= k:
+                lace("scalar", to_lace.pop(0))
+
+        for n, (beat, run) in enumerate(zip(BEATS, RUNS)):
+            for k in beat[E_PASSES:] if n == 0 else beat:
                 copy_turned()
-                widen_w(k + 2)
-            if k > 0:
-                widen_w(k + 3)
-            copy_turned()
-            for n in range(min(len(finished), SILUS)):
+                quantise_w(k)
+                ahead()
+                if k + 1 < STEPS:
+                    lace("vector", k + 1, range(k + 1 == HELPED[0], WIDE // B))
+                if n == FIRST_C and to_quantise:
+                    quantise_f(to_quantise.pop(0))
+                    ahead()
+                scalar_prepares(k + 2)
+                if n >= FIRST_C - 1 and to_widen:
+                    widen_w(to_widen.pop(0))
+            if run == RUNS[-1]:
+                break
+            lace("gpsimd", k + 1)
+            if n + 1 < len(late_f):
+                for m in late_f[n + 1]:
+                    scale_f(m, "scalar")
+            for j in range(min(len(finished), SILUS * (len(BEATS[n + 1]) == 1))):
                 finish()
-            lace("vector", k + 1, range(1, WIDE // B))
-            quantise_w(k)
-            lace("vector", k + 1, range(1))
-            if run:
-                ahead(k)
-            else:
-                advance(next_run)
-            if k == 0:
-                turn_e(1)
-            if k == 1:
-                quantise_e(k)
-                advance(next_run)
-            lace("gpsimd", k + 2)
-            lace("scalar", k + 2)
-            if k + 3 < TILES:
-                scale_f(k + 3, "scalar")
-            for product in run:
+            for product in run[:len(run) - KEPT * (run == RUNS[-2])]:
                 empty(product)
-            if 1 < k < PAIRS:
-                quantise_e(k)
-                advance(next_run)
-            if k + 2 < TILES:
-                scale_f(k + 2, "vector")
-            if k < TILES:
-                quantise_f(k)
-            if k == 0:
-                quantise_e(k)
-            if 0 < k < PAIRS - 1:
-                turn_e(k + 1)
-            if k + 2 < TILES:
-                turn_f(k + 2)
-            if run or k + 1 in RUNS:
-                ahead(k)
-            else:
-                advance(next_run)
+                ahead()
+            if n < len(late_f):
+                scale_f(late_f[n][0], "vector")
+                if n < E_PASSES:
+                    quantise_e(n + 2)
+                if n == 0:
+                    ahead()
+                    turn_e(PAIRS - 1)
+                turn_f(late_f[n][0])
+                ahead()
+                for m in late_f[n][1:]:
+                    scale_f(m, "vector")
+                    turn_f(m)
+                for j in range(1 + n // 2):
+                    quantise_f(to_quantise.pop(0))
+                ahead()
 
-        for n in range(SILUS):
-            finish()
-        lace("vector", LAST_A)
-        quantise_w(LAST_A - 1)
-        quantise_w(LAST_A)
-        advance(half_products("c", LAST))
-        lace("gpsimd", STEPS - 1)
-        lace("scalar", STEPS - 1)
-        for product, following in zip(RUNS[LAST_A - 1], half_products("a", LAST)):
-            empty(product)
-            advance([following])
         while finished:
             finish()
-        quantise_w(STEPS - 1)
-        advance(RUNS[STEPS - 1])
-        for product in RUNS[STEPS - 1]:
+        for product in RUNS[-2][len(RUNS[-2]) - KEPT:] + RUNS[-1]:
             empty(product)
-            if finished:
-                finish()
+            ahead()
+            finish()

@@ -35,7 +35,7 @@ BANKS = 8
 WORK_BUFFERS = 4
 GPSIMD_COLUMNS = 288
 F_SHARE = 1
-SILUS = 3
+SILUS = 2
 VISIT = {"vector": 2, "scalar": 2, "gpsimd": 4}
 PLANE_BUFFERS = 5
 W_BUFFERS = 8
@@ -96,7 +96,7 @@ KEPT = 1
 
 
 def f_passes_on_scalar(m):
-    return int(m == 0) if m < PAIRS else F_SHARE
+    return int(m == 0) if m < PAIRS else F_SHARE + (m < PAIRS + 2)
 
 
 def share(engine, k):
@@ -142,9 +142,13 @@ def tile_drafter_feature_fusion_d2_kernel(tc, e, f_bytes, f_scale, w_bytes, w_sc
         f_raw = {}
 
         def load_w(k):
-            for g, n0, width in UNITS[k]:
-                w_raw[(g, n0)] = once.tile([P, ROWS, width], U8, name="w_raw%d_%d" % (g, n0))
-                nc.sync.dma_start(out=w_raw[(g, n0)][:], in_=w_v[:, g, :, n0:n0 + width])
+            for h, (g, n0, width) in enumerate(UNITS[k]):
+                part = h if k < E_PASSES else 0
+                if part == h or h == 0:
+                    w_raw[(k, part)] = once.tile([P, UNIT // (1 + (k < E_PASSES))], U8, name="w_raw%d_%d" % (k, part))
+                first = (h - part) * ROWS * width
+                nc.sync.dma_start(out=w_raw[(k, part)][:, first:first + ROWS * width].rearrange("p (t c) -> p t c", t=ROWS),
+                                  in_=w_v[:, g, :, n0:n0 + width])
 
         def load_e(pair):
             raw = once.tile([P, 2 * E], BF16, name="e_raw%d" % pair)
@@ -214,10 +218,10 @@ def tile_drafter_feature_fusion_d2_kernel(tc, e, f_bytes, f_scale, w_bytes, w_sc
                 planes[k] = work.tile([P, UNIT], BF16, align_bytes=64, name="w_planes", bufs=PLANE_BUFFERS)
             else:
                 planes[k] = work.tile([P, UNIT], BF16, align_bytes=64, name="w_planes", tag="f_wide" if spent < WORK_BUFFERS else "turned")
-            for h, (g, n0, width) in enumerate(UNITS[k]):
-                nc.scalar.copy(out=planes[k][:, h * ROWS * width:(h + 1) * ROWS * width],
-                               in_=w_raw[(g, n0)][:].rearrange("p t c -> p (t c)").bitcast(FP8))
-                if between and h == 0:
+            parts = 1 + (k < E_PASSES)
+            for part in range(parts):
+                nc.scalar.copy(out=planes[k][:, part * UNIT // parts:(part + 1) * UNIT // parts], in_=w_raw[(k, part)][:].bitcast(FP8))
+                if between and part == 0:
                     between()
 
         def lace(engine, k, blocks=range(WIDE // B)):
@@ -324,16 +328,16 @@ def tile_drafter_feature_fusion_d2_kernel(tc, e, f_bytes, f_scale, w_bytes, w_sc
                 count = WIDE // width
                 whole = list(A_PASSES if kind == "a" else C_PASSES)
                 made = done.setdefault(product, [])
-                for i in range(count):
-                    m = m0 + i
-                    key = ("e", m // 2) if kind == "a" else ("f", m)
-                    x_first = E_PASSES * (m % 2) if kind == "a" else -E_PASSES
-                    for g in whole:
+                for g in whole:
+                    for i in range(count):
+                        m = m0 + i
+                        key = ("e", m // 2) if kind == "a" else ("f", m)
                         if key in x_mx and (g, n0) in w_mx and (i, g) not in made and g < stop:
                             if product not in banks:
                                 banks[product] = take_bank([P, count, width], BANK[product])
                             made.append((i, g))
-                            x_cols = slice((x_first + g) * P, (x_first + g + 1) * P)
+                            x_first = g + (E_PASSES * (m % 2) if kind == "a" else -E_PASSES)
+                            x_cols = slice(x_first * P, (x_first + 1) * P)
                             x, w = x_mx[key], w_mx[(g, n0)]
                             nc.tensor.matmul_mx(out=banks[product][1][:, i, :], lhsT=x[0][:, x_cols].bitcast(FP8X4), lhsT_scale=x[1][:, x_cols],
                                                 rhs=w[0].bitcast(FP8X4), rhs_scale=w[1],
@@ -354,9 +358,11 @@ def tile_drafter_feature_fusion_d2_kernel(tc, e, f_bytes, f_scale, w_bytes, w_sc
                 finished.append(product)
             free_banks.append(number)
 
-        def finish():
+        def finish(count=1):
             kind, n0, width, m0 = product = finished.pop(0)
-            stop = m0 + WIDE // width
+            stop = m0 + count * WIDE // width
+            if count == 2:
+                finished.pop(0)
             for tiles in ([slice(m0, m0 + 1), slice(m0 + 1, stop)] if product == RUNS[-1][-1] else [slice(m0, stop)]):
                 z = sums[:, n0 // WIDE, tiles, n0 % WIDE:n0 % WIDE + width]
                 nc.scalar.activation(out=z, in_=z, func=ACT.Silu)
@@ -439,11 +445,13 @@ def tile_drafter_feature_fusion_d2_kernel(tc, e, f_bytes, f_scale, w_bytes, w_sc
             if n + 1 < len(late_f):
                 for m in late_f[n + 1]:
                     scale_f(m, "scalar")
-            for j in range(min(len(finished), SILUS * (len(BEATS[n + 1]) == 1))):
-                finish()
+            for j in range(min(len(finished) // 2, SILUS * (len(BEATS[n + 1]) == 1) * (1 + (run == RUNS[-2])))):
+                finish(2)
             for product in run[:len(run) - KEPT * (run == RUNS[-2])]:
                 empty(product)
                 ahead()
+                if run == RUNS[-2]:
+                    finish()
             if n < len(late_f):
                 scale_f(late_f[n][0], "vector")
                 if n < E_PASSES:
@@ -460,8 +468,6 @@ def tile_drafter_feature_fusion_d2_kernel(tc, e, f_bytes, f_scale, w_bytes, w_sc
                     quantise_f(to_quantise.pop(0))
                 ahead()
 
-        while finished:
-            finish()
         for product in RUNS[-2][len(RUNS[-2]) - KEPT:] + RUNS[-1]:
             empty(product)
             ahead()

@@ -33,10 +33,11 @@ CHUNKS = N // WIDE
 UNIT = ROWS * WIDE
 BANKS = 8
 WORK_BUFFERS = 4
-GPSIMD_COLUMNS = 288
+GPSIMD_COLUMNS = 320
+COVER = 96
 F_SHARE = 1
 SILUS = 2
-VISIT = {"vector": 2, "scalar": 2, "gpsimd": 4}
+VISIT = {"vector": 2, "scalar": 2, "gpsimd": 1}
 PLANE_BUFFERS = 5
 W_BUFFERS = 8
 
@@ -96,13 +97,16 @@ KEPT = 1
 
 
 def f_passes_on_scalar(m):
-    return int(m == 0) if m < PAIRS else F_SHARE + (m < PAIRS + 2)
+    return int(m == 0) if m < PAIRS else F_SHARE + (m != TILES - 2)
 
 
 def share(engine, k):
-    gpsimd_first = WIDE - (0 if k not in HELPED else GPSIMD_COLUMNS if k < STEPS - 1 else HALF)
-    scalar_end = 0 if k < SCALAR_FROM else B if k in HELPED or k < TILES else HALF
-    return {"scalar": (0, scalar_end), "vector": (scalar_end, gpsimd_first), "gpsimd": (gpsimd_first, WIDE)}[engine]
+    if k in HELPED:
+        gpsimd_first = WIDE - (GPSIMD_COLUMNS if k < STEPS - 1 else HALF)
+        vector_end = gpsimd_first if k < SCALAR_FROM else COVER if k < STEPS - 1 else B
+        return {"vector": (0, vector_end), "scalar": (vector_end, gpsimd_first), "gpsimd": (gpsimd_first, WIDE)}[engine]
+    scalar_end = 0 if k < SCALAR_FROM else B if k < TILES else HALF
+    return {"scalar": (0, scalar_end), "vector": (scalar_end, WIDE), "gpsimd": (WIDE, WIDE)}[engine]
 
 
 def tile_drafter_feature_fusion_d2_kernel(tc, e, f_bytes, f_scale, w_bytes, w_scale, trust, b, out):

@@ -33,11 +33,11 @@ CHUNKS = N // WIDE
 UNIT = ROWS * WIDE
 BANKS = 8
 WORK_BUFFERS = 4
-GPSIMD_COLUMNS = 320
+GPSIMD_COLUMNS = 304
 COVER = 96
 F_SHARE = 1
 SILUS = 2
-VISIT = {"vector": 2, "scalar": 2, "gpsimd": 1}
+VISIT = {"vector": 4, "scalar": 4, "gpsimd": 1}
 PLANE_BUFFERS = 5
 W_BUFFERS = 8
 

@@ -33,12 +33,12 @@ CHUNKS = N // WIDE
 UNIT = ROWS * WIDE
 BANKS = 8
 WORK_BUFFERS = 4
-GPSIMD_COLUMNS = 304
-COVER = 96
+GPSIMD_COLUMNS = 320
 F_SHARE = 1
 SILUS = 2
 VISIT = {"vector": 4, "scalar": 4, "gpsimd": 1}
 PLANE_BUFFERS = 5
+TURNED_BUFFERS = 5
 W_BUFFERS = 8
 
 
@@ -97,16 +97,20 @@ KEPT = 1
 
 
 def f_passes_on_scalar(m):
-    return int(m == 0) if m < PAIRS else F_SHARE + (m != TILES - 2)
+    return int(m == 0) if m < PAIRS else F_SHARE + (m < PAIRS + 2)
 
 
 def share(engine, k):
+    owners = ["vector", "vector" if k < SCALAR_FROM else "scalar", "vector", "vector"]
     if k in HELPED:
-        gpsimd_first = WIDE - (GPSIMD_COLUMNS if k < STEPS - 1 else HALF)
-        vector_end = gpsimd_first if k < SCALAR_FROM else COVER if k < STEPS - 1 else B
-        return {"vector": (0, vector_end), "scalar": (vector_end, gpsimd_first), "gpsimd": (gpsimd_first, WIDE)}[engine]
-    scalar_end = 0 if k < SCALAR_FROM else B if k < TILES else HALF
-    return {"scalar": (0, scalar_end), "vector": (scalar_end, WIDE), "gpsimd": (WIDE, WIDE)}[engine]
+        owners[2:] = ["gpsimd", "gpsimd"]
+    elif k >= TILES:
+        owners[0] = "scalar"
+    runs = [(B * n, B * (n + 1), owners[n]) for n in range(WIDE // B)]
+    if k in HELPED[:-1]:
+        cover = B + HALF - GPSIMD_COLUMNS
+        runs = [(0, cover, "vector"), runs[1], runs[3], (cover, B, "gpsimd"), runs[2]]
+    return [(c0, c1) for c0, c1, owner in runs if owner == engine]
 
 
 def tile_drafter_feature_fusion_d2_kernel(tc, e, f_bytes, f_scale, w_bytes, w_scale, trust, b, out):
@@ -134,6 +138,8 @@ def tile_drafter_feature_fusion_d2_kernel(tc, e, f_bytes, f_scale, w_bytes, w_sc
         o_v = out.rearrange("(p m) n -> p m n", m=TILES)
         w_v = w_bytes.rearrange("(g p t) n -> p g t n", p=P, t=ROWS)
 
+        w_rows = w_bytes.rearrange("(g r) n -> r g n", g=PASSES)
+
         f_scales = once.tile([P, TILES * F_BLOCKS], F32)
         nc.scalar.dma_start(out=f_scales[:], in_=f_scale.rearrange("(p m) j -> p (m j)", m=TILES))
         nc.scalar.dma_start(out=w_scale_rows[0:P:QUADRANT], in_=w_scale.rearrange("(g q) j -> q g j", q=P // QUADRANT))
@@ -146,16 +152,18 @@ def tile_drafter_feature_fusion_d2_kernel(tc, e, f_bytes, f_scale, w_bytes, w_sc
         f_raw = {}
 
         def load_w(k):
-            for h, (g, n0, width) in enumerate(UNITS[k]):
-                part = h if k < E_PASSES else 0
-                if part == h or h == 0:
-                    w_raw[(k, part)] = once.tile([P, UNIT // (1 + (k < E_PASSES))], U8, name="w_raw%d_%d" % (k, part))
-                first = (h - part) * ROWS * width
-                nc.sync.dma_start(out=w_raw[(k, part)][:, first:first + ROWS * width].rearrange("p (t c) -> p t c", t=ROWS),
-                                  in_=w_v[:, g, :, n0:n0 + width])
+            g, n0, width = UNITS[k][0]
+            if k < E_PASSES:
+                for part in range(2):
+                    w_raw[(k, part)] = once.tile([P, ROWS, HALF], U8, name="w_raw%d_%d" % (k, part))
+                    nc.sync.dma_start(out=w_raw[(k, part)][:], in_=w_v[:, g, :, part * HALF:(part + 1) * HALF])
+            else:
+                w_raw[(k, 0)] = once.tile([P, ROWS, WIDE // width, width], U8, name="w_raw%d" % k)
+                nc.sync.dma_start(out=w_raw[(k, 0)][:].rearrange("p t h c -> p (t h) c"),
+                                  in_=w_rows[:, g:g + WIDE // width, n0:n0 + width])
 
         def load_e(pair):
-            raw = once.tile([P, 2 * E], BF16, name="e_raw%d" % pair)
+            raw = once.tile([P, 2 * E], BF16, align_bytes=64, name="e_raw%d" % pair)
             nc.sync.dma_start(out=raw[:], in_=e_v[:, 2 * pair:2 * pair + 2, :].rearrange("p m k -> p (m k)"))
             e_raw[pair] = raw
 
@@ -207,6 +215,7 @@ def tile_drafter_feature_fusion_d2_kernel(tc, e, f_bytes, f_scale, w_bytes, w_sc
         planes = {}
         laced = {}
         w_mx = {}
+        spent_e = [e_raw[pair][:, n * WIDE:(n + 1) * WIDE].rearrange("p (c t) -> p c t", t=ROWS) for pair in range(PAIRS) for n in range(2 * E // WIDE)]
 
         def scaled(engine, dst, src, scale):
             if engine == "vector":
@@ -216,34 +225,39 @@ def tile_drafter_feature_fusion_d2_kernel(tc, e, f_bytes, f_scale, w_bytes, w_sc
             else:
                 nc.scalar.activation(out=dst, in_=src, func=ACT.Copy, scale=scale)
 
+        def flat(raw):
+            return raw[:].rearrange("p t c -> p (t c)" if len(raw.shape) == 3 else "p t h c -> p (t h c)")
+
         def widen_w(k, between=None):
             spent = k - 2 * PLANE_BUFFERS
             if spent < 0:
                 planes[k] = work.tile([P, UNIT], BF16, align_bytes=64, name="w_planes", bufs=PLANE_BUFFERS)
             else:
-                planes[k] = work.tile([P, UNIT], BF16, align_bytes=64, name="w_planes", tag="f_wide" if spent < WORK_BUFFERS else "turned")
+                tag, bufs = ("f_wide", WORK_BUFFERS) if spent < WORK_BUFFERS else ("turned", TURNED_BUFFERS)
+                planes[k] = work.tile([P, UNIT], BF16, align_bytes=64, name="w_planes", tag=tag, bufs=bufs)
             parts = 1 + (k < E_PASSES)
             for part in range(parts):
-                nc.scalar.copy(out=planes[k][:, part * UNIT // parts:(part + 1) * UNIT // parts], in_=w_raw[(k, part)][:].bitcast(FP8))
+                nc.scalar.copy(out=planes[k][:, part * UNIT // parts:(part + 1) * UNIT // parts], in_=flat(w_raw[(k, part)]).bitcast(FP8))
                 if between and part == 0:
                     between()
 
         def lace(engine, k, blocks=range(WIDE // B)):
-            first, stop = share(engine, k)
-            for n in ([3, 1, 2] if engine == "gpsimd" else range(WIDE // B) if k < E_PASSES else reversed(range(WIDE // B))):
-                c0, c1 = max(first, B * n), min(stop, B * (n + 1))
-                if c0 < c1 and n in blocks:
-                    half = c0 // HALF
-                    if (k, half) not in laced:
-                        name, bufs = ("w_low", 3) if half == 0 else ("w_gate", 1) if k in GATED else ("w_high", 2)
-                        laced[(k, half)] = work.tile([P, HALF, ROWS], BF16, align_bytes=64, name=name, bufs=bufs)
-                    h = c0 // UNITS[k][0][2]
-                    g, n0, width = UNITS[k][h]
-                    dst = laced[(k, half)][:, c0 - half * HALF:c1 - half * HALF].rearrange("p (c i) t -> p c t i", i=VISIT[engine])
-                    rows = planes[k][:].rearrange("p (h t c) -> p h t c", t=ROWS, c=width)[:, h]
-                    src = rows[:, :, c0 - h * width:c1 - h * width].rearrange("p t (c i) -> p c t i", i=VISIT[engine])
-                    j = (n0 + c0 - h * width) // B
-                    scaled(engine, dst, src, w_scales[:, g, j:j + 1])
+            for c0, c1 in share(engine, k):
+                if c0 // B in blocks:
+                    part = min(c0 // B, 2)
+                    if engine == "scalar":
+                        laced[(k, part)] = spent_e.pop(0)
+                    elif (k, part) not in laced:
+                        name, bufs = [("w_first", 2), ("w_second", 2), ("w_gate", 1) if k in GATED else ("w_upper", 2)][part]
+                        laced[(k, part)] = work.tile([P, B if part < 2 else HALF, ROWS], BF16, align_bytes=64, name=name, bufs=bufs)[:]
+                    g, n0, width = UNITS[k][c0 // UNITS[k][0][2]]
+                    dst = laced[(k, part)][:, c0 - part * B:c1 - part * B].rearrange("p (c i) t -> p c t i", i=VISIT[engine])
+                    if k < E_PASSES:
+                        rows = planes[k][:].rearrange("p (h t c) -> p h t c", t=ROWS, c=HALF)[:, c0 // HALF, :, c0 % HALF:c0 % HALF + c1 - c0]
+                    else:
+                        rows = planes[k][:].rearrange("p (t c) -> p t c", t=ROWS)[:, :, c0:c1]
+                    j = (n0 + c0 % width) // B
+                    scaled(engine, dst, rows.rearrange("p t (c i) -> p c t i", i=VISIT[engine]), w_scales[:, g, j:j + 1])
 
         def mx_tiles(name, bufs):
             codes = work.tile([P, WIDE], U32, align_bytes=256, name=name + "_codes", bufs=bufs)
@@ -257,10 +271,10 @@ def tile_drafter_feature_fusion_d2_kernel(tc, e, f_bytes, f_scale, w_bytes, w_sc
 
         def quantise_w(k):
             codes, scales = mx_tiles("w", W_BUFFERS)
-            for half in range(2):
-                cols = slice(half * HALF, (half + 1) * HALF)
+            for part in ((1, 2, 0) if k + 1 in HELPED else (1, 0, 2)):
+                cols = slice(part * B, (part + 1) * B if part < 2 else WIDE)
                 nc.vector.quantize_mx(out=codes[:, cols].bitcast(FP8X4), scales=scales[:, cols],
-                                      in_=laced[(k, half)][:].rearrange("p c t -> p (c t)"))
+                                      in_=laced[(k, part)].rearrange("p c t -> p (c t)"))
             for h, (g, n0, width) in enumerate(UNITS[k]):
                 w_mx[(g, n0)] = (codes[:, h * width:(h + 1) * width], scales[:, h * width:(h + 1) * width])
             if k < E_PASSES:
@@ -303,7 +317,7 @@ def tile_drafter_feature_fusion_d2_kernel(tc, e, f_bytes, f_scale, w_bytes, w_sc
             while in_psum:
                 key, half, number, bank = in_psum.pop(0)
                 if half == 0:
-                    turned[key] = work.tile([P, D], BF16, align_bytes=64, name="turned")
+                    turned[key] = work.tile([P, D], BF16, align_bytes=64, name="turned", bufs=TURNED_BUFFERS)
                 dst = turned[key][:, D // 2 * half:D // 2 * (half + 1)].bitcast(F32).rearrange("p (h r u) -> p h r u", h=2, u=2)
                 nc.scalar.copy(out=dst, in_=bank[:].rearrange("p h u r -> p h r u"))
                 free_banks.append(number)
@@ -367,10 +381,14 @@ def tile_drafter_feature_fusion_d2_kernel(tc, e, f_bytes, f_scale, w_bytes, w_sc
             stop = m0 + count * WIDE // width
             if count == 2:
                 finished.pop(0)
-            for tiles in ([slice(m0, m0 + 1), slice(m0 + 1, stop)] if product == RUNS[-1][-1] else [slice(m0, stop)]):
-                z = sums[:, n0 // WIDE, tiles, n0 % WIDE:n0 % WIDE + width]
-                nc.scalar.activation(out=z, in_=z, func=ACT.Silu)
-                nc.sync.dma_start(out=o_v[:, tiles, n0:n0 + width], in_=z)
+            whole = [slice(m0, stop)]
+            by_tile = [slice(m, m + 1) for m in range(m0, stop)]
+            z = sums[:, n0 // WIDE, :, n0 % WIDE:n0 % WIDE + width]
+            for tiles in (by_tile if product in RUNS[-1] else whole):
+                nc.scalar.activation(out=z[:, tiles], in_=z[:, tiles], func=ACT.Silu)
+                if product == RUNS[-1][-1] or tiles.stop == stop:
+                    stored = tiles if product == RUNS[-1][-1] else whole[0]
+                    nc.sync.dma_start(out=o_v[:, stored, n0:n0 + width], in_=z[:, stored])
 
         def ahead():
             for product in [product for run in RUNS for product in run if product not in emptied]:
@@ -416,7 +434,7 @@ def tile_drafter_feature_fusion_d2_kernel(tc, e, f_bytes, f_scale, w_bytes, w_sc
         turn_f(3)
         widen_w(4)
         scale_f(PAIRS, "scalar")
-        lace("vector", HELPED[0], range(1))
+        lace("vector", HELPED[0], range(1, 2))
         quantise_f(1)
 
         late_f = [HIGH[:1], HIGH[1:3], HIGH[3:]]
@@ -436,7 +454,7 @@ def tile_drafter_feature_fusion_d2_kernel(tc, e, f_bytes, f_scale, w_bytes, w_sc
                 quantise_w(k)
                 ahead()
                 if k + 1 < STEPS:
-                    lace("vector", k + 1, range(k + 1 == HELPED[0], WIDE // B))
+                    lace("vector", k + 1, range(1) if k + 1 in HELPED else range(WIDE // B))
                 if n == FIRST_C and to_quantise:
                     quantise_f(to_quantise.pop(0))
                     ahead()

@@ -51,11 +51,11 @@ def half_units(n0, passes):
 
 
 def wide_products(kind, n, tiles):
-    return [(kind, n * WIDE, WIDE, m) for m in tiles]
+    return [(kind, n * WIDE, WIDE, range(m, m + 1)) for m in tiles]
 
 
 def half_products(kind, n0, pairs=range(PAIRS)):
-    return [(kind, n0, HALF, 2 * pair) for pair in pairs]
+    return [(kind, n0, HALF, range(2 * pair, 2 * pair + 2)) for pair in pairs]
 
 
 A_PASSES, C_PASSES = range(E_PASSES), range(E_PASSES, PASSES)
@@ -70,13 +70,14 @@ RUNS = [wide_products("a", 0, LOW),
         half_products("a", WIDE, [2]) + wide_products("a", 0, HIGH[2:]) + half_products("a", WIDE, [3]),
         wide_products("c", 0, LOW), wide_products("c", 0, HIGH), half_products("a", WIDE + HALF),
         wide_products("c", 1, LOW), wide_products("c", 1, HIGH), wide_products("a", 2, LOW), wide_products("a", 2, HIGH),
-        half_products("c", LAST - HALF), half_products("c", LAST)]
+        half_products("c", LAST - HALF),
+        half_products("c", LAST, range(PAIRS - 1)) + [("c", LAST, HALF, range(m, m + 1)) for m in HIGH[2:]]]
 FIRST_C = min(n for n, run in enumerate(RUNS) if run[0][0] == "c")
 BANK = {product: j + BANKS // 2 * (max(0, n - FIRST_C) % 2) for n, run in enumerate(RUNS) for j, product in enumerate(run)}
 
 
 def last_unit(product):
-    kind, n0, width, m0 = product
+    kind, n0, width, tiles = product
     return max(k for k, unit in enumerate(UNITS) for g, first, _ in unit if g in (A_PASSES if kind == "a" else C_PASSES) and first == n0)
 
 
@@ -91,6 +92,7 @@ def plan_beats():
 
 BEATS = plan_beats()
 HELPED = [beat[0] for beat in BEATS[1:]]
+LAST_UNHELPED = max(set(range(STEPS)) - set(HELPED))
 GATED = HELPED + [k - 1 for k in HELPED]
 SCALAR_FROM = BEATS[2][0]
 KEPT = 1
@@ -104,7 +106,7 @@ def share(engine, k):
     owners = ["vector", "vector" if k < SCALAR_FROM else "scalar", "vector", "vector"]
     if k in HELPED:
         owners[2:] = ["gpsimd", "gpsimd"]
-    elif k >= TILES:
+    elif k == LAST_UNHELPED:
         owners[0] = "scalar"
     runs = [(B * n, B * (n + 1), owners[n]) for n in range(WIDE // B)]
     if k in HELPED[:-1]:
@@ -271,7 +273,7 @@ def tile_drafter_feature_fusion_d2_kernel(tc, e, f_bytes, f_scale, w_bytes, w_sc
 
         def quantise_w(k):
             codes, scales = mx_tiles("w", W_BUFFERS)
-            for part in ((1, 2, 0) if k + 1 in HELPED else (1, 0, 2)):
+            for part in ((1, 2, 0) if k + 1 in HELPED[:-1] else (1, 0, 2)):
                 cols = slice(part * B, (part + 1) * B if part < 2 else WIDE)
                 nc.vector.quantize_mx(out=codes[:, cols].bitcast(FP8X4), scales=scales[:, cols],
                                       in_=laced[(k, part)].rearrange("p c t -> p (c t)"))
@@ -342,78 +344,93 @@ def tile_drafter_feature_fusion_d2_kernel(tc, e, f_bytes, f_scale, w_bytes, w_sc
 
         def advance(group, stop=PASSES):
             for product in group:
-                kind, n0, width, m0 = product
-                count = WIDE // width
+                kind, n0, width, tiles = product
                 whole = list(A_PASSES if kind == "a" else C_PASSES)
                 made = done.setdefault(product, [])
                 for g in whole:
-                    for i in range(count):
-                        m = m0 + i
+                    for i, m in enumerate(tiles):
                         key = ("e", m // 2) if kind == "a" else ("f", m)
                         if key in x_mx and (g, n0) in w_mx and (i, g) not in made and g < stop:
                             if product not in banks:
-                                banks[product] = take_bank([P, count, width], BANK[product])
+                                banks[product] = take_bank([P, len(tiles), width], BANK[product])
                             made.append((i, g))
                             x_first = g + (E_PASSES * (m % 2) if kind == "a" else -E_PASSES)
                             x_cols = slice(x_first * P, (x_first + 1) * P)
                             x, w = x_mx[key], w_mx[(g, n0)]
                             nc.tensor.matmul_mx(out=banks[product][1][:, i, :], lhsT=x[0][:, x_cols].bitcast(FP8X4), lhsT_scale=x[1][:, x_cols],
                                                 rhs=w[0].bitcast(FP8X4), rhs_scale=w[1],
-                                                start=len(made) == 1, stop=len(made) == count * len(whole))
+                                                start=len(made) == 1, stop=len(made) == len(tiles) * len(whole))
 
         def empty(product):
-            kind, n0, width, m0 = product
+            kind, n0, width, tiles = product
             number, bank = banks[product]
             emptied.append(product)
-            count = WIDE // width
-            part = sums[:, n0 // WIDE, m0:m0 + count, n0 % WIDE:n0 % WIDE + width]
+            part = sums[:, n0 // WIDE, tiles.start:tiles.stop, n0 % WIDE:n0 % WIDE + width]
             if kind == "a":
-                nc.vector.tensor_tensor(out=part, in0=bank[:], in1=bias[:, n0:n0 + width].unsqueeze(1).to_broadcast([P, count, width]), op=ADD)
+                nc.vector.tensor_tensor(out=part, in0=bank[:], in1=bias[:, n0:n0 + width].unsqueeze(1).to_broadcast([P, len(tiles), width]), op=ADD)
             else:
-                for i in range(count):
-                    nc.vector.scalar_tensor_tensor(out=part[:, i, :], in0=bank[:, i, :], scalar=trusts[:, m0 + i:m0 + i + 1],
+                for i, m in enumerate(tiles):
+                    nc.vector.scalar_tensor_tensor(out=part[:, i, :], in0=bank[:, i, :], scalar=trusts[:, m:m + 1],
                                                    in1=part[:, i, :], op0=MULT, op1=ADD)
                 finished.append(product)
             free_banks.append(number)
 
         def finish(count=1):
-            kind, n0, width, m0 = product = finished.pop(0)
-            stop = m0 + count * WIDE // width
+            kind, n0, width, tiles = product = finished.pop(0)
+            whole = slice(tiles.start, tiles.start + count * len(tiles))
             if count == 2:
                 finished.pop(0)
-            whole = [slice(m0, stop)]
-            by_tile = [slice(m, m + 1) for m in range(m0, stop)]
             z = sums[:, n0 // WIDE, :, n0 % WIDE:n0 % WIDE + width]
-            for tiles in (by_tile if product in RUNS[-1] else whole):
-                nc.scalar.activation(out=z[:, tiles], in_=z[:, tiles], func=ACT.Silu)
-                if product == RUNS[-1][-1] or tiles.stop == stop:
-                    stored = tiles if product == RUNS[-1][-1] else whole[0]
-                    nc.sync.dma_start(out=o_v[:, stored, n0:n0 + width], in_=z[:, stored])
+            for part in ([slice(m, m + 1) for m in tiles] if product in RUNS[-1] else [whole]):
+                nc.scalar.activation(out=z[:, part], in_=z[:, part], func=ACT.Silu)
+            nc.sync.dma_start(out=o_v[:, whole, n0:n0 + width], in_=z[:, whole])
 
         def ahead():
             for product in [product for run in RUNS for product in run if product not in emptied]:
-                kind, n0, width, m0 = product
+                kind, n0, width, tiles = product
                 number = BANK[product]
                 turns_to_come = [n for n in to_turn if BANKS // 2 + 2 * (n % 2) == number - number % 2]
                 if product not in banks and (number not in free_banks or turns_to_come):
                     break
-                waits = kind == "c" and width == WIDE and m0 in HIGH and (PASSES - 1, n0) not in w_mx
+                waits = kind == "c" and width == WIDE and tiles.start in HIGH and (PASSES - 1, n0) not in w_mx
                 advance([product], PASSES - 2 if waits else PASSES)
                 if product not in banks:
                     break
 
+        to_widen = list(range(STEPS))
+        to_lace = list(range(SCALAR_FROM, STEPS))
+
+        def widen_up_to(k):
+            while to_widen and to_widen[0] <= k:
+                widen_w(to_widen.pop(0))
+
+        def scalar_laces_up_to(k):
+            while to_lace and to_lace[0] <= k:
+                lace("scalar", to_lace.pop(0))
+
+        def step(k):
+            quantise_w(k)
+            ahead()
+            if k + 1 < STEPS:
+                lace("vector", k + 1, range(1) if k + 1 in HELPED else range(WIDE // B))
+
+        def empty_all(products):
+            for product in products:
+                empty(product)
+                ahead()
+
         scale_f(0, "scalar")
-        widen_w(0, spread_w_scale)
+        widen_w(to_widen.pop(0), spread_w_scale)
         scale_f(0, "vector")
         turn_f(0)
         scale_f(1, "vector")
-        widen_w(1)
+        widen_up_to(1)
         copy_turned()
         lace("vector", 0)
         turn_f(1)
         turn_e(0)
         copy_turned()
-        widen_w(2)
+        widen_up_to(2)
         lace("vector", 1)
         quantise_w(0)
         turn_e(1)
@@ -422,75 +439,90 @@ def tile_drafter_feature_fusion_d2_kernel(tc, e, f_bytes, f_scale, w_bytes, w_sc
         quantise_f(0)
         quantise_e(0)
         copy_turned()
-        turn_f(2)
         ahead()
-        widen_w(3)
+        turn_f(2)
+        widen_up_to(3)
         scale_f(3, "vector")
         lace("vector", 2)
         quantise_e(1)
         ahead()
+        widen_up_to(4)
         copy_turned()
         turn_e(2)
-        turn_f(3)
-        widen_w(4)
-        scale_f(PAIRS, "scalar")
-        lace("vector", HELPED[0], range(1, 2))
+        scale_f(4, "scalar")
+        lace("vector", 3, range(1, 2))
         quantise_f(1)
 
-        late_f = [HIGH[:1], HIGH[1:3], HIGH[3:]]
-        to_widen = list(range(5, STEPS))
-        to_lace = list(range(SCALAR_FROM, STEPS))
-        to_quantise = list(range(2, TILES))
+        copy_turned()
+        step(2)
+        widen_up_to(5)
+        scalar_laces_up_to(4)
+        lace("gpsimd", 3)
+        scale_f(5, "scalar")
+        empty_all(RUNS[0][:2])
+        turn_e(3)
+        copy_turned()
+        empty_all(RUNS[0][2:])
+        scale_f(4, "vector")
+        quantise_e(2)
+        ahead()
+        turn_f(3)
+        quantise_f(2)
 
-        def scalar_prepares(k):
-            while to_widen and to_widen[0] <= k + 1:
-                widen_w(to_widen.pop(0))
-            while to_lace and to_lace[0] <= k:
-                lace("scalar", to_lace.pop(0))
+        copy_turned()
+        scale_f(6, "scalar")
+        step(3)
+        widen_up_to(6)
+        lace("gpsimd", 4)
+        empty_all(RUNS[1][:1])
+        turn_f(4)
+        copy_turned()
+        scalar_laces_up_to(5)
+        scale_f(7, "scalar")
+        empty_all(RUNS[1][1:])
+        quantise_e(3)
+        scale_f(5, "vector")
+        advance(RUNS[2][1:3])
+        turn_f(5)
+        ahead()
+        scale_f(6, "vector")
+        turn_f(6)
+        quantise_f(3)
 
-        for n, (beat, run) in enumerate(zip(BEATS, RUNS)):
-            for k in beat[E_PASSES:] if n == 0 else beat:
-                copy_turned()
-                quantise_w(k)
-                ahead()
-                if k + 1 < STEPS:
-                    lace("vector", k + 1, range(1) if k + 1 in HELPED else range(WIDE // B))
-                if n == FIRST_C and to_quantise:
+        copy_turned()
+        step(4)
+        widen_up_to(7)
+        scalar_laces_up_to(6)
+        widen_up_to(8)
+        lace("gpsimd", 5)
+        empty_all(RUNS[2])
+        scale_f(7, "vector")
+        turn_f(7)
+        quantise_f(4)
+        quantise_f(5)
+        ahead()
+        copy_turned()
+
+        to_quantise = list(HIGH[2:])
+        for n in range(FIRST_C, len(RUNS)):
+            run = RUNS[n]
+            for k in BEATS[n]:
+                step(k)
+                if to_quantise:
                     quantise_f(to_quantise.pop(0))
                     ahead()
-                scalar_prepares(k + 2)
-                if n >= FIRST_C - 1 and to_widen:
-                    widen_w(to_widen.pop(0))
+                scalar_laces_up_to(k + 2)
+                widen_up_to(k + 4)
             if run == RUNS[-1]:
                 break
             lace("gpsimd", k + 1)
-            if n + 1 < len(late_f):
-                for m in late_f[n + 1]:
-                    scale_f(m, "scalar")
             for j in range(min(len(finished) // 2, SILUS * (len(BEATS[n + 1]) == 1) * (1 + (run == RUNS[-2])))):
                 finish(2)
             for product in run[:len(run) - KEPT * (run == RUNS[-2])]:
-                empty(product)
-                ahead()
+                empty_all([product])
                 if run == RUNS[-2]:
                     finish()
-            if n < len(late_f):
-                scale_f(late_f[n][0], "vector")
-                if n < E_PASSES:
-                    quantise_e(n + 2)
-                if n == 0:
-                    ahead()
-                    turn_e(PAIRS - 1)
-                turn_f(late_f[n][0])
-                ahead()
-                for m in late_f[n][1:]:
-                    scale_f(m, "vector")
-                    turn_f(m)
-                for j in range(1 + n // 2):
-                    quantise_f(to_quantise.pop(0))
-                ahead()
 
         for product in RUNS[-2][len(RUNS[-2]) - KEPT:] + RUNS[-1]:
-            empty(product)
-            ahead()
+            empty_all([product])
             finish()

@@ -99,7 +99,7 @@ KEPT = 1
 
 
 def f_passes_on_scalar(m):
-    return int(m == 0) if m < PAIRS else F_SHARE + (m < PAIRS + 2)
+    return int(m == 0) if m < PAIRS else F_SHARE + (m < TILES - 1)
 
 
 def share(engine, k):

@@ -377,13 +377,14 @@ def tile_drafter_feature_fusion_d2_kernel(tc, e, f_bytes, f_scale, w_bytes, w_sc
 
         def finish(count=1):
             kind, n0, width, tiles = product = finished.pop(0)
-            whole = slice(tiles.start, tiles.start + count * len(tiles))
+            stop = tiles.start + count * len(tiles)
             if count == 2:
                 finished.pop(0)
             z = sums[:, n0 // WIDE, :, n0 % WIDE:n0 % WIDE + width]
-            for part in ([slice(m, m + 1) for m in tiles] if product in RUNS[-1] else [whole]):
+            for part in ([slice(m, m + 1) for m in tiles] if product in RUNS[-1] else [slice(tiles.start, stop)]):
                 nc.scalar.activation(out=z[:, part], in_=z[:, part], func=ACT.Silu)
-            nc.sync.dma_start(out=o_v[:, whole, n0:n0 + width], in_=z[:, whole])
+            if stop % 2 == 0:
+                nc.sync.dma_start(out=o_v[:, stop - 2:stop, n0:n0 + width], in_=z[:, stop - 2:stop])
 
         def ahead():
             for product in [product for run in RUNS for product in run if product not in emptied]:

from contextlib import ExitStack

import concourse.mybir as mybir
from concourse.masks import make_identity

T, E, D, N = 1024, 1024, 2048, 1536
FLOPS = 2 * T * (E + D) * N

F32 = mybir.dt.float32
BF16 = mybir.dt.bfloat16
U32 = mybir.dt.uint32
U8 = mybir.dt.uint8
FP8 = mybir.dt.float8_e4m3fn
FP8X4 = mybir.dt.float8_e4m3fn_x4
ADD = mybir.AluOpType.add
MULT = mybir.AluOpType.mult
ACT = mybir.ActivationFunctionType

P = 128
B = 128
ROWS = 4
K_PASS = P * ROWS
QUADRANT = 32
TILES = T // P
PAIRS = TILES // 2
PASSES = (E + D) // K_PASS
E_PASSES = E // K_PASS
F_BLOCKS = D // B
W_BLOCKS = N // B
WIDE = 512
HALF = WIDE // 2
CHUNKS = N // WIDE
UNIT = ROWS * WIDE
BANKS = 8
WORK_BUFFERS = 4
GPSIMD_COLUMNS = 320
F_SHARE = 1
SILUS = 2
VISIT = {"vector": 4, "scalar": 4, "gpsimd": 1}
PLANE_BUFFERS = 5
TURNED_BUFFERS = 5
W_BUFFERS = 8


def wide_units(n, passes):
    return [[(g, n * WIDE, WIDE)] for g in passes]


def half_units(n0, passes):
    return [[(g, n0, HALF), (g + 1, n0, HALF)] for g in passes[::2]]


def wide_products(kind, n, tiles):
    return [(kind, n * WIDE, WIDE, range(m, m + 1)) for m in tiles]


def half_products(kind, n0, pairs=range(PAIRS)):
    return [(kind, n0, HALF, range(2 * pair, 2 * pair + 2)) for pair in pairs]


A_PASSES, C_PASSES = range(E_PASSES), range(E_PASSES, PASSES)
LAST = N - HALF
LOW, HIGH = range(PAIRS), range(PAIRS, TILES)
UNITS = ([[(g, 0, HALF), (g, HALF, HALF)] for g in A_PASSES] + half_units(WIDE, A_PASSES) + wide_units(0, C_PASSES)
         + half_units(WIDE + HALF, A_PASSES) + wide_units(1, C_PASSES) + wide_units(2, A_PASSES)
         + half_units(LAST - HALF, C_PASSES) + half_units(LAST, C_PASSES))
STEPS = len(UNITS)
RUNS = [wide_products("a", 0, LOW),
        half_products("a", WIDE, [0, 1]) + wide_products("a", 0, HIGH[:2]),
        half_products("a", WIDE, [2]) + wide_products("a", 0, HIGH[2:]) + half_products("a", WIDE, [3]),
        wide_products("c", 0, LOW), wide_products("c", 0, HIGH), half_products("a", WIDE + HALF),
        wide_products("c", 1, LOW), wide_products("c", 1, HIGH), wide_products("a", 2, LOW), wide_products("a", 2, HIGH),
        half_products("c", LAST - HALF),
        half_products("c", LAST, range(PAIRS - 1)) + [("c", LAST, HALF, range(m, m + 1)) for m in HIGH[2:]]]
FIRST_C = min(n for n, run in enumerate(RUNS) if run[0][0] == "c")
BANK = {product: j + BANKS // 2 * (max(0, n - FIRST_C) % 2) for n, run in enumerate(RUNS) for j, product in enumerate(run)}


def last_unit(product):
    kind, n0, width, tiles = product
    return max(k for k, unit in enumerate(UNITS) for g, first, _ in unit if g in (A_PASSES if kind == "a" else C_PASSES) and first == n0)


def plan_beats():
    beats = []
    stop = 0
    for run in RUNS:
        first, stop = stop, min(STEPS, max([stop + 1] + [last_unit(product) + 2 for product in run]))
        beats.append(range(first, stop))
    return beats


BEATS = plan_beats()
HELPED = [beat[0] for beat in BEATS[1:]]
LAST_UNHELPED = max(set(range(STEPS)) - set(HELPED))
GATED = HELPED + [k - 1 for k in HELPED]
SCALAR_FROM = BEATS[2][0]
KEPT = 1


def f_passes_on_scalar(m):
    return int(m == 0) if m < PAIRS else F_SHARE + (m < TILES - 1)


def share(engine, k):
    owners = ["vector", "vector" if k < SCALAR_FROM else "scalar", "vector", "vector"]
    if k in HELPED:
        owners[2:] = ["gpsimd", "gpsimd"]
    elif k == LAST_UNHELPED:
        owners[0] = "scalar"
    runs = [(B * n, B * (n + 1), owners[n]) for n in range(WIDE // B)]
    if k in HELPED[:-1]:
        cover = B + HALF - GPSIMD_COLUMNS
        runs = [(0, cover, "vector"), runs[1], runs[3], (cover, B, "gpsimd"), runs[2]]
    return [(c0, c1) for c0, c1, owner in runs if owner == engine]


def tile_drafter_feature_fusion_d2_kernel(tc, e, f_bytes, f_scale, w_bytes, w_scale, trust, b, out):
    nc = tc.nc
    with ExitStack() as ctx:
        once = ctx.enter_context(tc.tile_pool(name="once", bufs=1))
        work = ctx.enter_context(tc.tile_pool(name="work", bufs=WORK_BUFFERS))
        psum = ctx.enter_context(tc.psum_pool(name="psum", bufs=1))

        w_scale_rows = once.tile([P, PASSES, W_BLOCKS], F32)
        nc.vector.memset(w_scale_rows[:], 0.0)
        ctx.enter_context(tc.manual_schedule())
        ident = once.tile([P, P], F32)
        nc.vector.memset(ident[:], 0.0)
        make_identity(nc, ident[:], nomemset=True)
        zero = once.tile([P, 1], F32)
        nc.vector.memset(zero[:], 0.0)
        quadrants = once.tile([P, P], F32)
        nc.vector.memset(quadrants[:], 0.0)
        for q in range(P // QUADRANT):
            nc.vector.memset(quadrants[QUADRANT * q:QUADRANT * (q + 1), QUADRANT * q:QUADRANT * (q + 1)], 1.0)

        e_v = e.rearrange("(p m) k -> p m k", m=TILES)
        f_v = f_bytes.rearrange("(p m) k -> p m k", m=TILES)
        o_v = out.rearrange("(p m) n -> p m n", m=TILES)
        w_v = w_bytes.rearrange("(g p t) n -> p g t n", p=P, t=ROWS)

        w_rows = w_bytes.rearrange("(g r) n -> r g n", g=PASSES)

        f_scales = once.tile([P, TILES * F_BLOCKS], F32)
        nc.scalar.dma_start(out=f_scales[:], in_=f_scale.rearrange("(p m) j -> p (m j)", m=TILES))
        nc.scalar.dma_start(out=w_scale_rows[0:P:QUADRANT], in_=w_scale.rearrange("(g q) j -> q g j", q=P // QUADRANT))

        warm = once.tile([P, 1], F32)
        nc.scalar.activation(out=warm[:], in_=zero[:], func=ACT.Silu)

        w_raw = {}
        e_raw = {}
        f_raw = {}

        def load_w(k):
            g, n0, width = UNITS[k][0]
            if k < E_PASSES:
                for part in range(2):
                    w_raw[(k, part)] = once.tile([P, ROWS, HALF], U8, name="w_raw%d_%d" % (k, part))
                    nc.sync.dma_start(out=w_raw[(k, part)][:], in_=w_v[:, g, :, part * HALF:(part + 1) * HALF])
            else:
                w_raw[(k, 0)] = once.tile([P, ROWS, WIDE // width, width], U8, name="w_raw%d" % k)
                nc.sync.dma_start(out=w_raw[(k, 0)][:].rearrange("p t h c -> p (t h) c"),
                                  in_=w_rows[:, g:g + WIDE // width, n0:n0 + width])

        def load_e(pair):
            raw = once.tile([P, 2 * E], BF16, align_bytes=64, name="e_raw%d" % pair)
            nc.sync.dma_start(out=raw[:], in_=e_v[:, 2 * pair:2 * pair + 2, :].rearrange("p m k -> p (m k)"))
            e_raw[pair] = raw

        def load_f(m):
            raw = once.tile([P, D], U8, name="f_raw%d" % m)
            for cols in ([slice(D // 2, D), slice(0, D // 2)] if m == 0 else [slice(0, D)]):
                nc.sync.dma_start(out=raw[:, cols], in_=f_v[:, m, cols])
            f_raw[m] = raw

        bias = once.tile([P, N], BF16)
        trusts = once.tile([P, TILES], BF16)
        load_f(0)
        load_f(1)
        load_w(0)
        load_w(1)
        for pair in range(2):
            load_e(pair)
            if pair == 1:
                load_w(2)
            load_f(pair + 2)
        load_w(3)
        for m in range(PAIRS, TILES):
            load_w(m)
            if m - 2 < PAIRS:
                load_e(m - 2)
            load_f(m)
            if m - PAIRS < 2:
                cols = slice(0, WIDE) if m == PAIRS else slice(WIDE, N)
                nc.sync.dma_start(out=bias[:, cols], in_=b[cols].partition_broadcast(P))
        nc.sync.dma_start(out=trusts[:], in_=trust.rearrange("(p m) o -> p (m o)", m=TILES))
        for k in range(TILES, STEPS):
            load_w(k)

        free_banks = list(range(BANKS))
        to_turn = list(range(PAIRS + TILES))

        def take_bank(shape, number):
            free_banks.remove(number)
            return number, psum.tile(shape, F32, name="bank%d" % number)

        w_scales = once.tile([P, PASSES, W_BLOCKS], F32)

        def spread_w_scale():
            number, bank = take_bank([P, PASSES * W_BLOCKS], 0)
            nc.tensor.matmul(bank[:], lhsT=quadrants[:], rhs=w_scale_rows[:].rearrange("p g j -> p (g j)"), start=True, stop=True)
            nc.scalar.copy(out=w_scales[:].rearrange("p g j -> p (g j)"), in_=bank[:])
            free_banks.append(number)

        planes = {}
        laced = {}
        w_mx = {}
        spent_e = [e_raw[pair][:, n * WIDE:(n + 1) * WIDE].rearrange("p (c t) -> p c t", t=ROWS) for pair in range(PAIRS) for n in range(2 * E // WIDE)]

        def scaled(engine, dst, src, scale):
            if engine == "vector":
                nc.vector.tensor_scalar(out=dst, in0=src, scalar1=scale, scalar2=None, op0=MULT)
            elif engine == "gpsimd":
                nc.gpsimd.tensor_scalar(out=dst, in0=src, scalar1=scale, scalar2=0.0, op0=MULT, op1=ADD)
            else:
                nc.scalar.activation(out=dst, in_=src, func=ACT.Copy, scale=scale)

        def flat(raw):
            return raw[:].rearrange("p t c -> p (t c)" if len(raw.shape) == 3 else "p t h c -> p (t h c)")

        def widen_w(k, between=None):
            spent = k - 2 * PLANE_BUFFERS
            if spent < 0:
                planes[k] = work.tile([P, UNIT], BF16, align_bytes=64, name="w_planes", bufs=PLANE_BUFFERS)
            else:
                tag, bufs = ("f_wide", WORK_BUFFERS) if spent < WORK_BUFFERS else ("turned", TURNED_BUFFERS)
                planes[k] = work.tile([P, UNIT], BF16, align_bytes=64, name="w_planes", tag=tag, bufs=bufs)
            parts = 1 + (k < E_PASSES)
            for part in range(parts):
                nc.scalar.copy(out=planes[k][:, part * UNIT // parts:(part + 1) * UNIT // parts], in_=flat(w_raw[(k, part)]).bitcast(FP8))
                if between and part == 0:
                    between()

        def lace(engine, k, blocks=range(WIDE // B)):
            for c0, c1 in share(engine, k):
                if c0 // B in blocks:
                    part = min(c0 // B, 2)
                    if engine == "scalar":
                        laced[(k, part)] = spent_e.pop(0)
                    elif (k, part) not in laced:
                        name, bufs = [("w_first", 2), ("w_second", 2), ("w_gate", 1) if k in GATED else ("w_upper", 2)][part]
                        laced[(k, part)] = work.tile([P, B if part < 2 else HALF, ROWS], BF16, align_bytes=64, name=name, bufs=bufs)[:]
                    g, n0, width = UNITS[k][c0 // UNITS[k][0][2]]
                    dst = laced[(k, part)][:, c0 - part * B:c1 - part * B].rearrange("p (c i) t -> p c t i", i=VISIT[engine])
                    if k < E_PASSES:
                        rows = planes[k][:].rearrange("p (h t c) -> p h t c", t=ROWS, c=HALF)[:, c0 // HALF, :, c0 % HALF:c0 % HALF + c1 - c0]
                    else:
                        rows = planes[k][:].rearrange("p (t c) -> p t c", t=ROWS)[:, :, c0:c1]
                    j = (n0 + c0 % width) // B
                    scaled(engine, dst, rows.rearrange("p t (c i) -> p c t i", i=VISIT[engine]), w_scales[:, g, j:j + 1])

        def mx_tiles(name, bufs):
            codes = work.tile([P, WIDE], U32, align_bytes=256, name=name + "_codes", bufs=bufs)
            scales = work.tile([P, WIDE], U8, align_bytes=256, name=name + "_scales", bufs=bufs)
            return codes, scales

        def quantise(src, name, bufs):
            codes, scales = mx_tiles(name, bufs)
            nc.vector.quantize_mx(out=codes[:].bitcast(FP8X4), scales=scales[:], in_=src)
            return codes, scales

        def quantise_w(k):
            codes, scales = mx_tiles("w", W_BUFFERS)
            for part in ((1, 2, 0) if k + 1 in HELPED[:-1] else (1, 0, 2)):
                cols = slice(part * B, (part + 1) * B if part < 2 else WIDE)
                nc.vector.quantize_mx(out=codes[:, cols].bitcast(FP8X4), scales=scales[:, cols],
                                      in_=laced[(k, part)].rearrange("p c t -> p (c t)"))
            for h, (g, n0, width) in enumerate(UNITS[k]):
                w_mx[(g, n0)] = (codes[:, h * width:(h + 1) * width], scales[:, h * width:(h + 1) * width])
            if k < E_PASSES:
                w_mx[(k, 0)] = (codes[:], scales[:])

        f_wide = {}
        turned = {}
        x_mx = {}
        in_psum = []
        words_a_pass = K_PASS // 2

        def scale_f(m, engine):
            if m not in f_wide:
                f_wide[m] = work.tile([P, D], BF16, align_bytes=64, name="f_wide")
            split = (K_PASS // B) * f_passes_on_scalar(m)
            for j in (range(split) if engine == "scalar" else reversed(range(split, F_BLOCKS))):
                src = f_raw[m][:, j * B:(j + 1) * B].bitcast(FP8)
                scale = f_scales[:, m * F_BLOCKS + j:m * F_BLOCKS + j + 1]
                if engine == "scalar":
                    scaled(engine, f_wide[m][:, j * B:(j + 1) * B], src, scale)
                else:
                    g, q = divmod(j, K_PASS // B)
                    by_parity = f_wide[m][:, g * K_PASS:(g + 1) * K_PASS].rearrange("p (u r e) -> p r u e", u=2, e=2)
                    scaled(engine, by_parity[:, QUADRANT * q:QUADRANT * (q + 1)], src.rearrange("p (r u e) -> p r u e", u=2, e=2), scale)

        def turn(src, key, unsorted):
            words = src[:].bitcast(F32)
            first_bank = BANKS // 2 + 2 * (to_turn.pop(0) % 2)
            for half in range(2):
                number, bank = take_bank([P, 2, 2, P], first_bank + half)
                for h in range(2):
                    g = 2 * half + h
                    first = words_a_pass * g
                    for u in range(2):
                        cols = slice(first + u, first + words_a_pass, 2) if g < unsorted else slice(first + P * u, first + P * (u + 1))
                        nc.tensor.transpose(bank[:, h, u, :], words[:, cols], ident[:])
                in_psum.append((key, half, number, bank))

        def copy_turned():
            while in_psum:
                key, half, number, bank = in_psum.pop(0)
                if half == 0:
                    turned[key] = work.tile([P, D], BF16, align_bytes=64, name="turned", bufs=TURNED_BUFFERS)
                dst = turned[key][:, D // 2 * half:D // 2 * (half + 1)].bitcast(F32).rearrange("p (h r u) -> p h r u", h=2, u=2)
                nc.scalar.copy(out=dst, in_=bank[:].rearrange("p h u r -> p h r u"))
                free_banks.append(number)

        def turn_e(pair):
            turn(e_raw[pair], ("e", pair), 2 * E_PASSES)

        def turn_f(m):
            turn(f_wide[m], ("f", m), f_passes_on_scalar(m))

        def quantise_e(pair):
            x_mx[("e", pair)] = quantise(turned[("e", pair)][:], "e", PAIRS)

        def quantise_f(m):
            x_mx[("f", m)] = quantise(turned[("f", m)][:], "f", TILES)

        banks = {}
        done = {}
        finished = []
        emptied = []
        sums = once.tile([P, CHUNKS, TILES, WIDE], F32)

        def advance(group, stop=PASSES):
            for product in group:
                kind, n0, width, tiles = product
                whole = list(A_PASSES if kind == "a" else C_PASSES)
                made = done.setdefault(product, [])
                for g in whole:
                    for i, m in enumerate(tiles):
                        key = ("e", m // 2) if kind == "a" else ("f", m)
                        if key in x_mx and (g, n0) in w_mx and (i, g) not in made and g < stop:
                            if product not in banks:
                                banks[product] = take_bank([P, len(tiles), width], BANK[product])
                            made.append((i, g))
                            x_first = g + (E_PASSES * (m % 2) if kind == "a" else -E_PASSES)
                            x_cols = slice(x_first * P, (x_first + 1) * P)
                            x, w = x_mx[key], w_mx[(g, n0)]
                            nc.tensor.matmul_mx(out=banks[product][1][:, i, :], lhsT=x[0][:, x_cols].bitcast(FP8X4), lhsT_scale=x[1][:, x_cols],
                                                rhs=w[0].bitcast(FP8X4), rhs_scale=w[1],
                                                start=len(made) == 1, stop=len(made) == len(tiles) * len(whole))

        def empty(product):
            kind, n0, width, tiles = product
            number, bank = banks[product]
            emptied.append(product)
            part = sums[:, n0 // WIDE, tiles.start:tiles.stop, n0 % WIDE:n0 % WIDE + width]
            if kind == "a":
                nc.vector.tensor_tensor(out=part, in0=bank[:], in1=bias[:, n0:n0 + width].unsqueeze(1).to_broadcast([P, len(tiles), width]), op=ADD)
            else:
                for i, m in enumerate(tiles):
                    nc.vector.scalar_tensor_tensor(out=part[:, i, :], in0=bank[:, i, :], scalar=trusts[:, m:m + 1],
                                                   in1=part[:, i, :], op0=MULT, op1=ADD)
                finished.append(product)
            free_banks.append(number)

        def finish(count=1):
            kind, n0, width, tiles = product = finished.pop(0)
            stop = tiles.start + count * len(tiles)
            if count == 2:
                finished.pop(0)
            z = sums[:, n0 // WIDE, :, n0 % WIDE:n0 % WIDE + width]
            for part in ([slice(m, m + 1) for m in tiles] if product in RUNS[-1] else [slice(tiles.start, stop)]):
                nc.scalar.activation(out=z[:, part], in_=z[:, part], func=ACT.Silu)
            if stop % 2 == 0:
                nc.sync.dma_start(out=o_v[:, stop - 2:stop, n0:n0 + width], in_=z[:, stop - 2:stop])

        def ahead():
            for product in [product for run in RUNS for product in run if product not in emptied]:
                kind, n0, width, tiles = product
                number = BANK[product]
                turns_to_come = [n for n in to_turn if BANKS // 2 + 2 * (n % 2) == number - number % 2]
                if product not in banks and (number not in free_banks or turns_to_come):
                    break
                waits = kind == "c" and width == WIDE and tiles.start in HIGH and (PASSES - 1, n0) not in w_mx
                advance([product], PASSES - 2 if waits else PASSES)
                if product not in banks:
                    break

        to_widen = list(range(STEPS))
        to_lace = list(range(SCALAR_FROM, STEPS))

        def widen_up_to(k):
            while to_widen and to_widen[0] <= k:
                widen_w(to_widen.pop(0))

        def scalar_laces_up_to(k):
            while to_lace and to_lace[0] <= k:
                lace("scalar", to_lace.pop(0))

        def step(k):
            quantise_w(k)
            ahead()
            if k + 1 < STEPS:
                lace("vector", k + 1, range(1) if k + 1 in HELPED else range(WIDE // B))

        def empty_all(products):
            for product in products:
                empty(product)
                ahead()

        scale_f(0, "scalar")
        widen_w(to_widen.pop(0), spread_w_scale)
        scale_f(0, "vector")
        turn_f(0)
        scale_f(1, "vector")
        widen_up_to(1)
        copy_turned()
        lace("vector", 0)
        turn_f(1)
        turn_e(0)
        copy_turned()
        widen_up_to(2)
        lace("vector", 1)
        quantise_w(0)
        turn_e(1)
        scale_f(2, "vector")
        quantise_w(1)
        quantise_f(0)
        quantise_e(0)
        copy_turned()
        ahead()
        turn_f(2)
        widen_up_to(3)
        scale_f(3, "vector")
        lace("vector", 2)
        quantise_e(1)
        ahead()
        widen_up_to(4)
        copy_turned()
        turn_e(2)
        scale_f(4, "scalar")
        lace("vector", 3, range(1, 2))
        quantise_f(1)

        copy_turned()
        step(2)
        widen_up_to(5)
        scalar_laces_up_to(4)
        lace("gpsimd", 3)
        scale_f(5, "scalar")
        empty_all(RUNS[0][:2])
        turn_e(3)
        copy_turned()
        empty_all(RUNS[0][2:])
        scale_f(4, "vector")
        quantise_e(2)
        ahead()
        turn_f(3)
        quantise_f(2)

        copy_turned()
        scale_f(6, "scalar")
        step(3)
        widen_up_to(6)
        lace("gpsimd", 4)
        empty_all(RUNS[1][:1])
        turn_f(4)
        copy_turned()
        scalar_laces_up_to(5)
        scale_f(7, "scalar")
        empty_all(RUNS[1][1:])
        quantise_e(3)
        scale_f(5, "vector")
        advance(RUNS[2][1:3])
        turn_f(5)
        ahead()
        scale_f(6, "vector")
        turn_f(6)
        quantise_f(3)

        copy_turned()
        step(4)
        widen_up_to(7)
        scalar_laces_up_to(6)
        widen_up_to(8)
        lace("gpsimd", 5)
        empty_all(RUNS[2])
        scale_f(7, "vector")
        turn_f(7)
        quantise_f(4)
        quantise_f(5)
        ahead()
        copy_turned()

        to_quantise = list(HIGH[2:])
        for n in range(FIRST_C, len(RUNS)):
            run = RUNS[n]
            for k in BEATS[n]:
                step(k)
                if to_quantise:
                    quantise_f(to_quantise.pop(0))
                    ahead()
                scalar_laces_up_to(k + 2)
                widen_up_to(k + 4)
            if run == RUNS[-1]:
                break
            lace("gpsimd", k + 1)
            for j in range(min(len(finished) // 2, SILUS * (len(BEATS[n + 1]) == 1) * (1 + (run == RUNS[-2])))):
                finish(2)
            for product in run[:len(run) - KEPT * (run == RUNS[-2])]:
                empty_all([product])
                if run == RUNS[-2]:
                    finish()

        for product in RUNS[-2][len(RUNS[-2]) - KEPT:] + RUNS[-1]:
            empty_all([product])
            finish()
